import numpy as np, ml_dtypes
CORES = [24,25,26,27,28,29,30,31]
N = 8
BF = ml_dtypes.bfloat16
L, WX, W, FD, RO = 128, 8192, 2048, 256, 4
LW = 11
WT = 2 * np.arange(16) + 1
KINDS = np.array([[16, 0, 0, 0], [15, 1, 0, 0], [8, 8, 0, 0], [4, 4, 4, 4], [13, 1, 1, 1], [7, 6, 2, 1], [14, 2, 0, 0], [6, 5, 5, 0]])
SEQ = np.stack([np.repeat(np.arange(4), a) for a in KINDS])
def move(a):
    return np.ascontiguousarray(a.reshape(N, 8, 16, N, L // N).transpose(3, 1, 2, 0, 4)).reshape(N, 8, 16, L)
def pack(X, C, M, S, Z):
    return {"x0": np.ascontiguousarray(X.reshape(N, 128, WX)).astype(np.float32).astype(BF), "cm": np.ascontiguousarray((W * M + C).reshape(N, 128, W)).astype(np.int32),
            "s0": np.ascontiguousarray(S.reshape(N, 128, L)).astype(np.int32), "z0": np.ascontiguousarray(Z.reshape(N, 128, L)).astype(np.float32).astype(BF)}
def parts(rng):
    X = rng.integers(0, 256, (N, 8, 16, WX)); C = rng.integers(0, W, (N, 8, 16, W)); M = rng.integers(0, W, (N, 8, 16, W))
    share = rng.choice(np.array([0.1, 0.3, 0.6]), (N, 8, 1, 1)); pool = rng.integers(0, W, (N, 8, 1, 64))
    few = np.take_along_axis(pool, rng.integers(0, 64, (N, 8, 1, 16 * W)), 3).reshape(N, 8, 16, W)
    C = np.where(rng.random(C.shape) < share, few, C)
    return X, C, M, rng.integers(0, W, (N, 8, 16, L)), rng.integers(0, 256, (N, 8, 16, L))
def classes(rng, kinds):
    s = np.take_along_axis(np.argsort(rng.random((L, 4)), axis=1), SEQ[kinds], 1)
    return np.take_along_axis(s, np.argsort(rng.random((L, 16)), axis=1), 1).T
def juries(rng, X, C, S, Z, q, g, cl):
    v = rng.permutation(W); off = rng.integers(0, W, 16); kind = int(rng.integers(0, 4))
    C[q, g] = v[(np.arange(W)[None, :] + off[:, None]) % W]
    base = np.zeros(16, np.int64) if kind == 0 else np.full(16, 255) if kind == 1 else rng.integers(0, 256, 16)
    Z[q, g] = base[np.argsort(rng.random((16, L)), axis=0)]
    u = int(np.add.reduce(base)); h = (((v * (u + 1)) >> 5) + v) & (WX - 1)
    b = np.add.reduce(X[q, g][:, h] * WT[:, None], axis=0) & 3
    start = rng.integers(0, W, (1, L))
    for c in range(4):
        m = (cl == c).astype(np.int64); before = np.add.accumulate(m, axis=0) - m
        pl = np.flatnonzero(b == c)
        if len(pl) == 0: pl = np.arange(W)
        S[q, g] = np.where(m == 1, (pl[(start + before) % len(pl)] - off[:, None]) % W, S[q, g])
    return off
def setup_inputs(rng):
    return pack(*parts(rng))
def setup_inputs_spread(rng):
    def uneven(n, hi, *shape):
        return np.minimum((hi * rng.random((N, 8, 16, n)) ** rng.choice(np.array([0.125, 0.5, 1.0, 2.0, 5.0]), shape)).astype(np.int64), hi - 1)
    return pack(uneven(WX, 256, N, 8, 1, WX), uneven(W, W, N, 8, 1, 1), uneven(W, W, N, 8, 16, 1), uneven(L, W, N, 8, 1, L), uneven(L, 256, N, 8, 1, L))
def setup_inputs_ends(rng):
    p = np.array([0.0, 0.1, 0.5, 0.9, 1.0])
    X = 255 * (rng.random((N, 8, 16, WX)) < rng.choice(p, (N, 8, 1, WX))).astype(np.int64)
    C = (W - 1) * rng.integers(0, 2, (N, 8, 16, W)); S = (W - 1) * rng.integers(0, 2, (N, 8, 16, L))
    Z = 255 * (rng.random((N, 8, 16, L)) < rng.choice(p, (N, 8, 1, L))).astype(np.int64)
    Z[..., L - 1] = 255; Z[..., 0] = 255; Z[..., 1] = 0; Z[..., L - 2] = 0
    C[:, :, 15, W - 1] = W - 1; S[:, :, 15, L - 1] = W - 1; S[:, :, 15, 0] = W - 1
    X[:, 0] = X[:, 0, :1]
    X[:, :, :, WX - 1] = 255; X[:, ::2, :, 0] = 255; X[:, 1::2, :, 0] = 0
    C[:, 7, :, W - 1] = W - 1; S[:, 7, :, L - 1] = W - 1; S[:, 7, :, 2] = W - 1
    C[:, 5, :, 0] = 0; C[:, 5, :, W - 1] = W - 1
    S[:, 5] = (W - 1) * (np.arange(16)[:, None] == rng.integers(0, 16, (N, 1, L)))
    Z[:, 5] = np.where(Z[:, 5, :1] > 0, 255, 0)
    X[:, 5, :, (613 * np.arange(15)) & (WX - 1)] = 0
    for u in (0, 4080):
        h = ((((W - 1) * (u + 1)) >> 5) + W - 1) & (WX - 1)
        X[:, 5, :, h] = 0; X[:, 5, 0, h] = 255
    M = np.where(rng.random(C.shape) < 0.8, C, W - 1 - C)
    return pack(X, C, M, S, Z)
def setup_inputs_corners(rng):
    X, C, M, S, Z = parts(rng)
    for q in range(N):
        for g in range(8):
            off = juries(rng, X, C, S, Z, q, g, classes(rng, rng.integers(0, 8, L)))
            w = rng.random(L); c = rng.integers(0, W, L)
            S[q, g] = np.where((w < 0.15)[None, :], (c[None, :] - off[:, None]) % W, S[q, g])
            S[q, g, 15] = np.where(w > 0.8, (S[q, g, 0] + off[0] - off[15]) % W, S[q, g, 15])
    return pack(X, C, M, S, Z)
def setup_inputs_crowd(rng):
    X, C, M, S, Z = parts(rng)
    for q in range(N):
        for g in range(8):
            w = (g + q) % 8; kinds = np.full(L, (1, 1, 0, 5, 5, 6, 3, 4)[w]); one = int(rng.integers(0, L))
            if w == 1: kinds[one] = 0
            off = juries(rng, X, C, S, Z, q, g, classes(rng, kinds))
            if w == 3: S[q, g] = S[q, g, :, :1].copy()
            if w == 4: S[q, g] = ((int(rng.integers(0, W)) - off) % W)[:, None]
            if w == 5:
                mine = S[q, g, :, one].copy(); S[q, g] = S[q, g, :, (one + 1) % L].copy()[:, None]; S[q, g, :, one] = mine
    return pack(X, C, M, S, Z)
def setup_inputs_tops(rng):
    X, C, M, S, Z = parts(rng)
    X[:, 1::2] = 255 - (rng.random((N, 4, 16, WX)) < 0.25).astype(np.int64)
    C = np.where(rng.random(C.shape) < 0.5, rng.choice(np.array([W - 17, W - 5, W - 3, W - 1]), C.shape), rng.integers(W - 96, W, C.shape))
    lack = rng.integers(0, 17, (N, 8, 1, L)); lack[..., 0::4] = 4; lack[..., 1::4] = 6; lack[..., 2::4] = 0; lack[..., L - 1] = 4
    Z = 255 - (np.argsort(rng.random((N, 8, 16, L)), axis=2) < lack).astype(np.int64)
    C[:, :, 15, W - 1] = W - 5; S[:, :, 15, L - 1] = W - 1
    return pack(X, C, M, S, Z)
def check_inputs(d):
    bad = []
    for k, hi in (("x0", 255), ("cm", W * W - 1), ("s0", W - 1), ("z0", 255)):
        a = np.asarray(d[k]).astype(np.float64)
        if not (np.min(a) >= 0 and np.max(a) <= hi): bad.append("range of " + k)
        elif np.any(a != np.floor(a)): bad.append("whole numbers in " + k)
    return bad
def reference(x0, cm, s0, z0):
    X = x0.astype(np.float32).astype(np.int64).reshape(N, 8, 16, WX); both = cm.astype(np.int64).reshape(N, 8, 16, W)
    C = both & (W - 1); M = both >> LW
    S = s0.astype(np.int64).reshape(N, 8, 16, L); Z = z0.astype(np.float32).astype(np.int64).reshape(N, 8, 16, L)
    A = np.zeros((N, 8, 1, 1), np.int64); k = np.arange(16); lane = np.arange(L); less = (k[:, None] > k[None, :])[:, :, None]
    for t in range(RO):
        e = np.take_along_axis(C[:, :, (k + t) & 15], S, 3)
        same = (e[:, :, :, None, :] == e[:, :, None, :, :]) & less
        o = np.add.reduce(same.astype(np.int64), axis=3)
        u = np.add.reduce(Z, axis=2)[:, :, None, :]
        h = (((e * (u + 1)) >> 5) + e + 613 * o + A) & (WX - 1)
        x = np.take_along_axis(X, h.reshape(N, 8, 1, 16 * L), 3).reshape(N, 8, 16, 16, L)
        b = np.add.reduce(x * WT[:, None, None], axis=2) & 3
        count = np.stack([np.add.reduce((b == c).astype(np.int64), axis=2) for c in range(4)], axis=2)
        best = np.argmin(np.where(count == 0, 99, count), axis=2)[:, :, None, :]
        sv = b == best; si = sv.astype(np.int64)
        ns = np.add.reduce(si, axis=2)[:, :, None, :]; before = np.add.accumulate(si, axis=2) - si
        place = np.where(sv, before, ns + k[:, None] - before)
        order = np.zeros_like(e); np.put_along_axis(order, place, e, 2)
        first = np.argmax(sv, axis=2)[:, :, None, :]
        hf = np.take_along_axis(h, first, 2); xf = np.take_along_axis(x, first[:, :, None], 3)[:, :, :, 0]
        y = np.take_along_axis(M, e.reshape(N, 8, 1, 16 * L), 3).reshape(N, 8, 16, 16, L)
        Z = np.maximum.reduce(np.where(sv[:, :, None], x, 0), axis=3)
        S = np.maximum.reduce(np.where(sv[:, :, None], y, 0), axis=3)
        np.put_along_axis(C, np.broadcast_to((W // L) * lane + (u & (W // L - 1)), (N, 8, 16, L)), order, 3)
        np.put_along_axis(X, np.broadcast_to(hf - (hf & (L - 1)) + lane, (N, 8, 16, L)), (xf + Z) >> 1, 3)
        A = np.add.reduce((ns == 1).astype(np.int64), axis=3)[..., None]
        if t < RO - 1:
            S = move(S); Z = move(Z)
    yx = np.add.reduce(X.reshape(N, 128, WX // FD, FD) * np.arange(1, WX // FD + 1)[:, None], axis=2)
    yc = np.add.reduce(C.reshape(N, 128, W // FD, FD) * np.arange(1, W // FD + 1)[:, None], axis=2)
    return {"yx": yx.astype(np.float32), "yc": yc.astype(np.float32), "ys": np.ascontiguousarray(S).reshape(N, 128, L).astype(np.float32), "yz": np.ascontiguousarray(Z).reshape(N, 128, L).astype(np.float32).astype(BF)}

@@ -1,0 +1,662 @@
+import numpy as np
+from concourse.bass import DstId, RemoteDMATransfer
+from concourse.mybir import AluOpType, ActivationFunctionType
+
+AL = AluOpType
+AF = ActivationFunctionType
+RO, NS = 4, 2
+LH = 128 // NS
+Q = 16 // NS
+F16, BF, F32, I32, U16 = "float16", "bfloat16", "float32", "int32", "uint16"
+
+
+def sb(n, d):
+    return ("sbuf", [128] + (n if isinstance(n, list) else [n]), d)
+
+
+SCRATCH = {
+    "s0b": sb([8, 16], I32), "z0b": sb([8, 16], BF), "cmb": sb(2048, I32), "X": sb(8192, BF),
+    "C": sb(2048, I32), "M": sb(2056, I32),
+    "DJ": sb(160, BF), "BI": sb(128, BF), "CcM": sb(128, BF), "ki": sb(8, I32), "ia": sb(17, F32), "t5": sb(5, F32),
+    "Sf": sb(384, F32), "St": sb(384, F16), "rst": sb(512, BF), "cd": sb(384, BF), "col": sb(32, F32),
+    "R": sb(17, F32), "Rd": sb(16, F32), "Rd2": sb(16, F32), "tny": sb(64, F32), "J": sb(160, F16),
+    "Y": sb([16, 160], F16), "Wz": sb(144, BF),
+    "Sel": sb([8, 2], F32), "o129": sb(128, BF), "FC": sb(128, BF), "Ft": sb(128, F16), "sx": sb([128, 2], F16),
+    "K": sb([22, 128], F16), "Ab": sb(64, F16), "Cy": sb([8, 32], F16), "Dm": sb([8, 128], F16),
+    "Om": sb([8, 128], F16), "Cm": sb([9, 128], F16), "Fl": sb([4, 128], F16), "Bj": sb([4, 128], F16),
+    "Dg": sb([32, 128], BF), "one": sb(64, F16),
+    "snd": sb([3 * NS, 8, 2 * Q], F16), "lnd": sb([4 * NS, 8, 2 * Q], F16),
+    "Sl": sb(128, U16), "fl": sb([2, 128], F16), "G": sb(2048, F16), "E16": sb(128, F16),
+    "Pp": sb(128, F32), "eq": sb(1024, F16), "hi": sb(128, I32), "hj": sb(128, I32),
+    "hu": sb(128, U16), "kh": sb(256, F16), "xg": sb(2048, BF), "gq": sb([4, 128], F16), "fg": sb(128, F16),
+    "wn": sb(128, F16), "sv": sb(128, F16), "eu": sb(128, U16), "mg": sb(2048, F16), "ms": sb(2048, F16),
+    "xs": sb(2048, F16), "Rl": sb(128, F16), "V16": sb(128, F32), "Rr": sb([15, 128], F32),
+    "Ff": sb(128, F32), "sel": sb(256, F16), "ls": sb(384, F32), "lu": sb(24, U16), "junk": sb(128, F32),
+    "xa": sb(128, F32), "xh": sb(128, I32), "cs": sb(2048, BF),
+    "yxb": sb(256, F32), "ycb": sb(256, F32), "ysb": sb([8, 16], F32), "yzb": sb([8, 16], BF), "C16": sb(2048, F16),
+    "mi": sb(128, I32), "mp": sb(128, F32), "li": sb(16, I32), "lc": sb(8, U16), "old": sb(128, F32),
+    "adj": sb(128, F32), "vv": sb(128, F32),
+}
+for _b in range(8):
+    SCRATCH["p%d" % _b] = ("psum", [128, 512] if _b < 7 else [128, 32, 16], F32)
+SEMAPHORES = ["qV", "qS", "qP", "qG", "left", "stored"] + ["ld%d" % s for s in range(7)] + \
+    ["arr%d" % s for s in range(3 * NS)]
+
+LC, CC, CP, PAR, NL, L15, L14, WW, DG, NDG, THR, CQ, FB, STC, W8, SC, AC, KK, HI8 = range(19)
+BM, DMB, DMN, DMZ, ID, IN1, I3, I128, IN128, IN2K, IN16, T128, SG, ZF, BM128, LO, BE, TMP, TM2, TM3, B32, CN = range(22)
+
+PAR0 = {"cyc": 1.04, "fix": 30.0, "g": 1.56, "sc": 3.8, "pe": 0.55, "lat": 60.0, "xch": 3500.0, "snd": 900.0,
+        "bw": 400.0, "dma": 2000.0, "sfix": 65.0}
+OPT = {'seed':3226,'jit':0.05,'vg':1.6,'stag':0,'fs':1,'ccp':14,'pri':{'linFt-1':-4000,'tshj1':2000,'mmp20':4000,'linlnd0':-2000,'accjunk-1':-4000,'scanxs1':-500,'linAb-1':-500,'tthi1':2000,'linfl0':-1000,'send1':-500,'lincs0':500,'linycb-1':1000,'scanls-1':500,'ttvv-1':-500,'linlu-1':-1000,'linlc-1':1000,'tshj0':2000,'linRl-1':4000,'linsel-1':4000,'own1':-500,'lincs1':-500},'eng':{'xh':'V','mi':'V','Sl':'S','pk':'S','fl':'S','wn':'S','hh':'S','Rl':'S','A':'V','yb':'V','cv':'S','z16':'S','V16':'V','sx':'V','eh':'S','sel':'S'},'it':1,'pw':0.1,'pre':3}
+
+
+def S_(a, b, c=None):
+    return slice(a, b, c)
+
+
+def build(opt):
+    ops = []
+    acc = {}
+    tag = [-1]
+
+    def span(a):
+        if len(a) == 2 and a[0] == "p7":
+            return a[1].start, a[1].stop, a[1].stop - a[1].start
+        shp = SCRATCH[a[0]][1][1:]
+        ix = np.arange(int(np.prod(shp))).reshape(shp)[a[1:]]
+        return int(np.min(ix)), int(np.max(ix)) + 1, int(np.size(ix))
+
+    def two(a):
+        return SCRATCH[a[0]][2] in (F16, BF, U16)
+
+    def add(eng, kind, args, rd, wr, n, rate, extra=()):
+        me = len(ops)
+        deps = set(extra)
+        bank = set()
+        for lst, w in ((rd, False), (wr, True)):
+            for a in lst:
+                if SCRATCH[a[0]][0] == "psum":
+                    last = acc.setdefault(a[0], {})
+                    for e in list(last):
+                        if (e == "P") != (eng == "P"):
+                            deps.add(last[e])
+                        elif e != "P":
+                            bank.add(last[e])
+                    if eng == "P":
+                        last.clear()
+                    last[eng if eng in ("P", "V", "S") else me] = me
+                    continue
+                lo, hi, _ = span(a)
+                rec = acc.setdefault(a[0], [])
+                for (o, l2, h2, w2) in rec:
+                    if (w or w2) and l2 < hi and lo < h2:
+                        deps.add(o)
+                if w:
+                    rec[:] = [r for r in rec if not (lo <= r[1] and r[2] <= hi)]
+                rec.append((me, lo, hi, w))
+        deps.discard(me)
+        bank.discard(me)
+        ops.append({"eng": eng, "kind": kind, "args": args, "deps": deps, "bank": bank - deps, "n": n, "rate": rate,
+                    "tag": tag[0], "key": kind + (wr[0][0] if wr else "") + str(tag[0])})
+        return me
+
+    def vec(kind, out, ins, args, eng="V", more=()):
+        full = [x for x in ins if isinstance(x, tuple)]
+        rd = [p for x in full for p in ([x[1], x[2]] if x[0] == "ind" else [x])]
+        if out[0] == "ind":
+            return add(eng, kind, args, rd + [out[2]], [out[1]], 16 * span(out[2])[2], "sc")
+        if ins[0][0] == "ind":
+            rate = "g"
+        elif kind == "tt":
+            rate = 2.0 if all(SCRATCH[x[0]][0] == "sbuf" for x in full) else 1.0
+        else:
+            rate = 0.5 if all(two(x) for x in [out] + [x for x in full if span(x)[2] > 1]) else 1.0
+        return add(eng, kind, args, rd, [out] + list(more), span(out)[2], rate)
+
+    def cp(out, i):
+        return vec("cp", out, [i], (out, i))
+
+    def tt(out, a, b, op):
+        return vec("tt", out, [a, b], (out, a, b, op))
+
+    def ts(out, a, s1, op0, s2=None, op1=None):
+        return vec("ts", out, [a, s1, s2], (out, a, s1, s2, op0, op1))
+
+    def scan(out, a, b, init, op0, op1):
+        return vec("scan", out, [a, b], (out, a, b, init, op0, op1))
+
+    def ms(out, v):
+        return add("V", "ms", (out, v), [], [out], span(out)[2], 0.5 if two(out) else 1.0)
+
+    def lin(name, out, a, mul=1.0, addc=0.0, relu=False):
+        return vec("lin", out, [a, mul, addc], (out, a, mul, addc, relu), opt["eng"].get(name, "VS"))
+
+    def gather(name, out, win, off):
+        return add(opt["eng"].get(name, "VS"), "gat", (out, ("ind", win, off)), [win, off], [out], span(out)[2], "g")
+
+    def mm(lst, after=None):
+        n = sum(max(64, span(m[2])[2]) for m in lst)
+        return add("P", "mm", lst, [x for m in lst for x in (m[1], m[2])], [m[0] for m in lst], n, "pe",
+                   [] if after is None else [after])
+
+    def grp(out, pairs):
+        return [(out, l, r, j == 0, j == len(pairs) - 1) for j, (l, r) in enumerate(pairs)]
+
+    def iota(out, pat, base, cm):
+        return add("G", "iota", (out, pat, base, cm), [], [out], span(out)[2], "gp")
+
+    def c_(j):
+        return ("col", S_(j, j + 1))
+
+    def k_(j):
+        return ("K", j, S_(0, 128))
+
+    def y_(a, b):
+        return ("tny", S_(a, b))
+
+    def load(j, dst, src, nbytes):
+        me = add("Y", "ld", (dst, src, j), [], [dst], nbytes, "dma")
+        if j:
+            ops[me]["bank"].add(me - 1)
+
+    full = S_(0, 128)
+    quarters = [S_(512 * j, 512 * j + 512) for j in range(4)]
+    load(0, ("cmb", quarters[0]), ("cm", quarters[0]), 262144)
+    load(1, ("s0b", S_(0, 8), S_(0, 16)), ("s0", full), 65536)
+    for j in range(1, 4):
+        load(1 + j, ("cmb", quarters[j]), ("cm", quarters[j]), 262144)
+    load(5, ("z0b", S_(0, 8), S_(0, 16)), ("z0", full), 32768)
+    load(6, ("X", S_(0, 8192)), ("x0", S_(0, 8192)), 2097152)
+
+    DJ = ("DJ", S_(0, 160)); D0 = ("DJ", full); D4 = ("DJ", S_(0, 144))
+    R0 = ("R", S_(0, 1))
+    iota(("ki", S_(0, 1)), [[0, 1]], 0, 1)
+    iota(("ia", S_(0, 17)), [[1, 17]], 0, 0)
+    iota(DJ, [[1, 160]], 0, -1)
+    iota(("BI", full), [[16, 8], [0, 16]], 0, -1)
+    iota(("t5", S_(0, 5)), [[-1, 5]], 4, 0)
+    iota(("CcM", full), [[0, 8], [1, 4], [0, 4]], 0, 0)
+    iota(("FC", full), [[0, 8], [1, 16]], -15, 0)
+    iota(("Sf", full), [[16, 128]], 0, 0)
+    iota(("Sf", S_(128, 256)), [[Q, NS], [16, 8], [1, Q]], 0, 0)
+    iota(("Sf", S_(256, 384)), [[16 * Q, NS], [256, 8], [16, Q]], 0, 0)
+    for m in range(32):
+        add("G", "diag", (("Dg", m, full), ("DJ", S_(m + 1, m + 129))), [DJ], [("Dg", m, full)], 128, "gp")
+    ki = ("ki", S_(0, 1))
+    ts(("ki", S_(4, 5)), ki, 15, AL.bitwise_and)
+    ts(("ki", S_(5, 6)), ki, 2, AL.logical_shift_right, 3, AL.bitwise_and)
+    ts(("ki", S_(6, 7)), ki, 3, AL.bitwise_and)
+    ts(("ki", S_(7, 8)), ki, 1, AL.bitwise_and)
+    cp(("col", S_(0, 4)), ("ki", S_(4, 8)))
+    ts(("R", S_(0, 17)), ("ia", S_(0, 17)), c_(LC), AL.is_equal)
+    ts(("J", S_(0, 160)), DJ, 16.0, AL.is_equal)
+    for a in range(16):
+        lin("k", ("Y", a, S_(0, 160)), ("J", S_(0, 160)), ("R", S_(a, a + 1)))
+    for j, src, mul, addc in ((NL, LC, -1.0, 0.0), (L15, LC, -1.0, 15.0), (WW, PAR, -2.0, 1.0),
+                              (CQ, CC, 0.25, 0.0), (KK, LC, 1.0, 1536.0)):
+        lin("k", c_(j), c_(src), mul, addc)
+    ts(k_(BM), ("BI", full), c_(NL), AL.is_equal)
+    lin("k", k_(TMP), k_(BM), -1024.0, 1024.0)
+    tt(k_(DMB), D0, k_(TMP), AL.add)
+    ts(k_(ID), k_(DMB), 0.0, AL.is_equal)
+    for j, v in ((IN1, -1.0), (I3, 3.0), (I128, 2048.0), (IN2K, 4096.0), (IN16, -16.0)):
+        lin("k", k_(j), k_(ID), v)
+    for rep in range(2):
+        lin("k", ("Cy", S_(0, 8), S_(16 * rep, 16 * rep + 16)), k_(ID))
+    for j in range(2):
+        pk = "p%d" % (6 + j)
+        mm([x for d in range(4) for x in grp((pk, S_(128 * d, 128 * d + 128)), [
+            (k_(ID), k_(ID)), (k_(IN1), ("Cy", S_(0, 8), S_(4 * j + d + 1, 4 * j + d + 17)))])])
+        lin("k", ("Dm", S_(4 * j, 4 * j + 4), full), (pk, S_(0, 512)))
+    ts(y_(0, 8), ("ia", S_(1, 9)), c_(LC), AL.add, 16.0, AL.is_lt)
+    tt(y_(8, 16), y_(0, 8), ("ia", S_(1, 9)), AL.mult)
+    lin("k", c_(W8), y_(7, 8), 613.0)
+    for d in range(1, 9):
+        ts(("Om", d - 1, full), k_(DMB), y_(7 + d, 8 + d), AL.is_equal, 613.0 if d < 8 else c_(W8), AL.mult)
+    ts(("Wz", S_(0, 144)), D4, c_(L15), AL.is_equal, c_(WW), AL.mult)
+    lin("k", k_(BM128), k_(BM), 128.0)
+    lin("k", k_(BE), k_(BM), c_(CQ))
+    ms(("t5", S_(0, 1)), 0.0)
+    ts(y_(16, 21), ("t5", S_(0, 5)), c_(CC), AL.is_equal)
+    ts(y_(21, 26), ("t5", S_(0, 5)), c_(CP), AL.is_equal)
+    tt(c_(DG), c_(CC), c_(CP), AL.is_equal)
+    lin("k", c_(NDG), c_(DG), -7.0, -1.0)
+    tt(y_(26, 30), y_(16, 20), y_(17, 21), AL.subtract)
+    tt(y_(30, 34), y_(21, 25), y_(22, 26), AL.subtract)
+    tt(y_(34, 38), y_(26, 30), y_(30, 34), AL.subtract)
+    ts(y_(38, 42), y_(26, 30), c_(DG), AL.mult, -0.25, AL.mult)
+    tt(y_(42, 46), y_(34, 38), y_(38, 42), AL.add)
+    lin("k", y_(50, 54), y_(42, 46), 4.0)
+    for j in range(4):
+        lin("k", ("Bj", j, full), k_(ID), y_(50 + j, 51 + j))
+    mm([(("p6", S_(128 * j, 128 * j + 128)), k_(BM), ("Bj", j, full), True, True) for j in range(4)])
+    lin("k", ("Fl", S_(0, 4), full), ("p6", S_(0, 512)))
+    tt(y_(46, 47), y_(21, 22), y_(16, 17), AL.subtract)
+    ts(y_(47, 48), y_(46, 47), 64.0, AL.mult, c_(CP), AL.add)
+    lin("k", y_(48, 49), y_(16, 17), 16.0, -0.5)
+    ts(y_(49, 50), y_(48, 49), c_(DG), AL.mult, c_(CC), AL.subtract)
+    lin("k", c_(THR), y_(47, 48), 1.0, y_(49, 50))
+    ts(k_(TM2), ("CcM", full), c_(CC), AL.is_equal, c_(NDG), AL.mult)
+    lin("k", k_(TM3), k_(TM2), 1.0, c_(DG))
+    tt(k_(LO), k_(TM3), k_(BM), AL.mult)
+    tt(("Rd", S_(0, 16)), ("R", S_(0, 16)), ("R", S_(1, 17)), AL.subtract)
+    ts(k_(TM2), k_(DMB), -1.0, AL.is_equal, -2048.0, AL.mult)
+    tt(("Cm", 8, full), k_(TM2), k_(I128), AL.add)
+    tt(("Rd2", S_(0, 8)), ("R", S_(0, 8)), ("R", S_(8, 16)), AL.add)
+    for j in range(8):
+        lin("k", ("Cm", j, full), k_(BM), ("Rd2", S_(j, j + 1)))
+    ts(c_(L14), c_(LC), 8.0, AL.is_lt)
+    ts(c_(HI8), c_(LC), 8.0, AL.is_ge)
+    lin("k", c_(FB), ("R", S_(15, 16)), -4096.0)
+    ms(("one", S_(0, 64)), 1.0)
+    ms(("rst", S_(0, 512)), 1.0)
+    ms(("rst", S_(0, 512, 16)), 0.0)
+    lin("k", ("cd", S_(0, 16)), ("Rd", S_(0, 16)), 16384.0)
+    lin("k", ("cd", S_(15, 16)), ("Rd", S_(15, 16)), 16384.0, -32768.0)
+    for a, b in ((16, 16), (32, 32), (64, 64), (128, 128), (256, 128)):
+        lin("k", ("cd", S_(a, a + b)), ("cd", S_(0, b)))
+    tt(k_(DMN), D0, k_(TMP), AL.subtract)
+    ts(k_(T128), k_(DMN), 0.0, AL.is_gt, 2048.0, AL.mult)
+    tt(k_(DMZ), D0, k_(BM), AL.mult)
+    ts(k_(TM2), k_(DMZ), -1.0, AL.max, 1.0, AL.min)
+    lin("k", k_(TM3), k_(ID), -32.0)
+    tt(k_(SG), k_(TM3), k_(TM2), AL.subtract)
+    tt(k_(TM2), k_(I128), k_(T128), AL.subtract)
+    lin("k", k_(ZF), k_(TM2), 1.0 / 32)
+    ms(("o129", full), 16.0)
+    for j in range(2):
+        lin("k", ("Sel", S_(0, 8), j), ("K", BM, S_(0, 128, 16)), 2.0 * j - 1.0)
+    lin("k", ("kh", full), k_(BM), 0.0, c_(KK))
+    ts(c_(STC), ("R", S_(1, 2)), 24576.0, AL.mult, ("R", S_(2, 3)), AL.subtract)
+    lin("k", ("St", S_(0, 256)), ("Sf", S_(0, 256)), R0)
+    lin("k", ("St", S_(256, 384)), ("Sf", S_(256, 384)), R0, c_(STC))
+    lin("k", c_(SC), R0, 1.0, 2048.0)
+    lin("k", k_(B32), k_(BM), 1.0 / 32)
+    ts(y_(54, 55), c_(LC), 8.0, AL.is_lt, -16384.0, AL.mult)
+    ts(y_(55, 56), ("R", S_(8, 9)), -0.484375, AL.mult, y_(54, 55), AL.add)
+    lin("k", k_(CN), k_(BM), y_(55, 56))
+    ms(("M", S_(0, 8)), 0)
+    for w in quarters:
+        ts(("C", w), ("cmb", w), 2047, AL.bitwise_and)
+    for w in quarters:
+        lin("M", ("M", S_(w.start + 8, w.stop + 8)), ("cmb", w), 1.0 / 2048, -1023.5 / 2048)
+
+    Cw = ("C", S_(0, 2048)); Xw = ("X", S_(0, 8192)); Mw = ("M", S_(0, 2056))
+    blk = S_(0, 8)
+    arrive = {}
+    for t in range(RO):
+        last = t == RO - 1
+        par = t & 1
+        if last:
+            prev = None
+            for j in range(16):
+                prev = mm([(("p6", S_(0, 256)), ("Dg", m, full), ("X", S_(256 * m, 256 * m + 256)), m == 0, m == 31)
+                           for m in range(2 * j, 2 * j + 2)], prev)
+            lin("yb", ("yxb", S_(0, 256)), ("p6", S_(0, 256)))
+        for h in range(NS):
+            tag[0] = h
+            w = S_(LH * h, LH * h + LH)
+            o = 16 * LH * h
+            pa, pb, pc = "p%d" % (3 * h), "p%d" % (3 * h + 1), "p%d" % (3 * h + 2)
+            a0 = S_(0, LH)
+            s = NS * t + h
+            mine = S_(Q * h, Q * h + Q)
+            zz = ("lnd", s, blk, S_(Q, 2 * Q))
+            if t == 0:
+                lin("Sl", ("Sl", w), ("s0b", blk, mine))
+                lin("z16", zz, ("z0b", blk, mine), 1.0, R0)
+            else:
+                ops[lin("Sl", ("Sl", w), ("lnd", s, blk, S_(0, Q)))]["deps"].add(arrive[s])
+            chunks = [(LH * h + 32 * j, o + 512 * j) for j in range(LH // 32)]
+            for (l0, c0) in chunks:
+                gather("gC", ("G", S_(c0, c0 + 512)), Cw, ("Sl", S_(l0, l0 + 32)))
+            mm(grp((pc, a0), [(k_(B32), zz)]), arrive.get(s))
+            lin("fl", ("fl", par, w), (pc, a0), 2.0, 1536.0 - 0.0625 - 0.46875)
+            mm(grp((pa, a0), [(("Y", (k + t) & 15, S_(16 + ((k + t) & 15) - k, 144 + ((k + t) & 15) - k)),
+                               ("G", S_(o + k, o + 16 * LH, 16))) for k in range(16)]))
+            lin("E16", ("E16", w), (pa, a0))
+            if opt["pre"] >> h & 1:
+                lin("eu", ("eu", w), ("E16", w), 1.0, 8.0)
+                for (l0, c0) in chunks:
+                    gather("gM", ("mg", S_(c0, c0 + 512)), Mw, ("eu", S_(l0, l0 + 32)))
+            mm([((pb, S_(LH * d, LH * d + LH)), ("Dm", d, full), ("E16", w), True, True) for d in range(8)])
+            tt(("Pp", w), ("E16", w), (pc, a0), AL.mult)
+            e0 = 8 * LH * h
+            ts(("eq", S_(e0, e0 + 8 * LH)), (pb, S_(0, 8 * LH)), 0.0, AL.is_equal)
+            oa = grp((pa, a0), [(k_(ID), ("E16", w)), (k_(CN), ("one", a0))] + ([(k_(ID), ("Ab", a0))] if t else []) +
+                     [(("Om", d, full), ("eq", S_(e0 + LH * d, e0 + LH * d + LH))) for d in range(8)])
+            mm(oa[-8:], mm(oa[:-8]))
+            tt(("hi", w), ("Pp", w), (pa, a0), AL.add)
+            ts(("hj", w), ("hi", w), 8191, AL.bitwise_and)
+            lin("hu", ("hu", w), ("hj", w))
+            for (l0, c0) in chunks:
+                gather("gX", ("xg", S_(c0, c0 + 512)), Xw, ("hu", S_(l0, l0 + 32)))
+            lin("hh", ("kh", S_(128 + LH * h, 128 + LH * h + LH)), ("hj", w), 0.0078125, 1536.0 - 0.49609375)
+            mm(grp((pa, a0), [(("Wz", S_(15 - k, 143 - k)), ("xg", S_(o + k, o + 16 * LH, 16))) for k in range(16)]))
+            for j in range(4):
+                lin("gq", ("gq", j, w), (pa, a0), 0.25, 1536.0 - 0.375 + 0.25 * j)
+            mm(grp((pc, a0), [(("Fl", j, full), ("gq", j, w)) for j in range(4)]))
+            dl = grp((pb, a0), [(k_(I3), ("gq", 0, w))] + [(k_(IN1), ("gq", j, w)) for j in (1, 2, 3)] +
+                     [(k_(BE), ("wn", w))])
+            first = mm(dl[:4])
+            ts(("fg", w), (pc, a0), c_(THR), AL.is_gt)
+            mm(grp((pa, a0), [(k_(LO), ("fg", w))]))
+            lin("wn", ("wn", w), (pa, a0), 1.0, 1.0, True)
+            mm(dl[4:], first)
+            ts(("sv", w), (pb, a0), 0.0, AL.is_equal)
+            pre = opt["pre"] >> h & 1
+            if not pre:
+                mm(grp((pa, a0), [(k_(ID), ("E16", w)), (k_(IN2K), ("sv", w))]))
+                lin("eu", ("eu", w), (pa, a0), 1.0, 8.0 - 4096.0, True)
+            mm(grp((pa, a0), [(("Cm", 8, full), ("sv", w))]))
+            lin("sx", ("sx", w, 0), (pa, a0), c_(L14))
+            lin("sx", ("sx", w, 1), (pa, a0), c_(HI8), c_(FB))
+            for j, (l0, c0) in enumerate(chunks):
+                pk = (pc, pb)[j & 1]
+                cw = S_(c0, c0 + 512)
+                mm([((pk, S_(k, 512, 8)), ("Cm", k, full), ("sx", S_(l0, l0 + 32), S_(0, 2)), True, True)
+                    for k in range(8)])
+                steps = (pk, S_(0, 512))
+                if opt["ccp"] >> (2 * h + j) & 1:
+                    vec("lin", ("cs", cw), [steps], (("cs", cw), steps, 1.0, 0.0, False), "S")
+                    steps = ("cs", cw)
+                scan(("xs", cw), ("xg", cw), steps, -8192.0, AL.max, AL.add)
+                if pre:
+                    scan(("ms", cw), ("mg", cw), steps, -8192.0, AL.max, AL.add)
+            ends = S_(o + 15, o + 16 * LH, 16)
+            if not pre:
+                for (l0, c0) in chunks:
+                    cw = S_(c0, c0 + 512)
+                    gather("gM", ("mg", cw), Mw, ("eu", S_(l0, l0 + 32)))
+                    scan(("ms", cw), ("rst", S_(0, 512)), ("mg", cw), 0.0, AL.mult, AL.max)
+            if last:
+                lin("pk", ("ysb", blk, mine), ("ms", ends), 1.0, 2048.0 * pre)
+                lin("pk", ("yzb", blk, mine), ("xs", ends), 1.0, 2048.0)
+            else:
+                lin("pk", ("snd", s, blk, S_(0, Q)), ("ms", ends), 1.0, 2048.0 * pre)
+                lin("pk", ("snd", s, blk, S_(Q, 2 * Q)), ("xs", ends), 1.0, c_(SC))
+                whole = ("snd", s, blk, S_(0, 2 * Q))
+                own = add("Y", "own", (s,), [whole], [], 4096, "dma")
+                me = add("G", "send", (s,), [whole], [], 0, "snd")
+                arrive[s + NS] = add("R", "arr", (s,), [], [], 0, "xch", [me, own])
+        W = 128 // opt["fs"]
+        for r in range(opt["fs"]):
+            tag[0] = r if opt["fs"] > 1 else -1
+            w = S_(W * r, W * r + W)
+            n = W // 16
+
+            def seg(j, base=0):
+                return S_(base + W * j, base + W * j + W)
+
+            def lst(j):
+                return ("lu", S_(3 * n * r + n * j, 3 * n * r + n * j + n))
+            svw = ("sv", w)
+            v0 = 2 * W * r
+            vw = S_(v0, v0 + 2 * W)
+            mm(grp(("p7", seg(0)), [(k_(SG), svw)]))
+            lin("Rl", ("Rl", w), ("p7", seg(0)), 1.0, c_(LC), True)
+            mm(grp(("p6", seg(0)), [(k_(ID), ("E16", w)), (k_(T128), svw), (k_(I128), ("Rl", w))]))
+            lin("V16", ("V16", full), ("p6", seg(0)))
+            mm(grp(("p6", seg(0)), [(k_(ID), ("kh", w)), (k_(ZF), svw)]) +
+               grp(("p6", seg(1)), [(k_(ID), ("kh", seg(r, 128))), (k_(ZF), svw)]))
+            lin("sel", ("sel", vw), ("p6", S_(0, 2 * W)), 1.0, -1600.0, True)
+            mm(grp(("p6", seg(0)), [(k_(BM), ("St", w)), (k_(BM), ("sel", seg(0, v0)))]) +
+               grp(("p6", seg(1)), [(k_(BM), ("St", seg(r, 128))), (k_(BM128), ("sel", seg(1, v0)))]) +
+               [x for hh in range(NS) if W * r <= LH * hh < W * (r + 1) for x in grp(
+                   ("p6", S_(2 * W + LH * hh - W * r, 2 * W + LH * hh - W * r + LH)),
+                   [(k_(BM), ("St", S_(256 + LH * hh, 256 + LH * hh + LH))), (k_(BM), ("lnd", NS * t + hh, blk, S_(Q, 2 * Q))),
+                    (k_(IN16), ("fl", par, S_(LH * hh, LH * hh + LH)))])])
+            l0 = 3 * W * r
+            scan(("ls", S_(l0, l0 + 3 * W)), ("p6", S_(0, 3 * W)), ("cd", S_(0, 3 * W)), -65536.0, AL.max, AL.add)
+            if last:
+                lin("mi", ("mi", w), ("p6", seg(1)), 1.0 / 256, 1.0 - 127.5 / 256)
+            lin("lu", ("lu", S_(3 * n * r, 3 * n * r + 3 * n)), ("ls", S_(l0 + 15, l0 + 3 * W, 16)), 1.0, 16384.0)
+            prev = mm([(("p7", full), ("o129", full), ("FC", full), True, False)])
+            fm = [(("p7", blk, S_(max(p - 1, 0), p + 1)), ("Rr", p - 1, full) if p else ("V16", full),
+                   ("Sel", blk, S_(0 if p else 1, 2)), False, p == 15) for p in range(16)]
+            for p in range(16):
+                if p:
+                    lin("Rr", ("Rr", p - 1, full), ("V16", full), 1.0, -2048.0 * p, True)
+                if p % 2:
+                    prev = mm(fm[p - 1:p + 1], prev)
+                    ops[prev]["n"] *= 4
+            lin("Ft", ("Ft", full), ("p7", full))
+            mm(grp(("p7", S_(128, 256)), [(("Ft", full), k_(ID))]))
+            lin("Ff", ("Ff", w), ("p7", S_(128, 256)))
+            cp(("ind", Cw, lst(2)), ("Ff", w))
+            tt(("xa", w), ("ind", ("xg", S_(0, 2048)), lst(0)), ("xs", S_(16 * W * r + 15, 16 * W * (r + 1), 16)), AL.add)
+            lin("xh", ("xh", w), ("xa", w), 0.5, 1023.75)
+            if not last:
+                cp(("ind", Xw, lst(1)), ("xh", w))
+            else:
+                lc = ("lc", S_(n * r, n * r + n))
+                yw = ("yxb", S_(0, 256))
+                lin("mi", ("mp", w), ("mi", w))
+                lin("mi", ("li", S_(n * r, n * r + n)), ("ls", S_(l0 + W + 15, l0 + 2 * W, 16)), 1.0, 16384.0)
+                ts(("li", S_(8 + n * r, 8 + n * r + n)), ("li", S_(n * r, n * r + n)), 255, AL.bitwise_and)
+                lin("mi", lc, ("li", S_(8 + n * r, 8 + n * r + n)))
+                tt(("old", w), ("ind", Xw, lst(1)), ("mp", w), AL.mult)
+                tt(("adj", w), ("ind", yw, lc), ("old", w), AL.subtract)
+                tt(("vv", w), ("xh", w), ("mp", w), AL.mult)
+                tt(("ind", yw, lc), ("vv", w), ("adj", w), AL.add)
+        tag[0] = -1
+        if not last:
+            mm(grp(("p6", full), [(k_(BM), ("sv", full))]))
+            vec("acc", ("junk", full), [("p6", full)], (("junk", full), ("p6", full), c_(AC)), "S", [c_(AC)])
+            lin("A", ("Ab", S_(0, LH)), ("one", S_(0, LH)), c_(AC))
+        else:
+            prev = None
+            for j, w in enumerate(quarters):
+                lin("cv", ("C16", w), ("C", w))
+                prev = mm([(("p6", S_(0, 256)), ("Dg", m, full), ("C16", S_(256 * m, 256 * m + 256)), m == 0, m == 7)
+                           for m in (2 * j, 2 * j + 1)], prev)
+            lin("yb", ("ycb", S_(0, 256)), ("p6", S_(0, 256)))
+    for (y, src) in (("ys", ("ysb", blk, S_(0, 16))), ("yz", ("yzb", blk, S_(0, 16))),
+                     ("yx", ("yxb", S_(0, 256))), ("yc", ("ycb", S_(0, 256)))):
+        add("Y", "st", (y, src), [src], [], 131072, "dma")
+    return ops
+
+
+def cost(op, eng, pr):
+    r, n = op["rate"], op["n"]
+    if r == "dma":
+        return n / pr["bw"], pr["dma"]
+    if r == "snd":
+        return pr["snd"], 0.0
+    if r == "xch":
+        return 0.0, pr["xch"] - pr["dma"]
+    if r == "pe":
+        return n * pr["pe"], 60.0
+    if r == "gp":
+        return 170.0 + 2 * n * pr["cyc"], 0.0
+    if r in ("g", "sc"):
+        return (50.0 if eng == "V" else 65.0) + n * pr[r] * pr["cyc"], 0.0
+    if eng == "S":
+        return pr["sfix"] + max(64.0, n) * pr["cyc"], 0.0
+    return pr["fix"] + max(64.0, n * r) * pr["cyc"], 0.0
+
+
+def schedule(ops, opt, pr):
+    n = len(ops)
+    rng = np.random.RandomState(opt["seed"])
+    succ = [[] for _ in ops]
+    wait = [0] * n
+    for i, o in enumerate(ops):
+        for d in o["deps"] | o["bank"]:
+            succ[d].append(i)
+            wait[i] += 1
+    rank = [0.0] * n
+    for i in range(n - 1, -1, -1):
+        a, b = cost(ops[i], ops[i]["eng"][0], pr)
+        rank[i] = (a + b + pr["lat"]) * (1.0 + opt["jit"] * float(rng.rand())) + max([rank[j] for j in succ[i]] + [0.0])
+    for i in range(n):
+        rank[i] += opt["pri"].get(ops[i]["key"], 0.0) - opt["stag"] * max(ops[i]["tag"], 0)
+    pred = [sorted(o["deps"] | o["bank"]) for o in ops]
+    tab = [{e: cost(o, e, pr) for e in o["eng"]} for o in ops]
+    lat = pr["lat"]
+
+    def sweep(key, back):
+        before, after = (succ, pred) if back else (pred, succ)
+        wait = [len(x) for x in before]
+        busy = {e: [] for e in "VSPGYR"}
+        end = [0.0] * n
+        where = [None] * n
+        todo = [(key[i], i) for i in range(n) if not wait[i]]
+        while todo:
+            x = min(todo)
+            todo.remove(x)
+            i = x[1]
+            for j in after[i]:
+                wait[j] -= 1
+                if not wait[j]:
+                    todo.append((key[j], j))
+            best = None
+            for e in ops[i]["eng"]:
+                a, b = tab[i][e]
+                st = b if back else 0.0
+                for d in before[i]:
+                    hard = i in ops[d]["deps"] if back else d in ops[i]["deps"]
+                    if where[d] == e and (e == "P" or not hard):
+                        st = max(st, end[d])
+                    else:
+                        st = max(st, end[d] + lat + (b if back else tab[d][where[d]][1]))
+                for (s0, s1, _) in busy[e]:
+                    if st + a <= s0:
+                        break
+                    if s1 > st:
+                        st = s1
+                k = st + a * (opt["vg"] if e == "V" else 1.0)
+                if best is None or k < best[0]:
+                    best = (k, e, st, a)
+            _, e, st, a = best
+            busy[e].append((st, st + a, i))
+            busy[e].sort()
+            end[i] = st + a
+            where[i] = e
+        return busy, where, end
+
+    key = [-x for x in rank]
+    best = None
+    for it in range(opt["it"] + 1):
+        busy, where, end = sweep(key, False)
+        span = max(end[i] + tab[i][where[i]][1] for i in range(n))
+        if best is None or span < best[0]:
+            best = (span, {e: [x[2] for x in busy[e]] for e in busy}, where)
+        if it < opt["it"]:
+            end = sweep([-(end[i] + tab[i][where[i]][1]) for i in range(n)], True)[2]
+            key = [-end[i] - opt["pri"].get(ops[i]["key"], 0.0) * opt["pw"] for i in range(n)]
+    return best[1], best[2]
+
+
+PLAN = {}
+
+
+def rank_program(g, core, T, topo):
+    rank = T.rank_of(core)
+    if rank is None:
+        return
+    if not PLAN:
+        PLAN["ops"] = build(OPT)
+        PLAN["order"], PLAN["where"] = schedule(PLAN["ops"], OPT, PAR0)
+    ops, order, where = PLAN["ops"], PLAN["order"], PLAN["where"]
+    queue = {"V": g.vector, "S": g.scalar, "P": g.tensor, "G": g, "Y": g.sync}
+
+    def ap(x):
+        if not isinstance(x, tuple):
+            return x
+        if x[0] == "ind":
+            return ap(x[1]).indirect(ap(x[2]))
+        if len(x) == 2 and x[0] == "p7":
+            return T[x[0]][:, x[1].start // 16:x[1].stop // 16, :]
+        return T[x[0]][(slice(None),) + x[1:]]
+
+    deps = [[d for d in o["deps"] if where[d] != "P" or where[i] != "P"] + [d for d in o["bank"] if where[d] != where[i]]
+            for i, o in enumerate(ops)]
+    needed = set(d for i, o in enumerate(ops) for d in deps[i] if o["kind"] != "arr")
+    signal = {}
+    total = {}
+    for e in "VSPG":
+        n = 0
+        for i in order[e]:
+            if i in needed:
+                n += 1
+                signal[i] = ("q" + e, n)
+        total["q" + e] = n
+    for i in order["Y"]:
+        if ops[i]["kind"] == "ld":
+            signal[i] = ("ld%d" % ops[i]["args"][2], 16)
+    nr = len(T.cores)
+    per = min(len(topo.engines(core, c)) for c in T.cores if c != core) // nr
+    for i in order["R"]:
+        signal[i] = ("arr%d" % ops[i]["args"][0], per * (nr - 1) + 16)
+    sends = 0
+    for e in "YGPSV":
+        q = queue[e]
+        seen = {}
+        for i in order[e]:
+            want = {}
+            for d in deps[i]:
+                s, v = signal[d]
+                want[s] = max(want.get(s, 0), v)
+            for s in sorted(want):
+                if seen.get(s, 0) < want[s]:
+                    q.wait_ge(T.sem[s], want[s])
+                    seen[s] = want[s]
+            k, a = ops[i]["kind"], ops[i]["args"]
+            if k == "cp" or (k == "gat" and e == "V"):
+                ins = q.tensor_copy(ap(a[0]), ap(a[1]))
+            elif k == "gat":
+                ins = q.activation(ap(a[0]), ap(a[1]), AF.Copy)
+            elif k == "lin" and e == "S":
+                f = AF.Relu if a[4] else (AF.Identity if isinstance(a[3], tuple) else AF.Copy)
+                ins = q.activation(ap(a[0]), ap(a[1]), f, ap(a[3]), ap(a[2]))
+            elif k == "lin" and a[4]:
+                ins = q.tensor_scalar(ap(a[0]), ap(a[1]), ap(a[3]), 0.0, AL.add, AL.max)
+            elif k == "lin":
+                ins = q.tensor_scalar(ap(a[0]), ap(a[1]), ap(a[2]), ap(a[3]), AL.mult, AL.add)
+            elif k == "tt":
+                ins = q.tensor_tensor(ap(a[0]), ap(a[1]), ap(a[2]), a[3])
+            elif k == "ts" and a[5] is None:
+                ins = q.tensor_scalar(ap(a[0]), ap(a[1]), ap(a[2]), None, a[4])
+            elif k == "ts":
+                ins = q.tensor_scalar(ap(a[0]), ap(a[1]), ap(a[2]), ap(a[3]), a[4], a[5])
+            elif k == "scan":
+                ins = q.tensor_tensor_scan(ap(a[0]), ap(a[1]), ap(a[2]), a[3], a[4], a[5])
+            elif k == "ms":
+                ins = q.memset(ap(a[0]), a[1])
+            elif k == "acc":
+                ins = q.activation(ap(a[0]), ap(a[1]), AF.Relu, 2.0, -1.0, accum_out=ap(a[2]))
+            elif k == "mm":
+                for m in a:
+                    ins = q.matmul(ap(m[0]), ap(m[1]), ap(m[2]), m[3], m[4])
+            elif k == "iota" and SCRATCH[a[0][0]][2] == I32:
+                ins = q.iota(ap(a[0]), a[1], a[2], a[3])
+            elif k == "iota":
+                ins = q.iota(ap(a[0]), a[1], a[2], a[3], allow_small_or_imprecise_dtypes=True)
+            elif k == "diag":
+                ins = q.affine_select(ap(a[0]), ap(a[1]), [[-1, 128]], AL.is_equal, 0.0, 0, 1)
+            elif k == "own":
+                q.dma_start(T.lnd[:, a[0] + NS, rank], T.snd[:, a[0], rank]).then_inc(T.sem["arr%d" % a[0]], 16)
+            elif k == "ld":
+                q.dma_start(ap(a[0]), ap(a[1])).then_inc(T.sem["ld%d" % a[2]], 16)
+            elif k == "st":
+                q.dma_start(T[a[0]][:], ap(a[1])).then_inc(T.sem.stored, 16)
+            elif k == "send":
+                tr = []
+                for j in range(1, nr):
+                    b = (rank + j) % nr
+                    rid, pid, _ = topo.addr(T.cores[b])
+                    mask = sum(1 << x for x in topo.engines(core, T.cores[b])[per * (j - 1):per * j])
+                    tr.append(RemoteDMATransfer(dst_ids=[DstId(rid=rid, pnc=pid)], dma_engine_mask=mask,
+                                                remote_sem=T.sem["arr%d" % a[0]], src=T.snd[:, a[0], b],
+                                                dst=T.lnd[:, a[0] + NS, rank]))
+                q.remote_dma_fused(tr, local_sem=T.sem.left)
+                sends += 1
+            if i in signal and e != "Y":
+                ins.then_inc(T.sem[signal[i][0]], 1)
+        if e == "Y":
+            q.wait_ge(T.sem.stored, 64)
+            for s in sorted(total):
+                q.wait_ge(T.sem[s], total[s])
+        if e == "G":
+            q.wait_ge(T.sem.left, sends * per * (nr - 1))

@@ -21,18 +21,18 @@ SCRATCH = {
     "Sf": sb(384, F32), "St": sb(384, F16), "rst": sb(512, BF), "cd": sb(384, BF), "col": sb(32, F32),
     "R": sb(17, F32), "Rd": sb(16, F32), "Rd2": sb(16, F32), "tny": sb(64, F32), "J": sb(160, F16),
     "Y": sb([16, 160], F16), "Wz": sb(144, BF),
-    "Sel": sb([8, 2], F32), "o129": sb(128, BF), "FC": sb(128, BF), "Ft": sb(128, F16), "sx": sb([128, 2], F16),
-    "K": sb([22, 128], F16), "Ab": sb(64, F16), "Cy": sb([8, 32], F16), "Dm": sb([8, 128], F16),
+    "Sel": sb([2, 8, 2], F16), "o129": sb(128, BF), "FC": sb(128, BF), "Ft": sb(128, F16), "sx": sb([128, 2], F16),
+    "K": sb([22, 128], F16), "Ab": sb(128, F16), "Cy": sb([8, 32], F16), "Dm": sb([8, 128], F16),
     "Om": sb([8, 128], F16), "Cm": sb([9, 128], F16), "Fl": sb([4, 128], F16), "Bj": sb([4, 128], F16),
-    "Dg": sb([32, 128], BF), "one": sb(64, F16),
-    "snd": sb([3 * NS, 8, 2 * Q], F16), "lnd": sb([4 * NS, 8, 2 * Q], F16),
+    "Dg": sb([32, 128], BF), "one": sb(128, F16),
+    "snd": sb([3, 8, 32], F16), "lnd": sb([4, 8, 32], F16),
     "Sl": sb(128, U16), "fl": sb([2, 128], F16), "G": sb(2048, F16), "E16": sb(128, F16),
     "Pp": sb(128, F32), "eq": sb(1024, F16), "hi": sb(128, I32), "hj": sb(128, I32),
     "hu": sb(128, U16), "kh": sb(256, F16), "xg": sb(2048, BF), "gq": sb([4, 128], F16), "fg": sb(128, F16),
     "wn": sb(128, F16), "sv": sb(128, F16), "eu": sb(128, U16), "mg": sb(2048, F16), "ms": sb(2048, F16),
-    "xs": sb(2048, F16), "Rl": sb(128, F16), "V16": sb(128, F32), "Rr": sb([15, 128], F32),
+    "xs": sb(2048, F16), "Rl": sb(128, F16), "eh": sb(128, F16), "V16": sb(256, F16), "Rr": sb([15, 256], F16),
     "Ff": sb(128, F32), "sel": sb(256, F16), "ls": sb(384, F32), "lu": sb(24, U16), "junk": sb(128, F32),
-    "xa": sb(128, F32), "xh": sb(128, I32), "cs": sb(2048, BF),
+    "xa": sb(128, F32), "xh": sb(128, I32), "cs": sb(2048, BF), "ct": sb(16, BF), "cu": sb(128, U16),
     "yxb": sb(256, F32), "ycb": sb(256, F32), "ysb": sb([8, 16], F32), "yzb": sb([8, 16], BF), "C16": sb(2048, F16),
     "mi": sb(128, I32), "mp": sb(128, F32), "li": sb(16, I32), "lc": sb(8, U16), "old": sb(128, F32),
     "adj": sb(128, F32), "vv": sb(128, F32),
@@ -42,12 +42,12 @@ for _b in range(8):
 SEMAPHORES = ["qV", "qS", "qP", "qG", "left", "stored"] + ["ld%d" % s for s in range(7)] + \
     ["arr%d" % s for s in range(3 * NS)]
 
-LC, CC, CP, PAR, NL, L15, L14, WW, DG, NDG, THR, CQ, FB, STC, W8, SC, AC, KK, HI8 = range(19)
+LC, CC, CP, PAR, NL, L15, L14, WW, DG, NDG, THR, CQ, FB, STC, W8, SC, AC, KK, HI8, L15B = range(20)
 BM, DMB, DMN, DMZ, ID, IN1, I3, I128, IN128, IN2K, IN16, T128, SG, ZF, BM128, LO, BE, TMP, TM2, TM3, B32, CN = range(22)
 
-PAR0 = {"cyc": 1.04, "fix": 30.0, "g": 1.56, "sc": 3.8, "pe": 0.55, "lat": 60.0, "xch": 3500.0, "snd": 900.0,
-        "bw": 400.0, "dma": 2000.0, "sfix": 65.0}
-OPT = {'seed':3226,'jit':0.05,'vg':1.6,'stag':0,'fs':1,'ccp':14,'pri':{'linFt-1':-4000,'tshj1':2000,'mmp20':4000,'linlnd0':-2000,'accjunk-1':-4000,'scanxs1':-500,'linAb-1':-500,'tthi1':2000,'linfl0':-1000,'send1':-500,'lincs0':500,'linycb-1':1000,'scanls-1':500,'ttvv-1':-500,'linlu-1':-1000,'linlc-1':1000,'tshj0':2000,'linRl-1':4000,'linsel-1':4000,'own1':-500,'lincs1':-500},'eng':{'xh':'V','mi':'V','Sl':'S','pk':'S','fl':'S','wn':'S','hh':'S','Rl':'S','A':'V','yb':'V','cv':'S','z16':'S','V16':'V','sx':'V','eh':'S','sel':'S'},'it':1,'pw':0.1,'pre':3}
+PAR0 = {"cyc": 0.87, "fix": 40.0, "g": 1.56, "sc": 3.8, "pe": 0.5, "lat": 170.0, "xch": 3200.0, "snd": 900.0,
+        "bw": 400.0, "dma": 2000.0, "sfix": 30.0}
+OPT = {'seed':0,'jit':0,'vg':1.6,'stag':0,'fs':1,'ccp':1,'pri':{'ttold-1':1000,'tsfg1':-2000,'tssv0':2000,'tttny-1':-1000,'tski-1':-4000,'mmp00':-1000,'iotat5-1':-2000,'scanms0':4000,'linyzb0':1000,'ldcmb-1':-4000,'ttadj-1':4000,'mmp41':2000,'linkh-1':-1000,'linDm-1':2000,'linsnd1':-500,'linwn1':-2000,'linRl-1':-4000,'linSel-1':2000,'cpC-1':1000,'lineu0':2000,'linFf-1':-2000,'linsel-1':4000,'gatxg0':500,'ttcol-1':1000,'linmi-1':-2000,'tsfg0':-1000,'linmp-1':-4000,'diagDg-1':-4000,'ttxa-1':500},'eng':{'V16':'S','pk':'S','k':'S','z16':'V','mi':'S','eu':'V','xh':'S','Sl':'S','lu':'S','Ff':'S'},'it':1,'pw':0.1,'pre':3,'cg':15,'mg':1}
 
 
 def S_(a, b, c=None):
@@ -168,7 +168,7 @@ def build(opt):
     load(5, ("z0b", S_(0, 8), S_(0, 16)), ("z0", full), 32768)
     load(6, ("X", S_(0, 8192)), ("x0", S_(0, 8192)), 2097152)
 
-    DJ = ("DJ", S_(0, 160)); D0 = ("DJ", full); D4 = ("DJ", S_(0, 144))
+    DJ = ("DJ", S_(0, 160)); D0 = ("DJ", full)
     R0 = ("R", S_(0, 1))
     iota(("ki", S_(0, 1)), [[0, 1]], 0, 1)
     iota(("ia", S_(0, 17)), [[1, 17]], 0, 0)
@@ -192,14 +192,14 @@ def build(opt):
     ts(("J", S_(0, 160)), DJ, 16.0, AL.is_equal)
     for a in range(16):
         lin("k", ("Y", a, S_(0, 160)), ("J", S_(0, 160)), ("R", S_(a, a + 1)))
-    for j, src, mul, addc in ((NL, LC, -1.0, 0.0), (L15, LC, -1.0, 15.0), (WW, PAR, -2.0, 1.0),
+    for j, src, mul, addc in ((L15B, LC, -1.0, 15.0), (NL, LC, -1.0, 0.0), (WW, PAR, -2.0, 1.0),
                               (CQ, CC, 0.25, 0.0), (KK, LC, 1.0, 1536.0)):
         lin("k", c_(j), c_(src), mul, addc)
     ts(k_(BM), ("BI", full), c_(NL), AL.is_equal)
     lin("k", k_(TMP), k_(BM), -1024.0, 1024.0)
     tt(k_(DMB), D0, k_(TMP), AL.add)
     ts(k_(ID), k_(DMB), 0.0, AL.is_equal)
-    for j, v in ((IN1, -1.0), (I3, 3.0), (I128, 2048.0), (IN2K, 4096.0), (IN16, -16.0)):
+    for j, v in ((IN1, -1.0), (I3, 3.0), (I128, 128.0), (IN128, -128.0), (IN2K, 4096.0), (IN16, -16.0)):
         lin("k", k_(j), k_(ID), v)
     for rep in range(2):
         lin("k", ("Cy", S_(0, 8), S_(16 * rep, 16 * rep + 16)), k_(ID))
@@ -213,7 +213,7 @@ def build(opt):
     lin("k", c_(W8), y_(7, 8), 613.0)
     for d in range(1, 9):
         ts(("Om", d - 1, full), k_(DMB), y_(7 + d, 8 + d), AL.is_equal, 613.0 if d < 8 else c_(W8), AL.mult)
-    ts(("Wz", S_(0, 144)), D4, c_(L15), AL.is_equal, c_(WW), AL.mult)
+    ts(("Wz", S_(0, 144)), ("DJ", S_(0, 144)), c_(L15B), AL.is_equal, c_(WW), AL.mult)
     lin("k", k_(BM128), k_(BM), 128.0)
     lin("k", k_(BE), k_(BM), c_(CQ))
     ms(("t5", S_(0, 1)), 0.0)
@@ -241,31 +241,38 @@ def build(opt):
     tt(k_(LO), k_(TM3), k_(BM), AL.mult)
     tt(("Rd", S_(0, 16)), ("R", S_(0, 16)), ("R", S_(1, 17)), AL.subtract)
     ts(k_(TM2), k_(DMB), -1.0, AL.is_equal, -2048.0, AL.mult)
-    tt(("Cm", 8, full), k_(TM2), k_(I128), AL.add)
-    tt(("Rd2", S_(0, 8)), ("R", S_(0, 8)), ("R", S_(8, 16)), AL.add)
-    for j in range(8):
-        lin("k", ("Cm", j, full), k_(BM), ("Rd2", S_(j, j + 1)))
-    ts(c_(L14), c_(LC), 8.0, AL.is_lt)
-    ts(c_(HI8), c_(LC), 8.0, AL.is_ge)
-    lin("k", c_(FB), ("R", S_(15, 16)), -4096.0)
-    ms(("one", S_(0, 64)), 1.0)
-    ms(("rst", S_(0, 512)), 1.0)
-    ms(("rst", S_(0, 512, 16)), 0.0)
+    lin("k", k_(TM3), k_(ID), 2048.0)
+    tt(("Cm", 8, full), k_(TM2), k_(TM3), AL.add)
+    if opt["cg"] != 15:
+        tt(("Rd2", S_(0, 8)), ("R", S_(0, 8)), ("R", S_(8, 16)), AL.add)
+        for j in range(8):
+            lin("k", ("Cm", j, full), k_(BM), ("Rd2", S_(j, j + 1)))
+        ts(c_(L14), c_(LC), 8.0, AL.is_lt)
+        ts(c_(HI8), c_(LC), 8.0, AL.is_ge)
+        lin("k", c_(FB), ("R", S_(15, 16)), -4096.0)
+    if opt["cg"]:
+        lin("k", ("ct", S_(0, 16)), ("ia", S_(0, 16)), 2048.0, -4096.0)
+        lin("k", c_(L15), ("R", S_(15, 16)), -2.0, 2.0)
+    ms(("one", full), 1.0)
+    if opt["pre"] != 3:
+        ms(("rst", S_(0, 512)), 1.0)
+        ms(("rst", S_(0, 512, 16)), 0.0)
     lin("k", ("cd", S_(0, 16)), ("Rd", S_(0, 16)), 16384.0)
     lin("k", ("cd", S_(15, 16)), ("Rd", S_(15, 16)), 16384.0, -32768.0)
     for a, b in ((16, 16), (32, 32), (64, 64), (128, 128), (256, 128)):
         lin("k", ("cd", S_(a, a + b)), ("cd", S_(0, b)))
     tt(k_(DMN), D0, k_(TMP), AL.subtract)
-    ts(k_(T128), k_(DMN), 0.0, AL.is_gt, 2048.0, AL.mult)
+    ts(k_(T128), k_(DMN), 0.0, AL.is_gt, 128.0, AL.mult)
     tt(k_(DMZ), D0, k_(BM), AL.mult)
     ts(k_(TM2), k_(DMZ), -1.0, AL.max, 1.0, AL.min)
     lin("k", k_(TM3), k_(ID), -32.0)
     tt(k_(SG), k_(TM3), k_(TM2), AL.subtract)
     tt(k_(TM2), k_(I128), k_(T128), AL.subtract)
-    lin("k", k_(ZF), k_(TM2), 1.0 / 32)
-    ms(("o129", full), 16.0)
-    for j in range(2):
-        lin("k", ("Sel", S_(0, 8), j), ("K", BM, S_(0, 128, 16)), 2.0 * j - 1.0)
+    lin("k", k_(ZF), k_(TM2), 0.5)
+    ms(("o129", full), 129.0)
+    for v in range(2):
+        for j in range(2):
+            lin("k", ("Sel", v, S_(0, 8), j), ("K", BM, S_(0, 128, 16)), (2.0 * j - 1.0) * 128.0 ** v)
     lin("k", ("kh", full), k_(BM), 0.0, c_(KK))
     ts(c_(STC), ("R", S_(1, 2)), 24576.0, AL.mult, ("R", S_(2, 3)), AL.subtract)
     lin("k", ("St", S_(0, 256)), ("Sf", S_(0, 256)), R0)
@@ -287,6 +294,7 @@ def build(opt):
     for t in range(RO):
         last = t == RO - 1
         par = t & 1
+        pks = []
         if last:
             prev = None
             for j in range(16):
@@ -299,22 +307,25 @@ def build(opt):
             o = 16 * LH * h
             pa, pb, pc = "p%d" % (3 * h), "p%d" % (3 * h + 1), "p%d" % (3 * h + 2)
             a0 = S_(0, LH)
-            s = NS * t + h
             mine = S_(Q * h, Q * h + Q)
-            zz = ("lnd", s, blk, S_(Q, 2 * Q))
+            q0 = 2 * Q * h
+            zz = ("lnd", t, blk, S_(q0 + Q, q0 + 2 * Q))
             if t == 0:
                 lin("Sl", ("Sl", w), ("s0b", blk, mine))
                 lin("z16", zz, ("z0b", blk, mine), 1.0, R0)
             else:
-                ops[lin("Sl", ("Sl", w), ("lnd", s, blk, S_(0, Q)))]["deps"].add(arrive[s])
+                ops[lin("Sl", ("Sl", w), ("lnd", t, blk, S_(q0, q0 + Q)))]["deps"].add(arrive[t, h])
             chunks = [(LH * h + 32 * j, o + 512 * j) for j in range(LH // 32)]
             for (l0, c0) in chunks:
                 gather("gC", ("G", S_(c0, c0 + 512)), Cw, ("Sl", S_(l0, l0 + 32)))
-            mm(grp((pc, a0), [(k_(B32), zz)]), arrive.get(s))
+            mm(grp((pc, a0), [(k_(B32), zz)]), arrive.get((t, h)))
             lin("fl", ("fl", par, w), (pc, a0), 2.0, 1536.0 - 0.0625 - 0.46875)
-            mm(grp((pa, a0), [(("Y", (k + t) & 15, S_(16 + ((k + t) & 15) - k, 144 + ((k + t) & 15) - k)),
-                               ("G", S_(o + k, o + 16 * LH, 16))) for k in range(16)]))
-            lin("E16", ("E16", w), (pa, a0))
+            a1 = S_(128, 128 + LH)
+
+            def fold(src, rhs, wide, z0):
+                mm(grp((pa, a1), [(rhs(k), (src, S_(o + k, o + 16 * LH, 16))) for k in range(16)]))
+            fold("G", lambda k: ("Y", (k + t) & 15, S_(16 + ((k + t) & 15) - k, 144 + ((k + t) & 15) - k)), 2, 16 * h)
+            lin("E16", ("E16", w), (pa, a1))
             if opt["pre"] >> h & 1:
                 lin("eu", ("eu", w), ("E16", w), 1.0, 8.0)
                 for (l0, c0) in chunks:
@@ -332,9 +343,9 @@ def build(opt):
             for (l0, c0) in chunks:
                 gather("gX", ("xg", S_(c0, c0 + 512)), Xw, ("hu", S_(l0, l0 + 32)))
             lin("hh", ("kh", S_(128 + LH * h, 128 + LH * h + LH)), ("hj", w), 0.0078125, 1536.0 - 0.49609375)
-            mm(grp((pa, a0), [(("Wz", S_(15 - k, 143 - k)), ("xg", S_(o + k, o + 16 * LH, 16))) for k in range(16)]))
+            fold("xg", lambda k: ("Wz", S_(15 - k, 143 - k)), 1, 16 * h)
             for j in range(4):
-                lin("gq", ("gq", j, w), (pa, a0), 0.25, 1536.0 - 0.375 + 0.25 * j)
+                lin("gq", ("gq", j, w), (pa, a1), 0.25, 1536.0 - 0.375 + 0.25 * j)
             mm(grp((pc, a0), [(("Fl", j, full), ("gq", j, w)) for j in range(4)]))
             dl = grp((pb, a0), [(k_(I3), ("gq", 0, w))] + [(k_(IN1), ("gq", j, w)) for j in (1, 2, 3)] +
                      [(k_(BE), ("wn", w))])
@@ -349,15 +360,23 @@ def build(opt):
                 mm(grp((pa, a0), [(k_(ID), ("E16", w)), (k_(IN2K), ("sv", w))]))
                 lin("eu", ("eu", w), (pa, a0), 1.0, 8.0 - 4096.0, True)
             mm(grp((pa, a0), [(("Cm", 8, full), ("sv", w))]))
-            lin("sx", ("sx", w, 0), (pa, a0), c_(L14))
-            lin("sx", ("sx", w, 1), (pa, a0), c_(HI8), c_(FB))
+            cg = opt["cg"] >> (2 * h) & 3
+            if cg != 3:
+                lin("sx", ("sx", w, 0), (pa, a0), c_(L14))
+                lin("sx", ("sx", w, 1), (pa, a0), c_(HI8), c_(FB))
+            if cg:
+                lin("sx", ("cu", w), (pa, a0), 1.0 / 2048, c_(L15))
             for j, (l0, c0) in enumerate(chunks):
                 pk = (pc, pb)[j & 1]
                 cw = S_(c0, c0 + 512)
-                mm([((pk, S_(k, 512, 8)), ("Cm", k, full), ("sx", S_(l0, l0 + 32), S_(0, 2)), True, True)
-                    for k in range(8)])
                 steps = (pk, S_(0, 512))
-                if opt["ccp"] >> (2 * h + j) & 1:
+                if cg >> j & 1:
+                    gather("gS", ("cs", cw), ("ct", S_(0, 16)), ("cu", S_(l0, l0 + 32)))
+                    steps = ("cs", cw)
+                else:
+                    mm([((pk, S_(k, 512, 8)), ("Cm", k, full), ("sx", S_(l0, l0 + 32), S_(0, 2)), True, True)
+                        for k in range(8)])
+                if opt["ccp"] >> (2 * h + j) & 1 and not cg >> j & 1:
                     vec("lin", ("cs", cw), [steps], (("cs", cw), steps, 1.0, 0.0, False), "S")
                     steps = ("cs", cw)
                 scan(("xs", cw), ("xg", cw), steps, -8192.0, AL.max, AL.add)
@@ -373,12 +392,18 @@ def build(opt):
                 lin("pk", ("ysb", blk, mine), ("ms", ends), 1.0, 2048.0 * pre)
                 lin("pk", ("yzb", blk, mine), ("xs", ends), 1.0, 2048.0)
             else:
-                lin("pk", ("snd", s, blk, S_(0, Q)), ("ms", ends), 1.0, 2048.0 * pre)
-                lin("pk", ("snd", s, blk, S_(Q, 2 * Q)), ("xs", ends), 1.0, c_(SC))
-                whole = ("snd", s, blk, S_(0, 2 * Q))
-                own = add("Y", "own", (s,), [whole], [], 4096, "dma")
-                me = add("G", "send", (s,), [whole], [], 0, "snd")
-                arrive[s + NS] = add("R", "arr", (s,), [], [], 0, "xch", [me, own])
+                pks.append(lin("pk", ("snd", t, blk, S_(q0, q0 + Q)), ("ms", ends), 1.0, 2048.0 * pre))
+                pks.append(lin("pk", ("snd", t, blk, S_(q0 + Q, q0 + 2 * Q)), ("xs", ends), 1.0, c_(SC)))
+                if not opt["mg"]:
+                    a = (2 * t + h, t, S_(q0, q0 + 2 * Q))
+                    own = add("Y", "own", a, [], [], 4096, "dma", pks[-2:])
+                    me = add("G", "send", a, [], [], 0, "snd", pks[-2:])
+                    arrive[t + 1, h] = add("R", "arr", a, [], [], 0, "xch", [me, own])
+                elif h == NS - 1:
+                    a = (t, t, S_(0, 32))
+                    own = add("Y", "own", a, [], [], 8192, "dma", pks)
+                    me = add("G", "send", a, [], [], 0, "snd", pks)
+                    arrive[t + 1, 0] = arrive[t + 1, 1] = add("R", "arr", a, [], [], 0, "xch", [me, own])
         W = 128 // opt["fs"]
         for r in range(opt["fs"]):
             tag[0] = r if opt["fs"] > 1 else -1
@@ -395,8 +420,12 @@ def build(opt):
             vw = S_(v0, v0 + 2 * W)
             mm(grp(("p7", seg(0)), [(k_(SG), svw)]))
             lin("Rl", ("Rl", w), ("p7", seg(0)), 1.0, c_(LC), True)
-            mm(grp(("p6", seg(0)), [(k_(ID), ("E16", w)), (k_(T128), svw), (k_(I128), ("Rl", w))]))
-            lin("V16", ("V16", full), ("p6", seg(0)))
+            lin("eh", ("eh", w), ("E16", w), 0.0078125, 1536.0 - 0.49609375)
+            pl = [(k_(T128), svw), (k_(I128), ("Rl", w))]
+            mm(grp(("p6", seg(0)), [(k_(ID), ("E16", w)), (k_(IN128), ("eh", w))] + pl) +
+               grp(("p6", seg(1)), [(k_(ID), ("eh", w))] + pl))
+            lin("V16", ("V16", seg(0)), ("p6", seg(0)), 1.0, 196608.0)
+            lin("V16", ("V16", seg(1)), ("p6", seg(1)), 1.0, -1536.0)
             mm(grp(("p6", seg(0)), [(k_(ID), ("kh", w)), (k_(ZF), svw)]) +
                grp(("p6", seg(1)), [(k_(ID), ("kh", seg(r, 128))), (k_(ZF), svw)]))
             lin("sel", ("sel", vw), ("p6", S_(0, 2 * W)), 1.0, -1600.0, True)
@@ -404,7 +433,7 @@ def build(opt):
                grp(("p6", seg(1)), [(k_(BM), ("St", seg(r, 128))), (k_(BM128), ("sel", seg(1, v0)))]) +
                [x for hh in range(NS) if W * r <= LH * hh < W * (r + 1) for x in grp(
                    ("p6", S_(2 * W + LH * hh - W * r, 2 * W + LH * hh - W * r + LH)),
-                   [(k_(BM), ("St", S_(256 + LH * hh, 256 + LH * hh + LH))), (k_(BM), ("lnd", NS * t + hh, blk, S_(Q, 2 * Q))),
+                   [(k_(BM), ("St", S_(256 + LH * hh, 256 + LH * hh + LH))), (k_(BM), ("lnd", t, blk, S_(2 * Q * hh + Q, 2 * Q * hh + 2 * Q))),
                     (k_(IN16), ("fl", par, S_(LH * hh, LH * hh + LH)))])])
             l0 = 3 * W * r
             scan(("ls", S_(l0, l0 + 3 * W)), ("p6", S_(0, 3 * W)), ("cd", S_(0, 3 * W)), -65536.0, AL.max, AL.add)
@@ -412,14 +441,13 @@ def build(opt):
                 lin("mi", ("mi", w), ("p6", seg(1)), 1.0 / 256, 1.0 - 127.5 / 256)
             lin("lu", ("lu", S_(3 * n * r, 3 * n * r + 3 * n)), ("ls", S_(l0 + 15, l0 + 3 * W, 16)), 1.0, 16384.0)
             prev = mm([(("p7", full), ("o129", full), ("FC", full), True, False)])
-            fm = [(("p7", blk, S_(max(p - 1, 0), p + 1)), ("Rr", p - 1, full) if p else ("V16", full),
-                   ("Sel", blk, S_(0 if p else 1, 2)), False, p == 15) for p in range(16)]
+            fm = [(("p7", blk, S_(max(p - 1, 0), p + 1)), ("Rr", p - 1, seg(v)) if p else ("V16", seg(v)),
+                   ("Sel", v, blk, S_(0 if p else 1, 2)), False, p == 15 and v == 1) for p in range(16) for v in range(2)]
             for p in range(16):
                 if p:
-                    lin("Rr", ("Rr", p - 1, full), ("V16", full), 1.0, -2048.0 * p, True)
+                    lin("Rr", ("Rr", p - 1, vw), ("V16", vw), 1.0, -128.0 * p, True)
                 if p % 2:
-                    prev = mm(fm[p - 1:p + 1], prev)
-                    ops[prev]["n"] *= 4
+                    prev = mm(fm[2 * p - 2:2 * p + 2], prev)
             lin("Ft", ("Ft", full), ("p7", full))
             mm(grp(("p7", S_(128, 256)), [(("Ft", full), k_(ID))]))
             lin("Ff", ("Ff", w), ("p7", S_(128, 256)))
@@ -636,7 +664,7 @@ def rank_program(g, core, T, topo):
             elif k == "diag":
                 ins = q.affine_select(ap(a[0]), ap(a[1]), [[-1, 128]], AL.is_equal, 0.0, 0, 1)
             elif k == "own":
-                q.dma_start(T.lnd[:, a[0] + NS, rank], T.snd[:, a[0], rank]).then_inc(T.sem["arr%d" % a[0]], 16)
+                q.dma_start(T.lnd[:, a[1] + 1, rank, a[2]], T.snd[:, a[1], rank, a[2]]).then_inc(T.sem["arr%d" % a[0]], 16)
             elif k == "ld":
                 q.dma_start(ap(a[0]), ap(a[1])).then_inc(T.sem["ld%d" % a[2]], 16)
             elif k == "st":
@@ -648,8 +676,8 @@ def rank_program(g, core, T, topo):
                     rid, pid, _ = topo.addr(T.cores[b])
                     mask = sum(1 << x for x in topo.engines(core, T.cores[b])[per * (j - 1):per * j])
                     tr.append(RemoteDMATransfer(dst_ids=[DstId(rid=rid, pnc=pid)], dma_engine_mask=mask,
-                                                remote_sem=T.sem["arr%d" % a[0]], src=T.snd[:, a[0], b],
-                                                dst=T.lnd[:, a[0] + NS, rank]))
+                                                remote_sem=T.sem["arr%d" % a[0]], src=T.snd[:, a[1], b, a[2]],
+                                                dst=T.lnd[:, a[1] + 1, rank, a[2]]))
                 q.remote_dma_fused(tr, local_sem=T.sem.left)
                 sends += 1
             if i in signal and e != "Y":

@@ -1,3 +1,4 @@
+import math
 import numpy as np
 from concourse.bass import DstId, RemoteDMATransfer
 from concourse.mybir import AluOpType, ActivationFunctionType
@@ -6,7 +7,8 @@ AL = AluOpType
 AF = ActivationFunctionType
 RO, NS = 4, 2
 LH = 128 // NS
-Q = 16 // NS
+NB = 8 // NS
+STEP = 2048.0
 F16, BF, F32, I32, U16 = "float16", "bfloat16", "float32", "int32", "uint16"
 
 
@@ -15,56 +17,64 @@ def sb(n, d):
 
 
 SCRATCH = {
-    "s0b": sb([8, 16], I32), "z0b": sb([8, 16], BF), "cmb": sb(2048, I32), "X": sb(8192, BF),
-    "C": sb(2048, I32), "M": sb(2056, I32),
+    "s0b": sb(128, I32), "z0b": sb(128, BF), "cmb": sb(2048, I32), "X": sb(8192, BF),
+    "C": sb(2048, I32), "M": sb(2064, I32),
     "DJ": sb(160, BF), "BI": sb(128, BF), "CcM": sb(128, BF), "ki": sb(8, I32), "ia": sb(17, F32), "t5": sb(5, F32),
     "Sf": sb(384, F32), "St": sb(384, F16), "rst": sb(512, BF), "cd": sb(384, BF), "col": sb(32, F32),
-    "R": sb(17, F32), "Rd": sb(16, F32), "Rd2": sb(16, F32), "tny": sb(64, F32), "J": sb(160, F16),
-    "Y": sb([16, 160], F16), "Wz": sb(144, BF),
-    "Sel": sb([2, 8, 2], F16), "o129": sb(128, BF), "FC": sb(128, BF), "Ft": sb(128, F16), "sx": sb([128, 2], F16),
-    "K": sb([22, 128], F16), "Ab": sb(128, F16), "Cy": sb([8, 32], F16), "Dm": sb([8, 128], F16),
-    "Om": sb([8, 128], F16), "Cm": sb([9, 128], F16), "Fl": sb([4, 128], F16), "Bj": sb([4, 128], F16),
+    "R": sb(17, F32), "Rd": sb(16, F32), "tny": sb(64, F32), "Z": sb(2064, BF), "Wz": sb(144, BF),
+    "Sel": sb([2, 8, 2], F16), "o129": sb(128, BF), "FC": sb(128, BF), "Ft": sb(128, F16), "Fw": sb([2, 272], F16),
+    "K": sb([25, 128], F16), "Ab": sb(128, F16), "Cy": sb([8, 32], F16), "Dm": sb([8, 128], F16),
+    "Om": sb([8, 128], F16), "Cm": sb([8, 128], BF), "Fl": sb([4, 128], F16), "Bj": sb([4, 128], F16),
     "Dg": sb([32, 128], BF), "one": sb(128, F16),
-    "snd": sb([3, 8, 32], F16), "lnd": sb([4, 8, 32], F16),
-    "Sl": sb(128, U16), "fl": sb([2, 128], F16), "G": sb(2048, F16), "E16": sb(128, F16),
-    "Pp": sb(128, F32), "eq": sb(1024, F16), "hi": sb(128, I32), "hj": sb(128, I32),
+    "mS0": sb([21, 64], U16), "mS1": sb([6, 64], U16), "mz0": sb([21, 64], F16), "mz1": sb([6, 64], F16),
+    "mc0": sb([21, 4, 32], U16), "mc1": sb([6, 4, 32], U16), "Sl": sb(128, U16), "zf": sb(128, F16), "fl": sb([2, 128], F16), "G": sb(2048, F16), "E16": sb(128, F16),
+    "Pp": sb(128, F32), "eq": sb(1024, F16), "Qm": sb(128, F32), "hr": sb(128, BF), "I32": sb(128, F32),
+    "c16": sb(64, F16), "J": sb(256, BF), "OH": sb([8, 256], F16), "cT": sb(8, F32), "o16": sb(128, F16),
+    "R32": sb([16, 128], F32), "Sel32": sb([8, 2], F32), "Fw32": sb(272, F32), "Fz": sb([72, 16], F16), "yc0": sb(256, F32),
     "hu": sb(128, U16), "kh": sb(256, F16), "xg": sb(2048, BF), "gq": sb([4, 128], F16), "fg": sb(128, F16),
-    "wn": sb(128, F16), "sv": sb(128, F16), "eu": sb(128, U16), "mg": sb(2048, F16), "ms": sb(2048, F16),
+    "wn": sb(128, F16), "sv": sb([128, 2], F16), "eu": sb(128, U16), "mg": sb(2048, F16), "ms": sb(2048, F16),
     "xs": sb(2048, F16), "Rl": sb(128, F16), "eh": sb(128, F16), "V16": sb(256, F16), "Rr": sb([15, 256], F16),
     "Ff": sb(128, F32), "sel": sb(256, F16), "ls": sb(384, F32), "lu": sb(24, U16), "junk": sb(128, F32),
-    "xa": sb(128, F32), "xh": sb(128, I32), "cs": sb(2048, BF), "ct": sb(16, BF), "cu": sb(128, U16),
-    "yxb": sb(256, F32), "ycb": sb(256, F32), "ysb": sb([8, 16], F32), "yzb": sb([8, 16], BF), "C16": sb(2048, F16),
+    "xa": sb(128, F32), "xh": sb(128, I32), "cs": sb(2048, BF),
+    "yxb": sb(256, F32), "ycb": sb(256, F32), "ysb": sb(128, F32), "yzb": sb(128, BF), "C16": sb(2048, F16),
     "mi": sb(128, I32), "mp": sb(128, F32), "li": sb(16, I32), "lc": sb(8, U16), "old": sb(128, F32),
     "adj": sb(128, F32), "vv": sb(128, F32),
 }
 for _b in range(8):
     SCRATCH["p%d" % _b] = ("psum", [128, 512] if _b < 7 else [128, 32, 16], F32)
-SEMAPHORES = ["qV", "qS", "qP", "qG", "left", "stored"] + ["ld%d" % s for s in range(7)] + \
-    ["arr%d" % s for s in range(3 * NS)]
+SEMAPHORES = ["qV", "qS", "qP", "qG", "left", "stored"] + ["ld%d" % s for s in range(8)] + \
+    ["arr%d" % s for s in range(12)]
 
-LC, CC, CP, PAR, NL, L15, L14, WW, DG, NDG, THR, CQ, FB, STC, W8, SC, AC, KK, HI8, L15B = range(20)
-BM, DMB, DMN, DMZ, ID, IN1, I3, I128, IN128, IN2K, IN16, T128, SG, ZF, BM128, LO, BE, TMP, TM2, TM3, B32, CN = range(22)
+LC, CC, CP, PAR, NL, WW, DG, NDG, THR, CQ, STC, W8, SC, AC, KK, L15B, FB, M1, MB, NR8, R82 = range(21)
+BM, DMB, DMN, DMZ, ID, IN1, I3K, IN4K, I128, IN128, IN16, T128, SG, ZF, BM128, LO, BE, TMP, TM2, TM3, B32, CN, \
+    S3K, SN4K, SH8 = range(25)
 
-PAR0 = {"cyc": 0.87, "fix": 40.0, "g": 1.56, "sc": 3.8, "pe": 0.5, "lat": 170.0, "xch": 3200.0, "snd": 900.0,
-        "bw": 400.0, "dma": 2000.0, "sfix": 30.0}
-OPT = {'seed':0,'jit':0,'vg':1.6,'stag':0,'fs':1,'ccp':1,'pri':{'ttold-1':1000,'tsfg1':-2000,'tssv0':2000,'tttny-1':-1000,'tski-1':-4000,'mmp00':-1000,'iotat5-1':-2000,'scanms0':4000,'linyzb0':1000,'ldcmb-1':-4000,'ttadj-1':4000,'mmp41':2000,'linkh-1':-1000,'linDm-1':2000,'linsnd1':-500,'linwn1':-2000,'linRl-1':-4000,'linSel-1':2000,'cpC-1':1000,'lineu0':2000,'linFf-1':-2000,'linsel-1':4000,'gatxg0':500,'ttcol-1':1000,'linmi-1':-2000,'tsfg0':-1000,'linmp-1':-4000,'diagDg-1':-4000,'ttxa-1':500},'eng':{'V16':'S','pk':'S','k':'S','z16':'V','mi':'S','eu':'V','xh':'S','Sl':'S','lu':'S','Ff':'S'},'it':1,'pw':0.1,'pre':3,'cg':15,'mg':1}
+PAR0 = {"cyc": 0.87, "fix": 40.0, "g": 1.56, "sc": 3.8, "pe": 0.5, "lat": 170.0, "xch": 250.0, "row": 30.0,
+        "snd": 600.0, "trf": 45.0, "bw": 400.0, "dma": 2000.0, "sfix": 30.0}
+PAR1 = dict(PAR0, cyc=1.1, g=1.9, pe=0.58, sc=4.5, snd=1200.0, trf=80.0, xch=800.0, lat=220.0)
+OPT = {"seed": 0, "it": 2000, "moves": 20000, "slack": 100.0, "fs": [1, 1, 1, 1], "zc": 2, "sc": 2,
+       "pre": [3, 3, 3, 3], "ccp": [5, 5, 5, 15], "far": [3, 3, 3, 3], "gp": 32, "f32": 1, "cmb": 1,
+       "eng": {}}
 
 
 def S_(a, b, c=None):
     return slice(a, b, c)
 
 
-def build(opt):
+def build(opt, rank):
     ops = []
     acc = {}
-    tag = [-1]
+    tag = [-1, -1]
+    half, own = rank // NB, rank % NB
 
     def span(a):
         if len(a) == 2 and a[0] == "p7":
-            return a[1].start, a[1].stop, a[1].stop - a[1].start
+            return 0, a[1].start, a[1].stop - a[1].start
         shp = SCRATCH[a[0]][1][1:]
-        ix = np.arange(int(np.prod(shp))).reshape(shp)[a[1:]]
-        return int(np.min(ix)), int(np.max(ix)) + 1, int(np.size(ix))
+        ix = np.arange(int(np.prod(shp))).reshape(shp)[a[1:]].ravel().tolist()
+        if ix[-1] - ix[0] + 1 == len(ix):
+            return ((1 << len(ix)) - 1) << ix[0], ix[0], len(ix)
+        return sum(1 << j for j in ix), ix[0], len(ix)
 
     def two(a):
         return SCRATCH[a[0]][2] in (F16, BF, U16)
@@ -80,24 +90,24 @@ def build(opt):
                     for e in list(last):
                         if (e == "P") != (eng == "P"):
                             deps.add(last[e])
-                        elif e != "P":
+                        else:
                             bank.add(last[e])
                     if eng == "P":
                         last.clear()
                     last[eng if eng in ("P", "V", "S") else me] = me
                     continue
-                lo, hi, _ = span(a)
+                mine = span(a)[0]
                 rec = acc.setdefault(a[0], [])
-                for (o, l2, h2, w2) in rec:
-                    if (w or w2) and l2 < hi and lo < h2:
+                for (o, its, w2) in rec:
+                    if (w or w2) and its & mine:
                         deps.add(o)
                 if w:
-                    rec[:] = [r for r in rec if not (lo <= r[1] and r[2] <= hi)]
-                rec.append((me, lo, hi, w))
+                    rec[:] = [r for r in rec if r[1] & ~mine]
+                rec.append((me, mine, w))
         deps.discard(me)
         bank.discard(me)
         ops.append({"eng": eng, "kind": kind, "args": args, "deps": deps, "bank": bank - deps, "n": n, "rate": rate,
-                    "tag": tag[0], "key": kind + (wr[0][0] if wr else "") + str(tag[0])})
+                    "level": tag[1], "key": kind + (wr[0][0] if wr else "") + str(tag[0])})
         return me
 
     def vec(kind, out, ins, args, eng="V", more=()):
@@ -134,16 +144,22 @@ def build(opt):
     def gather(name, out, win, off):
         return add(opt["eng"].get(name, "VS"), "gat", (out, ("ind", win, off)), [win, off], [out], span(out)[2], "g")
 
-    def mm(lst, after=None):
-        n = sum(max(64, span(m[2])[2]) for m in lst)
-        return add("P", "mm", lst, [x for m in lst for x in (m[1], m[2])], [m[0] for m in lst], n, "pe",
-                   [] if after is None else [after])
+    def mm(lst):
+        n = sum(max(64, span(m[2])[2]) * (1 if two(m[2]) else 4) for m in lst)
+        return add("P", "mm", lst, [x for m in lst for x in (m[1], m[2])], [m[0] for m in lst], n, "pe")
 
     def grp(out, pairs):
         return [(out, l, r, j == 0, j == len(pairs) - 1) for j, (l, r) in enumerate(pairs)]
 
     def iota(out, pat, base, cm):
         return add("G", "iota", (out, pat, base, cm), [], [out], span(out)[2], "gp")
+
+    def put(out, src, pat, base, fill):
+        return add("G", "sel", (out, src, pat, AL.not_equal, fill, base, 1), [src], [out], span(out)[2], "gp")
+
+    def after(op, *deps):
+        ops[op]["deps"].update(d for d in deps if d is not None)
+        return op
 
     def c_(j):
         return ("col", S_(j, j + 1))
@@ -162,10 +178,10 @@ def build(opt):
     full = S_(0, 128)
     quarters = [S_(512 * j, 512 * j + 512) for j in range(4)]
     load(0, ("cmb", quarters[0]), ("cm", quarters[0]), 262144)
-    load(1, ("s0b", S_(0, 8), S_(0, 16)), ("s0", full), 65536)
+    load(1, ("s0b", full), ("s0", full), 65536)
     for j in range(1, 4):
         load(1 + j, ("cmb", quarters[j]), ("cm", quarters[j]), 262144)
-    load(5, ("z0b", S_(0, 8), S_(0, 16)), ("z0", full), 32768)
+    load(5, ("z0b", full), ("z0", full), 32768)
     load(6, ("X", S_(0, 8192)), ("x0", S_(0, 8192)), 2097152)
 
     DJ = ("DJ", S_(0, 160)); D0 = ("DJ", full)
@@ -176,31 +192,42 @@ def build(opt):
     iota(("BI", full), [[16, 8], [0, 16]], 0, -1)
     iota(("t5", S_(0, 5)), [[-1, 5]], 4, 0)
     iota(("CcM", full), [[0, 8], [1, 4], [0, 4]], 0, 0)
-    iota(("FC", full), [[0, 8], [1, 16]], -15, 0)
+    turn = LH * (1 - 2 * half)
     iota(("Sf", full), [[16, 128]], 0, 0)
-    iota(("Sf", S_(128, 256)), [[Q, NS], [16, 8], [1, Q]], 0, 0)
-    iota(("Sf", S_(256, 384)), [[16 * Q, NS], [256, 8], [16, Q]], 0, 0)
+    iota(("Sf", S_(128, 256)), [[turn, NS], [1, LH]], LH * half, 0)
+    iota(("Sf", S_(256, 384)), [[16 * turn, NS], [16, LH]], 16 * LH * half, 0)
+    ms(("Z", S_(0, 2064)), 0.0)
+    put(("Z", S_(16, 2064, 16)), ("Z", S_(16, 2064, 16)), [[-1, 16], [-16, 8]], 0, 1.0)
+    ms(("cs", S_(0, 512)), 0.0)
+    for k in (0, 4):
+        a = ("Cm", S_(k, k + 4), full)
+        put(a, ("cs", S_(0, 512)), [[-1, 4], [-16, 8], [0, 16]], -k, STEP)
+        put(a, a, [[-1, 4], [-16, 8], [0, 16]], -k - 1, -STEP)
     for m in range(32):
-        add("G", "diag", (("Dg", m, full), ("DJ", S_(m + 1, m + 129))), [DJ], [("Dg", m, full)], 128, "gp")
+        add("G", "sel", (("Dg", m, full), ("DJ", S_(m + 1, m + 129)), [[-1, 128]], AL.is_equal, 0.0, 0, 1),
+            [DJ], [("Dg", m, full)], 128, "gp")
     ki = ("ki", S_(0, 1))
+    unit, fb = (2048.0, 2048.0) if opt["f32"] else (128.0, 16512.0)
     ts(("ki", S_(4, 5)), ki, 15, AL.bitwise_and)
     ts(("ki", S_(5, 6)), ki, 2, AL.logical_shift_right, 3, AL.bitwise_and)
     ts(("ki", S_(6, 7)), ki, 3, AL.bitwise_and)
     ts(("ki", S_(7, 8)), ki, 1, AL.bitwise_and)
     cp(("col", S_(0, 4)), ("ki", S_(4, 8)))
     ts(("R", S_(0, 17)), ("ia", S_(0, 17)), c_(LC), AL.is_equal)
-    ts(("J", S_(0, 160)), DJ, 16.0, AL.is_equal)
-    for a in range(16):
-        lin("k", ("Y", a, S_(0, 160)), ("J", S_(0, 160)), ("R", S_(a, a + 1)))
     for j, src, mul, addc in ((L15B, LC, -1.0, 15.0), (NL, LC, -1.0, 0.0), (WW, PAR, -2.0, 1.0),
-                              (CQ, CC, 0.25, 0.0), (KK, LC, 1.0, 1536.0)):
+                              (CQ, CC, 1024.0, 0.0), (KK, LC, 1.0, 1536.0), (FB, LC, fb, -15 * fb)):
         lin("k", c_(j), c_(src), mul, addc)
     ts(k_(BM), ("BI", full), c_(NL), AL.is_equal)
     lin("k", k_(TMP), k_(BM), -1024.0, 1024.0)
     tt(k_(DMB), D0, k_(TMP), AL.add)
-    ts(k_(ID), k_(DMB), 0.0, AL.is_equal)
-    for j, v in ((IN1, -1.0), (I3, 3.0), (I128, 128.0), (IN128, -128.0), (IN2K, 4096.0), (IN16, -16.0)):
-        lin("k", k_(j), k_(ID), v)
+    ts(k_(ID), D0, 0.0, AL.is_equal)
+    for j, v in ((IN1, -1.0), (I3K, 12288.0), (IN4K, -4096.0), (I128, unit), (IN16, -16.0)) + \
+            ((IN128, -128.0),) * (1 - opt["f32"]):
+        ts(k_(j), D0, 0.0, AL.is_equal, v, AL.mult)
+    for j, v in ((S3K, 12288.0), (SN4K, -4096.0)) * (max(opt["far"]) > 0) + ((SH8, 1.0),) * (min(opt["far"]) < 3):
+        ts(k_(j), k_(DMB), -8.0, AL.is_equal, v, AL.mult)
+    lin("k", c_(NR8), ("R", S_(8, 9)), -1.0)
+    lin("k", c_(R82), ("R", S_(8, 9)), 2.0)
     for rep in range(2):
         lin("k", ("Cy", S_(0, 8), S_(16 * rep, 16 * rep + 16)), k_(ID))
     for j in range(2):
@@ -240,247 +267,330 @@ def build(opt):
     lin("k", k_(TM3), k_(TM2), 1.0, c_(DG))
     tt(k_(LO), k_(TM3), k_(BM), AL.mult)
     tt(("Rd", S_(0, 16)), ("R", S_(0, 16)), ("R", S_(1, 17)), AL.subtract)
-    ts(k_(TM2), k_(DMB), -1.0, AL.is_equal, -2048.0, AL.mult)
-    lin("k", k_(TM3), k_(ID), 2048.0)
-    tt(("Cm", 8, full), k_(TM2), k_(TM3), AL.add)
-    if opt["cg"] != 15:
-        tt(("Rd2", S_(0, 8)), ("R", S_(0, 8)), ("R", S_(8, 16)), AL.add)
-        for j in range(8):
-            lin("k", ("Cm", j, full), k_(BM), ("Rd2", S_(j, j + 1)))
-        ts(c_(L14), c_(LC), 8.0, AL.is_lt)
-        ts(c_(HI8), c_(LC), 8.0, AL.is_ge)
-        lin("k", c_(FB), ("R", S_(15, 16)), -4096.0)
-    if opt["cg"]:
-        lin("k", ("ct", S_(0, 16)), ("ia", S_(0, 16)), 2048.0, -4096.0)
-        lin("k", c_(L15), ("R", S_(15, 16)), -2.0, 2.0)
     ms(("one", full), 1.0)
-    if opt["pre"] != 3:
-        ms(("rst", S_(0, 512)), 1.0)
-        ms(("rst", S_(0, 512, 16)), 0.0)
+    ms(("rst", S_(0, 512)), 1.0)
+    ms(("rst", S_(0, 512, 16)), 0.0)
     lin("k", ("cd", S_(0, 16)), ("Rd", S_(0, 16)), 16384.0)
     lin("k", ("cd", S_(15, 16)), ("Rd", S_(15, 16)), 16384.0, -32768.0)
-    for a, b in ((16, 16), (32, 32), (64, 64), (128, 128), (256, 128)):
-        lin("k", ("cd", S_(a, a + b)), ("cd", S_(0, b)))
-    tt(k_(DMN), D0, k_(TMP), AL.subtract)
-    ts(k_(T128), k_(DMN), 0.0, AL.is_gt, 128.0, AL.mult)
-    tt(k_(DMZ), D0, k_(BM), AL.mult)
-    ts(k_(TM2), k_(DMZ), -1.0, AL.max, 1.0, AL.min)
-    lin("k", k_(TM3), k_(ID), -32.0)
-    tt(k_(SG), k_(TM3), k_(TM2), AL.subtract)
-    tt(k_(TM2), k_(I128), k_(T128), AL.subtract)
-    lin("k", k_(ZF), k_(TM2), 0.5)
-    ms(("o129", full), 129.0)
-    for v in range(2):
+    for a in (16, 32, 64, 128):
+        lin("k", ("cd", S_(a, 2 * a)), ("cd", S_(0, a)))
+    def beside(out, src, sign):
+        return add("G", "sel", (out, src, [[-sign, 128]], AL.is_gt, 0.0, 0, sign), [src], [out], 128, "gp")
+    beside(k_(DMN), k_(BM), 1)
+    put(k_(DMN), k_(DMN), [[-1, 128]], 0, -32.0)
+    beside(k_(DMZ), k_(BM), -1)
+    lin("k", k_(T128), k_(DMZ), unit)
+    tt(k_(SG), k_(DMN), k_(DMZ), AL.subtract)
+    lin("k", k_(ZF), k_(DMZ), -64.0)
+    put(k_(ZF), k_(ZF), [[-1, 128]], 0, 64.0)
+    heads = ("K", BM, S_(0, 128, 16))
+    iota(("FC", full), [[0, 8], [1, 16]], -15, 0)
+    ms(("o129", full), 16.0 if opt["f32"] else 129.0)
+    for v in range(2 - opt["f32"]):
         for j in range(2):
-            lin("k", ("Sel", v, S_(0, 8), j), ("K", BM, S_(0, 128, 16)), (2.0 * j - 1.0) * 128.0 ** v)
+            lin("k", ("Sel32", S_(0, 8), j) if opt["f32"] else ("Sel", v, S_(0, 8), j), heads, (2.0 * j - 1.0) * 128.0 ** v)
+    iota(("J", S_(0, 256)), [[1, 256]], 0, 0)
+    iota(("ki", S_(1, 2)), [[0, 1]], LH * half, 1)
+    ts(("ki", S_(2, 3)), ("ki", S_(1, 2)), 4, AL.logical_shift_right, 7, AL.bitwise_and)
+    lin("k", c_(M1), ("ki", S_(2, 3)), 1.0, 1.0)
+    lin("k", c_(MB), ("ki", S_(2, 3)), -256.0)
+    ms(("Fz", S_(0, 72), S_(0, 16)), 0.0)
+    if 2 in opt["fs"] and opt["f32"]:
+        ms(("Fw32", S_(0, 272)), 0.0)
+        for a, sg in ((16, 1.0), (15, -1.0), (144, 1.0)):
+            lin("k", ("Fw32", S_(a, a + 128, 16)), heads, sg)
+    elif 2 in opt["fs"]:
+        ms(("Fw", S_(0, 2), S_(0, 272)), 0.0)
+        for v in range(2):
+            for a, sg in ((16, 1.0), (15, -1.0), (144, 1.0)):
+                lin("k", ("Fw", v, S_(a, a + 128, 16)), heads, sg * 128.0 ** v)
     lin("k", ("kh", full), k_(BM), 0.0, c_(KK))
     ts(c_(STC), ("R", S_(1, 2)), 24576.0, AL.mult, ("R", S_(2, 3)), AL.subtract)
     lin("k", ("St", S_(0, 256)), ("Sf", S_(0, 256)), R0)
     lin("k", ("St", S_(256, 384)), ("Sf", S_(256, 384)), R0, c_(STC))
-    lin("k", c_(SC), R0, 1.0, 2048.0)
+    lin("k", c_(SC), R0, 1.0, STEP)
     lin("k", k_(B32), k_(BM), 1.0 / 32)
-    ts(y_(54, 55), c_(LC), 8.0, AL.is_lt, -16384.0, AL.mult)
-    ts(y_(55, 56), ("R", S_(8, 9)), -0.484375, AL.mult, y_(54, 55), AL.add)
-    lin("k", k_(CN), k_(BM), y_(55, 56))
+    lin("k", k_(CN), k_(BM), -43008.0)
+    ms(("c16", S_(0, LH)), 16.0)
+    ts(("I32", full), D0, 0.0, AL.is_equal)
     ms(("M", S_(0, 8)), 0)
+    ms(("M", S_(2056, 2064)), 0)
     for w in quarters:
         ts(("C", w), ("cmb", w), 2047, AL.bitwise_and)
     for w in quarters:
         lin("M", ("M", S_(w.start + 8, w.stop + 8)), ("cmb", w), 1.0 / 2048, -1023.5 / 2048)
 
-    Cw = ("C", S_(0, 2048)); Xw = ("X", S_(0, 8192)); Mw = ("M", S_(0, 2056))
-    blk = S_(0, 8)
+    Cw = ("C", S_(0, 2048)); Xw = ("X", S_(0, 8192)); Mw = ("M", S_(0, 2064))
     arrive = {}
+    calls = [0]
+
+    def landing(what, t, h):
+        return ("m%s%d" % (what, h), 7 * t - 4 if h == 0 else 2 * t - 1, S_(0, LH))
+
+    def leaving(what, t, h):
+        if opt["cmb"]:
+            part = S_(0, 16) if what == "S" else S_(16, 32)
+            return ("mc0", S_(7 * t + 3 - own, 7 * t + 7 - own), own, part) if h == 0 else ("mc1", 2 * t, S_(0, NB), part)
+        if h == 0:
+            return ("m%s0" % what, S_(7 * t + 3 - own, 7 * t + 7 - own), S_(16 * own, 16 * own + 16))
+        return ("m%s1" % what, 2 * t, S_(0, LH))
+
+    def send(what, t, hs, pks):
+        trs = []
+        for h in hs:
+            for j in range(NB):
+                if (h or j != own) and what == "c":
+                    src = ("mc0", 7 * t + 3 - own + j, own, S_(0, 32)) if h == 0 else ("mc1", 2 * t, j, S_(0, 32))
+                    trs.append((NB * (half ^ h) + j, src, landing(what, t + 1, h)[:2] + (own, S_(0, 32))))
+                elif h or j != own:
+                    b = NB * (half ^ h) + j
+                    src = ("m%s0" % what, 7 * t + 3 - own + j, S_(16 * own, 16 * own + 16)) if h == 0 else \
+                        ("m%s1" % what, 2 * t, S_(16 * j, 16 * j + 16))
+                    trs.append((b, src, landing(what, t + 1, h)[:2] + (S_(16 * own, 16 * own + 16),)))
+        per = 4 if len(trs) <= 4 else 2
+        a = (calls[0], trs, per)
+        calls[0] += 1
+        me = add("G", "send", a, [], [], len(trs), "snd", pks)
+        ops[me]["key"] += what
+        me = add("R", "arr", a, [], [], 128 // per, "xch", [me])
+        for h in hs:
+            arrive[what, t + 1, h] = me
+
     for t in range(RO):
         last = t == RO - 1
         par = t & 1
-        pks = []
+        tag[1] = t
+        pks = {"S": [], "z": []}
         if last:
-            prev = None
-            for j in range(16):
-                prev = mm([(("p6", S_(0, 256)), ("Dg", m, full), ("X", S_(256 * m, 256 * m + 256)), m == 0, m == 31)
-                           for m in range(2 * j, 2 * j + 2)], prev)
-            lin("yb", ("yxb", S_(0, 256)), ("p6", S_(0, 256)))
+            for m in range(32):
+                mm([(("p7", S_(0, 256)), ("Dg", m, full), ("X", S_(256 * m, 256 * m + 256)), m == 0, m == 31)])
+            lin("yb", ("yxb", S_(0, 256)), ("p7", S_(0, 256)))
+            for j, w in enumerate(quarters):
+                put(("C16", w), ("C", w), [[0, 512]], 1, 0.0)
+                mm([(("p7", S_(0, 256)), ("Dg", m, full), ("C16", S_(256 * m, 256 * m + 256)), m == 0, m == 7)
+                    for m in (2 * j, 2 * j + 1)])
+            lin("yb", ("yc0", S_(0, 256)), ("p7", S_(0, 256)))
+        zz = []
         for h in range(NS):
             tag[0] = h
             w = S_(LH * h, LH * h + LH)
+            real = S_(LH * (h ^ half), LH * (h ^ half) + LH)
             o = 16 * LH * h
             pa, pb, pc = "p%d" % (3 * h), "p%d" % (3 * h + 1), "p%d" % (3 * h + 2)
-            a0 = S_(0, LH)
-            mine = S_(Q * h, Q * h + Q)
-            q0 = 2 * Q * h
-            zz = ("lnd", t, blk, S_(q0 + Q, q0 + 2 * Q))
-            if t == 0:
-                lin("Sl", ("Sl", w), ("s0b", blk, mine))
-                lin("z16", zz, ("z0b", blk, mine), 1.0, R0)
-            else:
-                ops[lin("Sl", ("Sl", w), ("lnd", t, blk, S_(q0, q0 + Q)))]["deps"].add(arrive[t, h])
+            a0, a1 = S_(0, LH), S_(128, 128 + LH)
             chunks = [(LH * h + 32 * j, o + 512 * j) for j in range(LH // 32)]
-            for (l0, c0) in chunks:
-                gather("gC", ("G", S_(c0, c0 + 512)), Cw, ("Sl", S_(l0, l0 + 32)))
-            mm(grp((pc, a0), [(k_(B32), zz)]), arrive.get((t, h)))
+            if t == 0:
+                lin("Sl", ("Sl", w), ("s0b", real))
+                lin("z16", ("zf", w), ("z0b", real), 1.0, R0)
+                zz.append(("zf", w))
+                seats = [("Sl", S_(l0, l0 + 32)) for (l0, c0) in chunks]
+            elif opt["cmb"]:
+                row = landing("c", t, h)[:2]
+                after(lin("z16", ("zf", w), row + (S_(0, NB), S_(16, 32))), arrive["c", t, h])
+                zz.append(("zf", w))
+                seats = [row + (j, S_(0, 16)) for j in range(NB)]
+                arrive["S", t, h] = arrive["c", t, h]
+            else:
+                zz.append(landing("z", t, h))
+                seats = [landing("S", t, h)[:2] + (S_(l0 - LH * h, l0 - LH * h + 32),) for (l0, c0) in chunks]
+            n = 1024 // len(seats)
+            for j, s in enumerate(seats):
+                after(gather("gC", ("G", S_(o + n * j, o + n * j + n)), Cw, s), arrive.get(("S", t, h)))
+            after(mm(grp((pc, a0), [(k_(B32), zz[h])])), arrive.get(("z", t, h)))
             lin("fl", ("fl", par, w), (pc, a0), 2.0, 1536.0 - 0.0625 - 0.46875)
-            a1 = S_(128, 128 + LH)
 
-            def fold(src, rhs, wide, z0):
-                mm(grp((pa, a1), [(rhs(k), (src, S_(o + k, o + 16 * LH, 16))) for k in range(16)]))
-            fold("G", lambda k: ("Y", (k + t) & 15, S_(16 + ((k + t) & 15) - k, 144 + ((k + t) & 15) - k)), 2, 16 * h)
+            def fold(src, lhs):
+                mm(grp((pa, a1), [(lhs(k), (src, S_(o + k, o + 16 * LH, 16))) for k in range(16)]))
+            fold("G", lambda k: ("Z", S_(128 * ((k + t) & 15) + 16 - k, 128 * ((k + t) & 15) + 144 - k)))
             lin("E16", ("E16", w), (pa, a1))
-            if opt["pre"] >> h & 1:
+            pre = opt["pre"][t] >> h & 1
+            if pre:
                 lin("eu", ("eu", w), ("E16", w), 1.0, 8.0)
-                for (l0, c0) in chunks:
-                    gather("gM", ("mg", S_(c0, c0 + 512)), Mw, ("eu", S_(l0, l0 + 32)))
+                for l0 in range(w.start, w.stop, opt["gp"]):
+                    gather("gM", ("mg", S_(16 * l0, 16 * (l0 + opt["gp"]))), Mw, ("eu", S_(l0, l0 + opt["gp"])))
             mm([((pb, S_(LH * d, LH * d + LH)), ("Dm", d, full), ("E16", w), True, True) for d in range(8)])
             tt(("Pp", w), ("E16", w), (pc, a0), AL.mult)
             e0 = 8 * LH * h
             ts(("eq", S_(e0, e0 + 8 * LH)), (pb, S_(0, 8 * LH)), 0.0, AL.is_equal)
-            oa = grp((pa, a0), [(k_(ID), ("E16", w)), (k_(CN), ("one", a0))] + ([(k_(ID), ("Ab", a0))] if t else []) +
+            ts(("Qm", w), ("Pp", w), -0.484375, AL.add, 12582912.0, AL.add)
+            oa = grp((pa, a0), [(("I32", full), ("Qm", w)), (k_(CN), ("c16", a0)), (k_(ID), ("E16", w))] +
+                     ([(k_(ID), ("Ab", a0))] if t else []) +
                      [(("Om", d, full), ("eq", S_(e0 + LH * d, e0 + LH * d + LH))) for d in range(8)])
-            mm(oa[-8:], mm(oa[:-8]))
-            tt(("hi", w), ("Pp", w), (pa, a0), AL.add)
-            ts(("hj", w), ("hi", w), 8191, AL.bitwise_and)
-            lin("hu", ("hu", w), ("hj", w))
+            mm(oa[:-8])
+            mm(oa[-8:])
+            lin("hr", ("hr", w), (pa, a0), 1.0, -4095.5)
+            tt(("hu", w), (pa, a0), ("hr", w), AL.subtract)
             for (l0, c0) in chunks:
                 gather("gX", ("xg", S_(c0, c0 + 512)), Xw, ("hu", S_(l0, l0 + 32)))
-            lin("hh", ("kh", S_(128 + LH * h, 128 + LH * h + LH)), ("hj", w), 0.0078125, 1536.0 - 0.49609375)
-            fold("xg", lambda k: ("Wz", S_(15 - k, 143 - k)), 1, 16 * h)
+            lin("hh", ("kh", S_(128 + LH * h, 128 + LH * h + LH)), ("hu", w), 0.0078125, 1536.0 - 0.49609375)
+            fold("xg", lambda k: ("Wz", S_(15 - k, 143 - k)))
             for j in range(4):
                 lin("gq", ("gq", j, w), (pa, a1), 0.25, 1536.0 - 0.375 + 0.25 * j)
-            mm(grp((pc, a0), [(("Fl", j, full), ("gq", j, w)) for j in range(4)]))
-            dl = grp((pb, a0), [(k_(I3), ("gq", 0, w))] + [(k_(IN1), ("gq", j, w)) for j in (1, 2, 3)] +
-                     [(k_(BE), ("wn", w))])
-            first = mm(dl[:4])
+            tests = grp((pc, a0), [(("Fl", j, full), ("gq", j, w)) for j in range(4)])
+            mm(tests[:3])
+            mm(tests[3:])
+            dl = grp((pb, a0), [(k_(I3K), ("gq", 0, w))] + [(k_(IN4K), ("gq", j, w)) for j in (1, 2, 3)] +
+                     [(k_(ID), ("E16", w)), (k_(BE), ("wn", w))])
+            mm(dl[:5])
             ts(("fg", w), (pc, a0), c_(THR), AL.is_gt)
             mm(grp((pa, a0), [(k_(LO), ("fg", w))]))
+            far = grp((pc, a0), [(k_(S3K), ("gq", 0, w))] + [(k_(SN4K), ("gq", j, w)) for j in (1, 2, 3)] +
+                      [(k_(BE), ("wn", w))]) * (opt["far"][t] >> h & 1)
+            if far:
+                mm(far[:4])
             lin("wn", ("wn", w), (pa, a0), 1.0, 1.0, True)
-            mm(dl[4:], first)
-            ts(("sv", w), (pb, a0), 0.0, AL.is_equal)
-            pre = opt["pre"] >> h & 1
+            mm(dl[5:] + far[4:])
             if not pre:
-                mm(grp((pa, a0), [(k_(ID), ("E16", w)), (k_(IN2K), ("sv", w))]))
-                lin("eu", ("eu", w), (pa, a0), 1.0, 8.0 - 4096.0, True)
-            mm(grp((pa, a0), [(("Cm", 8, full), ("sv", w))]))
-            cg = opt["cg"] >> (2 * h) & 3
-            if cg != 3:
-                lin("sx", ("sx", w, 0), (pa, a0), c_(L14))
-                lin("sx", ("sx", w, 1), (pa, a0), c_(HI8), c_(FB))
-            if cg:
-                lin("sx", ("cu", w), (pa, a0), 1.0 / 2048, c_(L15))
-            for j, (l0, c0) in enumerate(chunks):
-                pk = (pc, pb)[j & 1]
-                cw = S_(c0, c0 + 512)
-                steps = (pk, S_(0, 512))
-                if cg >> j & 1:
-                    gather("gS", ("cs", cw), ("ct", S_(0, 16)), ("cu", S_(l0, l0 + 32)))
-                    steps = ("cs", cw)
-                else:
-                    mm([((pk, S_(k, 512, 8)), ("Cm", k, full), ("sx", S_(l0, l0 + 32), S_(0, 2)), True, True)
-                        for k in range(8)])
-                if opt["ccp"] >> (2 * h + j) & 1 and not cg >> j & 1:
-                    vec("lin", ("cs", cw), [steps], (("cs", cw), steps, 1.0, 0.0, False), "S")
-                    steps = ("cs", cw)
-                scan(("xs", cw), ("xg", cw), steps, -8192.0, AL.max, AL.add)
-                if pre:
-                    scan(("ms", cw), ("mg", cw), steps, -8192.0, AL.max, AL.add)
+                ts(("eu", w), (pb, a0), 8.0, AL.add, 2056.0, AL.min)
+            tt(("sv", w, 0), ("E16", w), (pb, a0), AL.is_equal)
+            if opt["far"][t] >> h & 1:
+                ts(("sv", w, 1), (pc, a0), c_(NR8), AL.is_equal, c_(R82), AL.add)
+            else:
+                mm(grp((pc, a0), [(k_(SH8), ("sv", w, 0))]))
+                lin("sx", ("sv", w, 1), (pc, a0), 1.0, c_(R82))
             ends = S_(o + 15, o + 16 * LH, 16)
-            if not pre:
-                for (l0, c0) in chunks:
-                    cw = S_(c0, c0 + 512)
+            steps = []
+            for j, (l0, c0) in enumerate(chunks):
+                pk = (pa, pc)[j & 1]
+                cw = S_(c0, c0 + 512)
+                mm([((pk, S_(k, 512, 8)), ("Cm", k, full), ("sv", S_(l0, l0 + 32), S_(0, 2)), True, True) for k in range(8)])
+                steps.append((pk, S_(0, 512)))
+                if opt["ccp"][t] >> (2 * h + j) & 1:
+                    vec("lin", ("cs", cw), [steps[j]], (("cs", cw), steps[j], 1.0, 0.0, False), "S")
+                    steps[j] = ("cs", cw)
+                if pre:
+                    scan(("ms", cw), ("mg", cw), steps[j], -4 * STEP, AL.max, AL.add)
+                else:
                     gather("gM", ("mg", cw), Mw, ("eu", S_(l0, l0 + 32)))
                     scan(("ms", cw), ("rst", S_(0, 512)), ("mg", cw), 0.0, AL.mult, AL.max)
             if last:
-                lin("pk", ("ysb", blk, mine), ("ms", ends), 1.0, 2048.0 * pre)
-                lin("pk", ("yzb", blk, mine), ("xs", ends), 1.0, 2048.0)
+                lin("pk", ("ysb", real), ("ms", ends), 1.0, STEP * pre)
             else:
-                pks.append(lin("pk", ("snd", t, blk, S_(q0, q0 + Q)), ("ms", ends), 1.0, 2048.0 * pre))
-                pks.append(lin("pk", ("snd", t, blk, S_(q0 + Q, q0 + 2 * Q)), ("xs", ends), 1.0, c_(SC)))
-                if not opt["mg"]:
-                    a = (2 * t + h, t, S_(q0, q0 + 2 * Q))
-                    own = add("Y", "own", a, [], [], 4096, "dma", pks[-2:])
-                    me = add("G", "send", a, [], [], 0, "snd", pks[-2:])
-                    arrive[t + 1, h] = add("R", "arr", a, [], [], 0, "xch", [me, own])
-                elif h == NS - 1:
-                    a = (t, t, S_(0, 32))
-                    own = add("Y", "own", a, [], [], 8192, "dma", pks)
-                    me = add("G", "send", a, [], [], 0, "snd", pks)
-                    arrive[t + 1, 0] = arrive[t + 1, 1] = add("R", "arr", a, [], [], 0, "xch", [me, own])
-        W = 128 // opt["fs"]
-        for r in range(opt["fs"]):
-            tag[0] = r if opt["fs"] > 1 else -1
+                pks["S"].append(lin("pk", leaving("S", t, h), ("ms", ends), 1.0, STEP * pre))
+                if (opt["sc"] == 2 or h) and not opt["cmb"]:
+                    send("S", t, [h] if opt["sc"] == 2 else [0, 1], pks["S"][-3 + opt["sc"]:])
+            for j, (l0, c0) in enumerate(chunks):
+                scan(("xs", S_(c0, c0 + 512)), ("xg", S_(c0, c0 + 512)), steps[j], -4 * STEP, AL.max, AL.add)
+            if last:
+                lin("pk", ("yzb", real), ("xs", ends), 1.0, STEP)
+            else:
+                pks["z"].append(lin("pk", leaving("z", t, h), ("xs", ends), 1.0, c_(SC)))
+                if opt["cmb"]:
+                    send("c", t, [h], [pks["S"][-1], pks["z"][-1]])
+                elif opt["zc"] == 2 or h:
+                    send("z", t, [h] if opt["zc"] == 2 else [0, 1], pks["z"][-3 + opt["zc"]:])
+        tag[0] = -1
+        mm([x for h in range(NS) for x in grp(("p6", S_(LH * h, LH * h + LH)), [
+            (k_(BM), ("St", S_(256 + LH * h, 256 + LH * h + LH))), (k_(BM), zz[h]),
+            (k_(IN16), ("fl", par, S_(LH * h, LH * h + LH)))])])
+        scan(("ls", S_(256, 384)), ("p6", full), ("cd", full), -65536.0, AL.max, AL.add)
+        lin("lu", ("lu", S_(16, 24)), ("ls", S_(256 + 15, 384, 16)), 1.0, 16384.0)
+        if last:
+            gather("o16", ("o16", full), Cw, ("lu", S_(16, 24)))
+            lin("cv", ("Ft", full), ("p6", full))
+            mm(grp(("p6", S_(128, 136)), [(("Ft", full), ("K", ID, S_(0, 128, 16)))]))
+            lin("cv", ("cT", S_(0, 8)), ("p6", S_(128, 136)), 1.0, c_(MB))
+            for q in range(8):
+                ts(("OH", q, S_(0, 256)), ("J", S_(0, 256)), ("cT", S_(q, q + 1)), AL.is_equal, c_(M1), AL.mult)
+        fs = 1 if last else opt["fs"][t]
+        W = 128 // fs
+        for r in range(fs):
+            tag[0] = r if fs > 1 else -1
             w = S_(W * r, W * r + W)
-            n = W // 16
+            pf, pv = ("p%d" % (3 * r + 1),) * 2 if fs > 1 else ("p4", "p1")
 
             def seg(j, base=0):
                 return S_(base + W * j, base + W * j + W)
-
-            def lst(j):
-                return ("lu", S_(3 * n * r + n * j, 3 * n * r + n * j + n))
-            svw = ("sv", w)
+            svw = ("sv", w, 0)
             v0 = 2 * W * r
             vw = S_(v0, v0 + 2 * W)
-            mm(grp(("p7", seg(0)), [(k_(SG), svw)]))
-            lin("Rl", ("Rl", w), ("p7", seg(0)), 1.0, c_(LC), True)
-            lin("eh", ("eh", w), ("E16", w), 0.0078125, 1536.0 - 0.49609375)
-            pl = [(k_(T128), svw), (k_(I128), ("Rl", w))]
-            mm(grp(("p6", seg(0)), [(k_(ID), ("E16", w)), (k_(IN128), ("eh", w))] + pl) +
-               grp(("p6", seg(1)), [(k_(ID), ("eh", w))] + pl))
-            lin("V16", ("V16", seg(0)), ("p6", seg(0)), 1.0, 196608.0)
-            lin("V16", ("V16", seg(1)), ("p6", seg(1)), 1.0, -1536.0)
-            mm(grp(("p6", seg(0)), [(k_(ID), ("kh", w)), (k_(ZF), svw)]) +
-               grp(("p6", seg(1)), [(k_(ID), ("kh", seg(r, 128))), (k_(ZF), svw)]))
-            lin("sel", ("sel", vw), ("p6", S_(0, 2 * W)), 1.0, -1600.0, True)
-            mm(grp(("p6", seg(0)), [(k_(BM), ("St", w)), (k_(BM), ("sel", seg(0, v0)))]) +
-               grp(("p6", seg(1)), [(k_(BM), ("St", seg(r, 128))), (k_(BM128), ("sel", seg(1, v0)))]) +
-               [x for hh in range(NS) if W * r <= LH * hh < W * (r + 1) for x in grp(
-                   ("p6", S_(2 * W + LH * hh - W * r, 2 * W + LH * hh - W * r + LH)),
-                   [(k_(BM), ("St", S_(256 + LH * hh, 256 + LH * hh + LH))), (k_(BM), ("lnd", t, blk, S_(2 * Q * hh + Q, 2 * Q * hh + 2 * Q))),
-                    (k_(IN16), ("fl", par, S_(LH * hh, LH * hh + LH)))])])
-            l0 = 3 * W * r
-            scan(("ls", S_(l0, l0 + 3 * W)), ("p6", S_(0, 3 * W)), ("cd", S_(0, 3 * W)), -65536.0, AL.max, AL.add)
-            if last:
-                lin("mi", ("mi", w), ("p6", seg(1)), 1.0 / 256, 1.0 - 127.5 / 256)
-            lin("lu", ("lu", S_(3 * n * r, 3 * n * r + 3 * n)), ("ls", S_(l0 + 15, l0 + 3 * W, 16)), 1.0, 16384.0)
-            prev = mm([(("p7", full), ("o129", full), ("FC", full), True, False)])
-            fm = [(("p7", blk, S_(max(p - 1, 0), p + 1)), ("Rr", p - 1, seg(v)) if p else ("V16", seg(v)),
-                   ("Sel", v, blk, S_(0 if p else 1, 2)), False, p == 15 and v == 1) for p in range(16) for v in range(2)]
-            for p in range(16):
-                if p:
-                    lin("Rr", ("Rr", p - 1, vw), ("V16", vw), 1.0, -128.0 * p, True)
-                if p % 2:
-                    prev = mm(fm[2 * p - 2:2 * p + 2], prev)
-            lin("Ft", ("Ft", full), ("p7", full))
-            mm(grp(("p7", S_(128, 256)), [(("Ft", full), k_(ID))]))
-            lin("Ff", ("Ff", w), ("p7", S_(128, 256)))
-            cp(("ind", Cw, lst(2)), ("Ff", w))
-            tt(("xa", w), ("ind", ("xg", S_(0, 2048)), lst(0)), ("xs", S_(16 * W * r + 15, 16 * W * (r + 1), 16)), AL.add)
-            lin("xh", ("xh", w), ("xa", w), 0.5, 1023.75)
-            if not last:
-                cp(("ind", Xw, lst(1)), ("xh", w))
+            mm(grp((pf, seg(0)), [(k_(SG), svw)]))
+            lin("Rl", ("Rl", w), (pf, seg(0)), 1.0, c_(LC), True)
+            ft = fs == 1
+            if opt["f32"]:
+                pl = grp((pv, seg(0)), [(k_(ID), ("E16", w)), (k_(T128), svw), (k_(I128), ("Rl", w))])
+                mm(pl[:2])
+                mm(pl[2:])
+                lin("V16", ("R32", 0, w), (pv, seg(0)))
+                if ft:
+                    mm([(("p7", full), ("o129", full), ("FC", full), True, False)] +
+                       [(("p7", full), ("o16", full), k_(IN1), False, False)] * last)
+                    fm = [(("p7", S_(0, 8), S_(max(p - 1, 0), p + 1)), ("R32", p, w),
+                           ("Sel32", S_(0, 8), S_(0 if p else 1, 2)), False, p == 15) for p in range(16)]
+                else:
+                    fm = grp((pf, seg(0)), [(("Fw32", S_(16 - p, 144 - p) if p else S_(144, 272)), ("R32", p, w))
+                                            for p in range(16)])
+                for p in range(16):
+                    if p:
+                        lin("Rr", ("R32", p, w), ("R32", 0, w), 1.0, -2048.0 * p, True)
+                    mm(fm[p:p + 1])
             else:
-                lc = ("lc", S_(n * r, n * r + n))
-                yw = ("yxb", S_(0, 256))
-                lin("mi", ("mp", w), ("mi", w))
-                lin("mi", ("li", S_(n * r, n * r + n)), ("ls", S_(l0 + W + 15, l0 + 2 * W, 16)), 1.0, 16384.0)
-                ts(("li", S_(8 + n * r, 8 + n * r + n)), ("li", S_(n * r, n * r + n)), 255, AL.bitwise_and)
-                lin("mi", lc, ("li", S_(8 + n * r, 8 + n * r + n)))
-                tt(("old", w), ("ind", Xw, lst(1)), ("mp", w), AL.mult)
-                tt(("adj", w), ("ind", yw, lc), ("old", w), AL.subtract)
-                tt(("vv", w), ("xh", w), ("mp", w), AL.mult)
-                tt(("ind", yw, lc), ("vv", w), ("adj", w), AL.add)
+                lin("eh", ("eh", w), ("E16", w), 0.0078125, 1536.0 - 0.49609375)
+                pl = [(k_(T128), svw), (k_(I128), ("Rl", w))]
+                mm(grp((pv, seg(0)), [(k_(ID), ("E16", w)), (k_(IN128), ("eh", w))] + pl) +
+                   grp((pv, seg(1)), [(k_(ID), ("eh", w))] + pl))
+                lin("V16", ("V16", seg(0, v0)), (pv, seg(0)), 1.0, 196608.0)
+                lin("V16", ("V16", seg(1, v0)), (pv, seg(1)), 1.0, -1536.0)
+                if ft:
+                    mm([(("p7", full), ("o129", full), ("FC", full), True, False)] +
+                       [(("p7", full), ("o16", full), k_(IN1), False, False)] * last)
+                    fm = [(("p7", S_(0, 8), S_(max(p - 1, 0), p + 1)), ("Rr", p - 1, seg(v)) if p else ("V16", seg(v)),
+                           ("Sel", v, S_(0, 8), S_(0 if p else 1, 2)), False, p == 15 and v == 1)
+                          for p in range(16) for v in range(2)]
+                else:
+                    fm = grp((pf, seg(0)), [(("Fw", v, S_(16 - p, 144 - p) if p else S_(144, 272)),
+                                             ("Rr", p - 1, seg(v, v0)) if p else ("V16", seg(v, v0)))
+                                            for p in range(16) for v in range(2)])
+                for p in range(16):
+                    if p:
+                        lin("Rr", ("Rr", p - 1, vw), ("V16", vw), 1.0, -128.0 * p, True)
+                    if p % 2:
+                        mm(fm[2 * p - 2:2 * p + 2])
+            if last:
+                break
+            if ft:
+                lin("Ft", ("Ft", full), ("p7", full))
+                mm(grp(("p7", S_(128, 256)), [(("Ft", full), k_(ID))]))
+                lin("Ff", ("Ff", w), ("p7", S_(128, 256)))
+            else:
+                lin("Ff", ("Ff", w), (pf, seg(0)), 1.0, c_(FB))
+            cp(("ind", Cw, ("lu", S_(16 + W * r // 16, 16 + W * (r + 1) // 16))), ("Ff", w))
         tag[0] = -1
+        up = S_(128, 256)
+        mm(grp(("p6", full), [(k_(ID), ("kh", full)), (k_(ZF), ("sv", full, 0))]) +
+           grp(("p6", up), [(k_(ID), ("kh", up)), (k_(ZF), ("sv", full, 0))]))
+        lin("sel", ("sel", S_(0, 256)), ("p6", S_(0, 256)), 1.0, -1600.0, True)
+        mm(grp(("p6", full), [(k_(BM), ("St", full)), (k_(BM), ("sel", full))]) +
+           grp(("p6", up), [(k_(BM), ("St", up)), (k_(BM128), ("sel", up))]))
+        scan(("ls", S_(0, 256)), ("p6", S_(0, 256)), ("cd", S_(0, 256)), -65536.0, AL.max, AL.add)
+        if last:
+            lin("mi", ("mi", full), ("p6", up), 1.0 / 256, 1.0 - 127.5 / 256)
+        lin("lu", ("lu", S_(0, 16)), ("ls", S_(15, 256, 16)), 1.0, 16384.0)
+        tt(("xa", full), ("ind", ("xg", S_(0, 2048)), ("lu", S_(0, 8))), ("xs", S_(15, 2048, 16)), AL.add)
+        lin("xh", ("xh", full), ("xa", full), 0.5, STEP / 2 - 0.25)
         if not last:
-            mm(grp(("p6", full), [(k_(BM), ("sv", full))]))
+            cp(("ind", Xw, ("lu", S_(8, 16))), ("xh", full))
+        else:
+            lc = ("lc", S_(0, 8))
+            yw = ("yxb", S_(0, 256))
+            lin("mi", ("mp", full), ("mi", full))
+            lin("mi", ("li", S_(0, 8)), ("ls", S_(128 + 15, 256, 16)), 1.0, 16384.0)
+            ts(("li", S_(8, 16)), ("li", S_(0, 8)), 255, AL.bitwise_and)
+            lin("mi", lc, ("li", S_(8, 16)))
+            tt(("old", full), ("ind", Xw, ("lu", S_(8, 16))), ("mp", full), AL.mult)
+            tt(("adj", full), ("ind", yw, lc), ("old", full), AL.subtract)
+            tt(("vv", full), ("xh", full), ("mp", full), AL.mult)
+            tt(("ind", yw, lc), ("vv", full), ("adj", full), AL.add)
+        if not last:
+            mm(grp(("p6", full), [(k_(BM), ("sv", full, 0))]))
             vec("acc", ("junk", full), [("p6", full)], (("junk", full), ("p6", full), c_(AC)), "S", [c_(AC)])
             lin("A", ("Ab", S_(0, LH)), ("one", S_(0, LH)), c_(AC))
         else:
-            prev = None
-            for j, w in enumerate(quarters):
-                lin("cv", ("C16", w), ("C", w))
-                prev = mm([(("p6", S_(0, 256)), ("Dg", m, full), ("C16", S_(256 * m, 256 * m + 256)), m == 0, m == 7)
-                           for m in (2 * j, 2 * j + 1)], prev)
-            lin("yb", ("ycb", S_(0, 256)), ("p6", S_(0, 256)))
-    for (y, src) in (("ys", ("ysb", blk, S_(0, 16))), ("yz", ("yzb", blk, S_(0, 16))),
-                     ("yx", ("yxb", S_(0, 256))), ("yc", ("ycb", S_(0, 256)))):
+            lin("Fz", ("Fz", S_(0, 72, 9), S_(0, 16)), ("p7", full))
+            fin = grp(("p4", S_(0, 256)), [(("Fz", S_(8 * q, 8 * q + 8), S_(0, 16)), ("OH", q, S_(0, 256))) for q in range(8)])
+            mm(fin)
+            tt(("ycb", S_(0, 256)), ("yc0", S_(0, 256)), ("p4", S_(0, 256)), AL.add)
+    for (y, src) in (("ys", ("ysb", full)), ("yz", ("yzb", full)), ("yx", ("yxb", S_(0, 256))), ("yc", ("ycb", S_(0, 256)))):
         add("Y", "st", (y, src), [src], [], 131072, "dma")
     return ops
 
@@ -490,9 +600,9 @@ def cost(op, eng, pr):
     if r == "dma":
         return n / pr["bw"], pr["dma"]
     if r == "snd":
-        return pr["snd"], 0.0
+        return pr["snd"] + n * pr["trf"], 0.0
     if r == "xch":
-        return 0.0, pr["xch"] - pr["dma"]
+        return n * pr["row"], pr["xch"]
     if r == "pe":
         return n * pr["pe"], 60.0
     if r == "gp":
@@ -506,87 +616,207 @@ def cost(op, eng, pr):
 
 def schedule(ops, opt, pr):
     n = len(ops)
-    rng = np.random.RandomState(opt["seed"])
-    succ = [[] for _ in ops]
-    wait = [0] * n
-    for i, o in enumerate(ops):
-        for d in o["deps"] | o["bank"]:
-            succ[d].append(i)
-            wait[i] += 1
-    rank = [0.0] * n
-    for i in range(n - 1, -1, -1):
-        a, b = cost(ops[i], ops[i]["eng"][0], pr)
-        rank[i] = (a + b + pr["lat"]) * (1.0 + opt["jit"] * float(rng.rand())) + max([rank[j] for j in succ[i]] + [0.0])
-    for i in range(n):
-        rank[i] += opt["pri"].get(ops[i]["key"], 0.0) - opt["stag"] * max(ops[i]["tag"], 0)
-    pred = [sorted(o["deps"] | o["bank"]) for o in ops]
-    tab = [{e: cost(o, e, pr) for e in o["eng"]} for o in ops]
     lat = pr["lat"]
+    pred = [[(d, d in o["deps"]) for d in sorted(o["deps"] | o["bank"])] for o in ops]
+    succ = [[] for _ in ops]
+    for i in range(n):
+        for d, hard in pred[i]:
+            succ[d].append((i, hard))
+    tab = [{e: cost(o, e, pr) for e in o["eng"]} for o in ops]
 
-    def sweep(key, back):
-        before, after = (succ, pred) if back else (pred, succ)
-        wait = [len(x) for x in before]
-        busy = {e: [] for e in "VSPGYR"}
+    def sweep(key, back, bias, fixed=None):
+        before = succ if back else pred
+        key = list(key)
+        for i in (range(n - 1, -1, -1) if back else range(n)):
+            for d, _ in before[i]:
+                if key[d] >= key[i]:
+                    key[i] = key[d] + 0.001
+        start = {e: [] for e in "VSPGYR"}
+        stop = {e: [] for e in "VSPGYR"}
+        order = {e: [] for e in "VSPGYR"}
         end = [0.0] * n
         where = [None] * n
-        todo = [(key[i], i) for i in range(n) if not wait[i]]
-        while todo:
-            x = min(todo)
-            todo.remove(x)
-            i = x[1]
-            for j in after[i]:
-                wait[j] -= 1
-                if not wait[j]:
-                    todo.append((key[j], j))
+        for i in np.argsort(key, kind="stable").tolist():
             best = None
-            for e in ops[i]["eng"]:
+            for e in (fixed[i] if fixed else ops[i]["eng"]):
                 a, b = tab[i][e]
                 st = b if back else 0.0
-                for d in before[i]:
-                    hard = i in ops[d]["deps"] if back else d in ops[i]["deps"]
-                    if where[d] == e and (e == "P" or not hard):
-                        st = max(st, end[d])
-                    else:
-                        st = max(st, end[d] + lat + (b if back else tab[d][where[d]][1]))
-                for (s0, s1, _) in busy[e]:
-                    if st + a <= s0:
-                        break
-                    if s1 > st:
-                        st = s1
-                k = st + a * (opt["vg"] if e == "V" else 1.0)
+                for d, hard in before[i]:
+                    x = end[d]
+                    if where[d] != e or (hard and e != "P"):
+                        x += lat + (b if back else tab[d][where[d]][1])
+                    if x > st:
+                        st = x
+                s0, s1 = start[e], stop[e]
+                p = m = len(s0)
+                while p and s1[p - 1] > st:
+                    p -= 1
+                while p < m and st + a > s0[p]:
+                    st = s1[p]
+                    p += 1
+                k = st + a * (bias[i] if e == "V" else 1.0)
                 if best is None or k < best[0]:
-                    best = (k, e, st, a)
-            _, e, st, a = best
-            busy[e].append((st, st + a, i))
-            busy[e].sort()
+                    best = (k, e, st, a, p)
+            _, e, st, a, p = best
+            start[e].insert(p, st)
+            stop[e].insert(p, st + a)
+            order[e].insert(p, i)
             end[i] = st + a
             where[i] = e
-        return busy, where, end
+        return max(end[i] + tab[i][where[i]][1] for i in range(n)), order, where, end
 
-    key = [-x for x in rank]
-    best = None
-    for it in range(opt["it"] + 1):
-        busy, where, end = sweep(key, False)
-        span = max(end[i] + tab[i][where[i]][1] for i in range(n))
-        if best is None or span < best[0]:
-            best = (span, {e: [x[2] for x in busy[e]] for e in busy}, where)
-        if it < opt["it"]:
-            end = sweep([-(end[i] + tab[i][where[i]][1]) for i in range(n)], True)[2]
-            key = [-end[i] - opt["pri"].get(ops[i]["key"], 0.0) * opt["pw"] for i in range(n)]
+    def passes(key, bias, more):
+        best = cur = sweep(key, False, bias)
+        for _ in range(more):
+            b = sweep([-(cur[3][i] + tab[i][cur[2][i]][1]) for i in range(n)], True, bias, cur[2])
+            cur = sweep([-x for x in b[3]], False, bias, cur[2])
+            best = cur if cur[0] < best[0] else best
+        return best
+
+    key = [0.0] * n
+    for i in range(n - 1, -1, -1):
+        key[i] = min([key[j] for j, _ in succ[i]] + [0.0]) - sum(tab[i][ops[i]["eng"][0]]) - lat
+    kinds = {}
+    for i, o in enumerate(ops):
+        kinds.setdefault(o["key"], []).append(i)
+    kinds = list(kinds.values())
+    rng = np.random.RandomState(opt["seed"])
+    bias = [1.4] * n
+    best = cur = passes(key, bias, 2)
+    for it in range(opt["it"]):
+        key = [cur[3][i] - tab[i][cur[2][i]][0] for i in range(n)]
+        b2 = list(bias)
+        u = rng.rand()
+        if u < 0.4:
+            for _ in range(rng.randint(1, 4)):
+                d = float(rng.randn()) * 1200.0
+                for i in kinds[rng.randint(len(kinds))]:
+                    key[i] += d
+        elif u < 0.7:
+            c = rng.rand() * cur[0]
+            d = (rng.randn(n) * 600.0).tolist()
+            key = [x + y if abs(x - c) < 3000.0 else x for x, y in zip(key, d)]
+        else:
+            x = (0.3, 1.0, 1.4, 2.0, 4.0)[rng.randint(5)]
+            for i in (kinds[rng.randint(len(kinds))] if u < 0.85 else rng.randint(0, n, 8).tolist()):
+                b2[i] = x
+        c = passes(key, b2, int(rng.rand() < 0.3))
+        if c[0] <= cur[0] + opt["slack"] * (1.0 - it / opt["it"]):
+            cur, bias = c, b2
+            best = c if c[0] < best[0] else best
     return best[1], best[2]
 
 
-PLAN = {}
+def polish(ops, order, where, opt, prs):
+    n, ns = len(ops), len(prs)
+    pred = [[(d, d in o["deps"]) for d in sorted(o["deps"] | o["bank"])] for o in ops]
+    succ = [[] for _ in ops]
+    for i in range(n):
+        for d, _ in pred[i]:
+            succ[d].append(i)
+    tabs = [[{e: cost(o, e, pr) for e in o["eng"]} for o in ops] for pr in prs]
+
+    def run(seq, where, s, p0, end, fin):
+        tab, lat = tabs[s], prs[s]["lat"]
+        free = {e: None for e in order}
+        p, left = p0 - 1, len(free)
+        while p >= 0 and left:
+            if free[where[seq[p]]] is None:
+                free[where[seq[p]]] = end[seq[p]]
+                left -= 1
+            p -= 1
+        for i in seq[p0:]:
+            e = where[i]
+            st = free[e] or 0.0
+            for d, hard in pred[i]:
+                x = end[d] if where[d] == e and (e == "P" or not hard) else fin[d]
+                if x > st:
+                    st = x
+            a, b = tab[i][e]
+            free[e] = end[i] = st + a
+            fin[i] = st + a + b + lat
+        return max(fin) - lat
+
+    def held(seq, where, s, end, fin):
+        last, before = {}, [None] * n
+        for i in seq:
+            before[i] = last.get(where[i])
+            last[where[i]] = i
+        i = fin.index(max(fin))
+        pairs = []
+        while i is not None:
+            e, nxt = where[i], None
+            for d, hard in pred[i]:
+                if (end[d] if where[d] == e and (e == "P" or not hard) else fin[d]) > end[i] - tabs[s][i][e][0] - 1e-6:
+                    nxt = d
+            if nxt is None and before[i] is not None:
+                nxt = before[i]
+                pairs.append((nxt, i))
+            i = nxt
+        return pairs
+
+    done, seq, pos = [False] * n, [], {e: 0 for e in order}
+    while len(seq) < n:
+        for e in order:
+            while pos[e] < len(order[e]) and all(done[d] for d, _ in pred[order[e][pos[e]]]):
+                done[order[e][pos[e]]] = True
+                seq.append(order[e][pos[e]])
+                pos[e] += 1
+    ends, fins = [[0.0] * n for _ in prs], [[0.0] * n for _ in prs]
+    base = [run(seq, where, s, 0, ends[s], fins[s]) for s in range(ns)]
+    weight = [base[0] / b / ns for b in base]
+    cur, fresh = base[0], True
+    best = (cur, seq, where)
+    rng = np.random.RandomState(opt["seed"])
+    at = [0] * n
+    for it in range(opt["moves"]):
+        if fresh:
+            seq = sorted(seq, key=lambda i: ends[0][i] - tabs[0][i][where[i]][0])
+            for p, i in enumerate(seq):
+                at[i] = p
+            pairs = [held(seq, where, s, ends[s], fins[s]) for s in range(ns)]
+            fresh = False
+        some = pairs[rng.randint(ns)]
+        u, v = some[rng.randint(len(some))]
+        r = rng.rand()
+        s2, w2 = list(seq), where
+        if r < 0.4:
+            p0 = max([at[u] - (rng.randint(12) if rng.rand() < 0.3 else 0)] + [at[d] + 1 for d, _ in pred[v]])
+            if p0 > at[u]:
+                continue
+            s2.insert(p0, s2.pop(at[v]))
+        elif r < 0.75:
+            p = min([at[v] + 1 + (rng.randint(25) if rng.rand() < 0.5 else 0), n] + [at[d] for d in succ[u]])
+            if p <= at[v]:
+                continue
+            p0 = at[u]
+            s2.insert(p - 1, s2.pop(p0))
+        else:
+            x = u if rng.rand() < 0.6 else v
+            if len(ops[x]["eng"]) < 2:
+                continue
+            w2 = list(where)
+            w2[x] = "S" if where[x] == "V" else "V"
+            p0 = at[x]
+        e2, f2 = [list(x) for x in ends], [list(x) for x in fins]
+        c = sum(weight[s] * run(s2, w2, s, p0, e2[s], f2[s]) for s in range(ns))
+        if c <= cur - 50.0 * 0.16 ** (it / opt["moves"]) * math.log(1.0 - rng.rand()):
+            cur, seq, where, ends, fins, fresh = c, s2, w2, e2, f2, True
+            best = (c, seq, where) if c < best[0] else best
+    return {e: [i for i in best[1] if best[2][i] == e] for e in order}, best[2]
+
+
+PLAN = []
 
 
 def rank_program(g, core, T, topo):
     rank = T.rank_of(core)
     if rank is None:
         return
+    ops = build(OPT, rank)
     if not PLAN:
-        PLAN["ops"] = build(OPT)
-        PLAN["order"], PLAN["where"] = schedule(PLAN["ops"], OPT, PAR0)
-    ops, order, where = PLAN["ops"], PLAN["order"], PLAN["where"]
+        PLAN.extend(polish(ops, *schedule(ops, OPT, PAR0), OPT, [PAR0, PAR1]))
+    order, where = PLAN
     queue = {"V": g.vector, "S": g.scalar, "P": g.tensor, "G": g, "Y": g.sync}
 
     def ap(x):
@@ -613,11 +843,10 @@ def rank_program(g, core, T, topo):
     for i in order["Y"]:
         if ops[i]["kind"] == "ld":
             signal[i] = ("ld%d" % ops[i]["args"][2], 16)
-    nr = len(T.cores)
-    per = min(len(topo.engines(core, c)) for c in T.cores if c != core) // nr
     for i in order["R"]:
-        signal[i] = ("arr%d" % ops[i]["args"][0], per * (nr - 1) + 16)
-    sends = 0
+        a = ops[i]["args"]
+        signal[i] = ("arr%d" % a[0], a[2] * len(a[1]))
+    left = 0
     for e in "YGPSV":
         q = queue[e]
         seen = {}
@@ -661,25 +890,21 @@ def rank_program(g, core, T, topo):
                 ins = q.iota(ap(a[0]), a[1], a[2], a[3])
             elif k == "iota":
                 ins = q.iota(ap(a[0]), a[1], a[2], a[3], allow_small_or_imprecise_dtypes=True)
-            elif k == "diag":
-                ins = q.affine_select(ap(a[0]), ap(a[1]), [[-1, 128]], AL.is_equal, 0.0, 0, 1)
-            elif k == "own":
-                q.dma_start(T.lnd[:, a[1] + 1, rank, a[2]], T.snd[:, a[1], rank, a[2]]).then_inc(T.sem["arr%d" % a[0]], 16)
+            elif k == "sel":
+                ins = q.affine_select(ap(a[0]), ap(a[1]), a[2], a[3], a[4], a[5], a[6])
             elif k == "ld":
                 q.dma_start(ap(a[0]), ap(a[1])).then_inc(T.sem["ld%d" % a[2]], 16)
             elif k == "st":
                 q.dma_start(T[a[0]][:], ap(a[1])).then_inc(T.sem.stored, 16)
             elif k == "send":
                 tr = []
-                for j in range(1, nr):
-                    b = (rank + j) % nr
+                for j, (b, src, dst) in enumerate(a[1]):
                     rid, pid, _ = topo.addr(T.cores[b])
-                    mask = sum(1 << x for x in topo.engines(core, T.cores[b])[per * (j - 1):per * j])
+                    mask = sum(1 << x for x in topo.engines(core, T.cores[b])[a[2] * j:a[2] * (j + 1)])
                     tr.append(RemoteDMATransfer(dst_ids=[DstId(rid=rid, pnc=pid)], dma_engine_mask=mask,
-                                                remote_sem=T.sem["arr%d" % a[0]], src=T.snd[:, a[1], b, a[2]],
-                                                dst=T.lnd[:, a[1] + 1, rank, a[2]]))
+                                                remote_sem=T.sem["arr%d" % a[0]], src=ap(src), dst=ap(dst)))
                 q.remote_dma_fused(tr, local_sem=T.sem.left)
-                sends += 1
+                left += a[2] * len(tr)
             if i in signal and e != "Y":
                 ins.then_inc(T.sem[signal[i][0]], 1)
         if e == "Y":
@@ -687,4 +912,4 @@ def rank_program(g, core, T, topo):
             for s in sorted(total):
                 q.wait_ge(T.sem[s], total[s])
         if e == "G":
-            q.wait_ge(T.sem.left, sends * per * (nr - 1))
+            q.wait_ge(T.sem.left, left)

@@ -18,43 +18,42 @@ def sb(n, d):
 
 SCRATCH = {
     "s0b": sb(128, I32), "z0b": sb(128, BF), "cmb": sb(2048, I32), "X": sb(8192, BF),
-    "C": sb(2048, I32), "M": sb(2064, I32),
+    "C": sb(2048, I32), "M": sb(2048, I32),
     "DJ": sb(160, BF), "BI": sb(128, BF), "CcM": sb(128, BF), "ki": sb(8, I32), "ia": sb(17, F32), "t5": sb(5, F32),
-    "Sf": sb(384, F32), "St": sb(384, F16), "rst": sb(512, BF), "cd": sb(384, BF), "col": sb(32, F32),
-    "R": sb(17, F32), "Rd": sb(16, F32), "tny": sb(64, F32), "Z": sb(2064, BF), "Wz": sb(144, BF),
-    "Sel": sb([2, 8, 2], F16), "o129": sb(128, BF), "FC": sb(128, BF), "Ft": sb(128, F16), "Fw": sb([2, 272], F16),
-    "K": sb([25, 128], F16), "Ab": sb(128, F16), "Cy": sb([8, 32], F16), "Dm": sb([8, 128], F16),
+    "St": sb(384, BF), "cd": sb(256, BF), "col": sb(32, F32), "R": sb(17, F32), "Rd": sb(16, F32),
+    "tny": sb(64, F32), "Z": sb(2064, BF), "Wz": sb(144, BF), "Sel": sb([8, 2], F32), "FC": sb(128, BF),
+    "K": sb([18, 128], F16), "CN": sb(128, BF), "I32": sb(128, F32), "Cy": sb([8, 32], F16), "Dm": sb([8, 128], F16),
     "Om": sb([8, 128], F16), "Cm": sb([8, 128], BF), "Fl": sb([4, 128], F16), "Bj": sb([4, 128], F16),
-    "Dg": sb([32, 128], BF), "one": sb(128, F16),
-    "mS0": sb([21, 64], U16), "mS1": sb([6, 64], U16), "mz0": sb([21, 64], F16), "mz1": sb([6, 64], F16),
-    "mc0": sb([21, 4, 32], U16), "mc1": sb([6, 4, 32], U16), "Sl": sb(128, U16), "zf": sb(128, F16), "fl": sb([2, 128], F16), "G": sb(2048, F16), "E16": sb(128, F16),
-    "Pp": sb(128, F32), "eq": sb(1024, F16), "Qm": sb(128, F32), "hr": sb(128, BF), "I32": sb(128, F32),
-    "c16": sb(64, F16), "J": sb(256, BF), "OH": sb([8, 256], F16), "cT": sb(8, F32), "o16": sb(128, F16),
-    "R32": sb([16, 128], F32), "Sel32": sb([8, 2], F32), "Fw32": sb(272, F32), "Fz": sb([72, 16], F16), "yc0": sb(256, F32),
+    "Dg": sb([32, 128], BF), "one": sb(128, BF), "J": sb(256, BF),
+    "mc": sb([36, 2, 64], U16), "Sl": sb(128, U16), "zf": sb([8, 16], F16), "xf": sb(128, BF),
+    "fl": sb([2, 128], F16), "G": sb(2048, F16), "E16": sb(128, F16),
+    "Pp": sb(128, F32), "eq": sb(1024, F16), "Qm": sb(128, F32), "hr": sb(128, BF),
+    "OH": sb([8, 256], F16), "cT": sb(8, F32), "o16": sb(128, F16), "Ft": sb(128, F16),
+    "R32": sb([16, 128], F32), "Fz": sb([72, 16], F16), "yc0": sb(256, F32),
     "hu": sb(128, U16), "kh": sb(256, F16), "xg": sb(2048, BF), "gq": sb([4, 128], F16), "fg": sb(128, F16),
-    "wn": sb(128, F16), "sv": sb([128, 2], F16), "eu": sb(128, U16), "mg": sb(2048, F16), "ms": sb(2048, F16),
-    "xs": sb(2048, F16), "Rl": sb(128, F16), "eh": sb(128, F16), "V16": sb(256, F16), "Rr": sb([15, 256], F16),
-    "Ff": sb(128, F32), "sel": sb(256, F16), "ls": sb(384, F32), "lu": sb(24, U16), "junk": sb(128, F32),
+    "wn": sb(128, F16), "sv": sb([129, 2], F16), "eu": sb(128, U16), "mg": sb(2048, F16), "ms": sb(2048, F16),
+    "xs": sb(2048, F16),
+    "Ff": sb(128, F32), "sel": sb(256, F16), "ls": sb(384, F32), "lu": sb(24, U16), "junk": sb(129, F32),
     "xa": sb(128, F32), "xh": sb(128, I32), "cs": sb(2048, BF),
     "yxb": sb(256, F32), "ycb": sb(256, F32), "ysb": sb(128, F32), "yzb": sb(128, BF), "C16": sb(2048, F16),
     "mi": sb(128, I32), "mp": sb(128, F32), "li": sb(16, I32), "lc": sb(8, U16), "old": sb(128, F32),
     "adj": sb(128, F32), "vv": sb(128, F32),
 }
 for _b in range(8):
-    SCRATCH["p%d" % _b] = ("psum", [128, 512] if _b < 7 else [128, 32, 16], F32)
+    SCRATCH["p%d" % _b] = ("psum", [128, 512] if _b != 4 else [128, 32, 16], F32)
 SEMAPHORES = ["qV", "qS", "qP", "qG", "left", "stored"] + ["ld%d" % s for s in range(8)] + \
-    ["arr%d" % s for s in range(12)]
+    ["arr%d" % s for s in range(NS * (RO - 1))]
 
-LC, CC, CP, PAR, NL, WW, DG, NDG, THR, CQ, STC, W8, SC, AC, KK, L15B, FB, M1, MB, NR8, R82 = range(21)
-BM, DMB, DMN, DMZ, ID, IN1, I3K, IN4K, I128, IN128, IN16, T128, SG, ZF, BM128, LO, BE, TMP, TM2, TM3, B32, CN, \
-    S3K, SN4K, SH8 = range(25)
+LC, CC, CP, PAR, WW, DG, NDG, THR, CQ, W8, AC, L15B, M1, MB, L2K, R82, R8H, NTH = range(18)
+BM, DMB, DMN, B2K, T2K, SG, ZF, BM128, LO, BE, TMP, TM2, TM3, B32, B512, S3K, SH8 = range(17)
 
-PAR0 = {"cyc": 0.87, "fix": 40.0, "g": 1.56, "sc": 3.8, "pe": 0.5, "lat": 170.0, "xch": 250.0, "row": 30.0,
-        "snd": 600.0, "trf": 45.0, "bw": 400.0, "dma": 2000.0, "sfix": 30.0}
-PAR1 = dict(PAR0, cyc=1.1, g=1.9, pe=0.58, sc=4.5, snd=1200.0, trf=80.0, xch=800.0, lat=220.0)
-OPT = {"seed": 0, "it": 2000, "moves": 20000, "slack": 100.0, "fs": [1, 1, 1, 1], "zc": 2, "sc": 2,
-       "pre": [3, 3, 3, 3], "ccp": [5, 5, 5, 15], "far": [3, 3, 3, 3], "gp": 32, "f32": 1, "cmb": 1,
-       "eng": {}}
+PAR0 = {"cyc": 0.87, "fix": 40.0, "g": 1.56, "sc": 3.8, "pe": 0.5, "lat": 170.0, "xch": 100.0, "row": 40.0,
+        "snd": 600.0, "trf": 45.0, "bw": 400.0, "dma": 1000.0, "sfix": 30.0}
+PAR1 = dict(PAR0, cyc=1.1, g=1.9, pe=0.58, sc=4.5, snd=1200.0, trf=80.0, xch=800.0, lat=220.0, dma=1800.0)
+OPT = {"seed": 0, "it": 600, "moves": 4000, "slack": 60.0, "ccp": [1, 1, 1, 5], "far": [3, 3, 3, 3],
+       "marks": 0.03, "reach": 60, "sign": 0, "xa": [0, 0, 0, 0], "rounds": 9, "parts": 0.1,
+       "pieces": [0, 576, 1152, 1728, 2048],
+       "gp": 32, "cut": 4, "gp_copies": ("eu", "z16", "mp", "lc", "cd"), "eng": {"gM": "S"}}
 
 
 def S_(a, b, c=None):
@@ -64,11 +63,11 @@ def S_(a, b, c=None):
 def build(opt, rank):
     ops = []
     acc = {}
-    tag = [-1, -1]
+    tag = [-1, -1, "constants"]
     half, own = rank // NB, rank % NB
 
     def span(a):
-        if len(a) == 2 and a[0] == "p7":
+        if len(a) == 2 and a[0] == "p4":
             return 0, a[1].start, a[1].stop - a[1].start
         shp = SCRATCH[a[0]][1][1:]
         ix = np.arange(int(np.prod(shp))).reshape(shp)[a[1:]].ravel().tolist()
@@ -107,7 +106,7 @@ def build(opt, rank):
         deps.discard(me)
         bank.discard(me)
         ops.append({"eng": eng, "kind": kind, "args": args, "deps": deps, "bank": bank - deps, "n": n, "rate": rate,
-                    "level": tag[1], "key": kind + (wr[0][0] if wr else "") + str(tag[0])})
+                    "level": tag[1], "part": tag[2], "key": kind + (wr[0][0] if wr else "") + str(tag[0])})
         return me
 
     def vec(kind, out, ins, args, eng="V", more=()):
@@ -157,6 +156,11 @@ def build(opt, rank):
     def put(out, src, pat, base, fill):
         return add("G", "sel", (out, src, pat, AL.not_equal, fill, base, 1), [src], [out], span(out)[2], "gp")
 
+    def copy(name, out, src):
+        if name in opt["gp_copies"]:
+            return put(out, src, [[0, span(out)[2]]], 1, 0.0)
+        return lin(name, out, src)
+
     def after(op, *deps):
         ops[op]["deps"].update(d for d in deps if d is not None)
         return op
@@ -170,70 +174,68 @@ def build(opt, rank):
     def y_(a, b):
         return ("tny", S_(a, b))
 
-    def load(j, dst, src, nbytes):
-        me = add("Y", "ld", (dst, src, j), [], [dst], nbytes, "dma")
-        if j:
+    def load(q, j, dst, src, nbytes):
+        me = add(q, "ld", (dst, src, j), [], [dst], nbytes, "dma")
+        if j and q == "Y":
             ops[me]["bank"].add(me - 1)
 
     full = S_(0, 128)
     quarters = [S_(512 * j, 512 * j + 512) for j in range(4)]
-    load(0, ("cmb", quarters[0]), ("cm", quarters[0]), 262144)
-    load(1, ("s0b", full), ("s0", full), 65536)
-    for j in range(1, 4):
-        load(1 + j, ("cmb", quarters[j]), ("cm", quarters[j]), 262144)
-    load(5, ("z0b", full), ("z0", full), 32768)
-    load(6, ("X", S_(0, 8192)), ("x0", S_(0, 8192)), 2097152)
+    pieces = [S_(a, b) for a, b in zip(opt["pieces"], opt["pieces"][1:])]
+    for j, w in enumerate(pieces):
+        load("Y", j, ("cmb", w), ("cm", w), 512 * (w.stop - w.start))
+    load("Y", 4, ("X", S_(0, 8192)), ("x0", S_(0, 8192)), 2097152)
+    load("S", 5, ("s0b", full), ("s0", full), 65536)
+    load("S", 6, ("z0b", full), ("z0", full), 32768)
 
     DJ = ("DJ", S_(0, 160)); D0 = ("DJ", full)
     R0 = ("R", S_(0, 1))
     iota(("ki", S_(0, 1)), [[0, 1]], 0, 1)
     iota(("ia", S_(0, 17)), [[1, 17]], 0, 0)
     iota(DJ, [[1, 160]], 0, -1)
-    iota(("BI", full), [[16, 8], [0, 16]], 0, -1)
+    iota(("BI", full), [[-16, 8], [0, 16]], 0, 1)
     iota(("t5", S_(0, 5)), [[-1, 5]], 4, 0)
     iota(("CcM", full), [[0, 8], [1, 4], [0, 4]], 0, 0)
     turn = LH * (1 - 2 * half)
-    iota(("Sf", full), [[16, 128]], 0, 0)
-    iota(("Sf", S_(128, 256)), [[turn, NS], [1, LH]], LH * half, 0)
-    iota(("Sf", S_(256, 384)), [[16 * turn, NS], [16, LH]], 16 * LH * half, 0)
-    ms(("Z", S_(0, 2064)), 0.0)
-    put(("Z", S_(16, 2064, 16)), ("Z", S_(16, 2064, 16)), [[-1, 16], [-16, 8]], 0, 1.0)
-    ms(("cs", S_(0, 512)), 0.0)
+    iota(("St", full), [[32, 128]], 0, 0)
+    iota(("St", S_(128, 256)), [[2 * turn, NS], [2, LH]], 2 * LH * half, 0)
+    iota(("St", S_(256, 384)), [[32 * turn, NS], [32, LH]], 32 * LH * half, 0)
+    ms(("Z", S_(0, 1040)), 0.0)
+    lin("k", ("Z", S_(1040, 2064)), ("Z", S_(0, 1024)))
     for k in (0, 4):
         a = ("Cm", S_(k, k + 4), full)
-        put(a, ("cs", S_(0, 512)), [[-1, 4], [-16, 8], [0, 16]], -k, STEP)
+        put(a, ("Z", S_(0, 512)), [[-1, 4], [-16, 8], [0, 16]], -k, STEP)
         put(a, a, [[-1, 4], [-16, 8], [0, 16]], -k - 1, -STEP)
+    put(("Z", S_(16, 2064, 16)), ("Z", S_(16, 2064, 16)), [[-1, 16], [-16, 8]], 0, 1.0)
+
+    def diag(out, v):
+        add("G", "sel", (out, ("DJ", S_(v, v + 128)), [[-1, 128]], AL.is_equal, 0.0, 0, 1), [DJ], [out], 128, "gp")
     for m in range(32):
-        add("G", "sel", (("Dg", m, full), ("DJ", S_(m + 1, m + 129)), [[-1, 128]], AL.is_equal, 0.0, 0, 1),
-            [DJ], [("Dg", m, full)], 128, "gp")
+        diag(("Dg", m, full), m + 1)
+    diag(("I32", full), 1)
+    ID = ("Dg", 0, full)
     ki = ("ki", S_(0, 1))
-    unit, fb = (2048.0, 2048.0) if opt["f32"] else (128.0, 16512.0)
     ts(("ki", S_(4, 5)), ki, 15, AL.bitwise_and)
     ts(("ki", S_(5, 6)), ki, 2, AL.logical_shift_right, 3, AL.bitwise_and)
     ts(("ki", S_(6, 7)), ki, 3, AL.bitwise_and)
     ts(("ki", S_(7, 8)), ki, 1, AL.bitwise_and)
     cp(("col", S_(0, 4)), ("ki", S_(4, 8)))
     ts(("R", S_(0, 17)), ("ia", S_(0, 17)), c_(LC), AL.is_equal)
-    for j, src, mul, addc in ((L15B, LC, -1.0, 15.0), (NL, LC, -1.0, 0.0), (WW, PAR, -2.0, 1.0),
-                              (CQ, CC, 1024.0, 0.0), (KK, LC, 1.0, 1536.0), (FB, LC, fb, -15 * fb)):
+    for j, src, mul, addc in ((L15B, LC, -1.0, 15.0), (WW, PAR, -2.0, 1.0), (CQ, CC, 0.25, 0.0), (L2K, LC, 2048.0, 0.0)):
         lin("k", c_(j), c_(src), mul, addc)
-    ts(k_(BM), ("BI", full), c_(NL), AL.is_equal)
+    ts(k_(BM), ("BI", full), c_(LC), AL.is_equal)
     lin("k", k_(TMP), k_(BM), -1024.0, 1024.0)
     tt(k_(DMB), D0, k_(TMP), AL.add)
-    ts(k_(ID), D0, 0.0, AL.is_equal)
-    for j, v in ((IN1, -1.0), (I3K, 12288.0), (IN4K, -4096.0), (I128, unit), (IN16, -16.0)) + \
-            ((IN128, -128.0),) * (1 - opt["f32"]):
-        ts(k_(j), D0, 0.0, AL.is_equal, v, AL.mult)
-    for j, v in ((S3K, 12288.0), (SN4K, -4096.0)) * (max(opt["far"]) > 0) + ((SH8, 1.0),) * (min(opt["far"]) < 3):
+    for j, v in ((S3K, 3.0),) * (max(opt["far"]) > 0) + ((SH8, 1.0),):
         ts(k_(j), k_(DMB), -8.0, AL.is_equal, v, AL.mult)
-    lin("k", c_(NR8), ("R", S_(8, 9)), -1.0)
     lin("k", c_(R82), ("R", S_(8, 9)), 2.0)
+    lin("k", c_(R8H), ("R", S_(8, 9)), 0.5)
     for rep in range(2):
-        lin("k", ("Cy", S_(0, 8), S_(16 * rep, 16 * rep + 16)), k_(ID))
+        lin("k", ("Cy", S_(0, 8), S_(16 * rep, 16 * rep + 16)), ID, -1.0)
     for j in range(2):
         pk = "p%d" % (6 + j)
         mm([x for d in range(4) for x in grp((pk, S_(128 * d, 128 * d + 128)), [
-            (k_(ID), k_(ID)), (k_(IN1), ("Cy", S_(0, 8), S_(4 * j + d + 1, 4 * j + d + 17)))])])
+            (ID, ID), (ID, ("Cy", S_(0, 8), S_(4 * j + d + 1, 4 * j + d + 17)))])])
         lin("k", ("Dm", S_(4 * j, 4 * j + 4), full), (pk, S_(0, 512)))
     ts(y_(0, 8), ("ia", S_(1, 9)), c_(LC), AL.add, 16.0, AL.is_lt)
     tt(y_(8, 16), y_(0, 8), ("ia", S_(1, 9)), AL.mult)
@@ -253,9 +255,8 @@ def build(opt, rank):
     tt(y_(34, 38), y_(26, 30), y_(30, 34), AL.subtract)
     ts(y_(38, 42), y_(26, 30), c_(DG), AL.mult, -0.25, AL.mult)
     tt(y_(42, 46), y_(34, 38), y_(38, 42), AL.add)
-    lin("k", y_(50, 54), y_(42, 46), 4.0)
     for j in range(4):
-        lin("k", ("Bj", j, full), k_(ID), y_(50 + j, 51 + j))
+        ts(("Bj", j, full), ID, y_(42 + j, 43 + j), AL.mult, -4.0 if j else 4.0, AL.mult)
     mm([(("p6", S_(128 * j, 128 * j + 128)), k_(BM), ("Bj", j, full), True, True) for j in range(4)])
     lin("k", ("Fl", S_(0, 4), full), ("p6", S_(0, 512)))
     tt(y_(46, 47), y_(21, 22), y_(16, 17), AL.subtract)
@@ -263,104 +264,72 @@ def build(opt, rank):
     lin("k", y_(48, 49), y_(16, 17), 16.0, -0.5)
     ts(y_(49, 50), y_(48, 49), c_(DG), AL.mult, c_(CC), AL.subtract)
     lin("k", c_(THR), y_(47, 48), 1.0, y_(49, 50))
+    if opt["sign"]:
+        lin("k", c_(NTH), c_(THR), -1.0)
     ts(k_(TM2), ("CcM", full), c_(CC), AL.is_equal, c_(NDG), AL.mult)
     lin("k", k_(TM3), k_(TM2), 1.0, c_(DG))
     tt(k_(LO), k_(TM3), k_(BM), AL.mult)
     tt(("Rd", S_(0, 16)), ("R", S_(0, 16)), ("R", S_(1, 17)), AL.subtract)
-    ms(("one", full), 1.0)
-    ms(("rst", S_(0, 512)), 1.0)
-    ms(("rst", S_(0, 512, 16)), 0.0)
+    iota(("one", full), [[0, 128]], 1, 0)
     lin("k", ("cd", S_(0, 16)), ("Rd", S_(0, 16)), 16384.0)
     lin("k", ("cd", S_(15, 16)), ("Rd", S_(15, 16)), 16384.0, -32768.0)
     for a in (16, 32, 64, 128):
-        lin("k", ("cd", S_(a, 2 * a)), ("cd", S_(0, a)))
+        copy("cd", ("cd", S_(a, 2 * a)), ("cd", S_(0, a)))
+
     def beside(out, src, sign):
         return add("G", "sel", (out, src, [[-sign, 128]], AL.is_gt, 0.0, 0, sign), [src], [out], 128, "gp")
-    beside(k_(DMN), k_(BM), 1)
-    put(k_(DMN), k_(DMN), [[-1, 128]], 0, -32.0)
-    beside(k_(DMZ), k_(BM), -1)
-    lin("k", k_(T128), k_(DMZ), unit)
-    tt(k_(SG), k_(DMN), k_(DMZ), AL.subtract)
-    lin("k", k_(ZF), k_(DMZ), -64.0)
+    lin("k", k_(B2K), k_(BM), 2048.0)
+    beside(k_(DMN), k_(B2K), 1)
+    put(k_(DMN), k_(DMN), [[-1, 128]], 0, -31.0 * 2048)
+    beside(k_(T2K), k_(B2K), -1)
+    tt(k_(SG), k_(DMN), k_(T2K), AL.subtract)
+    lin("k", k_(ZF), k_(T2K), -1.0 / 32)
     put(k_(ZF), k_(ZF), [[-1, 128]], 0, 64.0)
-    heads = ("K", BM, S_(0, 128, 16))
-    iota(("FC", full), [[0, 8], [1, 16]], -15, 0)
-    ms(("o129", full), 16.0 if opt["f32"] else 129.0)
-    for v in range(2 - opt["f32"]):
-        for j in range(2):
-            lin("k", ("Sel32", S_(0, 8), j) if opt["f32"] else ("Sel", v, S_(0, 8), j), heads, (2.0 * j - 1.0) * 128.0 ** v)
+    iota(("FC", full), [[0, 8], [16, 16]], -240, 0)
+    for j in range(2):
+        lin("k", ("Sel", S_(0, 8), j), ("K", BM, S_(0, 128, 16)), 2.0 * j - 1.0)
     iota(("J", S_(0, 256)), [[1, 256]], 0, 0)
     iota(("ki", S_(1, 2)), [[0, 1]], LH * half, 1)
     ts(("ki", S_(2, 3)), ("ki", S_(1, 2)), 4, AL.logical_shift_right, 7, AL.bitwise_and)
     lin("k", c_(M1), ("ki", S_(2, 3)), 1.0, 1.0)
     lin("k", c_(MB), ("ki", S_(2, 3)), -256.0)
-    ms(("Fz", S_(0, 72), S_(0, 16)), 0.0)
-    if 2 in opt["fs"] and opt["f32"]:
-        ms(("Fw32", S_(0, 272)), 0.0)
-        for a, sg in ((16, 1.0), (15, -1.0), (144, 1.0)):
-            lin("k", ("Fw32", S_(a, a + 128, 16)), heads, sg)
-    elif 2 in opt["fs"]:
-        ms(("Fw", S_(0, 2), S_(0, 272)), 0.0)
-        for v in range(2):
-            for a, sg in ((16, 1.0), (15, -1.0), (144, 1.0)):
-                lin("k", ("Fw", v, S_(a, a + 128, 16)), heads, sg * 128.0 ** v)
-    lin("k", ("kh", full), k_(BM), 0.0, c_(KK))
-    ts(c_(STC), ("R", S_(1, 2)), 24576.0, AL.mult, ("R", S_(2, 3)), AL.subtract)
-    lin("k", ("St", S_(0, 256)), ("Sf", S_(0, 256)), R0)
-    lin("k", ("St", S_(256, 384)), ("Sf", S_(256, 384)), R0, c_(STC))
-    lin("k", c_(SC), R0, 1.0, STEP)
+    add("G", "sel", (("Fz", S_(0, 72), S_(0, 16)), ("Z", S_(0, 1152)), [[0, 1152]], AL.is_equal, 0.0, 1, 1),
+        [("Z", S_(0, 1152))], [("Fz", S_(0, 72), S_(0, 16))], 1152, "gp")
+    ts(("kh", full), ("one", full), c_(LC), AL.mult, 1536.0, AL.add)
     lin("k", k_(B32), k_(BM), 1.0 / 32)
-    lin("k", k_(CN), k_(BM), -43008.0)
-    ms(("c16", S_(0, LH)), 16.0)
-    ts(("I32", full), D0, 0.0, AL.is_equal)
-    ms(("M", S_(0, 8)), 0)
-    ms(("M", S_(2056, 2064)), 0)
-    for w in quarters:
+    lin("k", k_(B512), k_(BM), 1.0 / 512)
+    lin("k", ("CN", full), k_(BM), -688128.0)
+    ms(c_(AC), 33.0 / 64)
+    ms(("sv", S_(128, 129), 0), 95.0 / 1024)
+    for w in pieces:
         ts(("C", w), ("cmb", w), 2047, AL.bitwise_and)
     for w in quarters:
-        lin("M", ("M", S_(w.start + 8, w.stop + 8)), ("cmb", w), 1.0 / 2048, -1023.5 / 2048)
+        lin("M", ("M", w), ("cmb", w), 1.0 / 2048, -1023.5 / 2048)
 
-    Cw = ("C", S_(0, 2048)); Xw = ("X", S_(0, 8192)); Mw = ("M", S_(0, 2064))
+    Cw = ("C", S_(0, 2048)); Xw = ("X", S_(0, 8192)); Mw = ("M", S_(0, 2048))
     arrive = {}
-    calls = [0]
 
-    def landing(what, t, h):
-        return ("m%s%d" % (what, h), 7 * t - 4 if h == 0 else 2 * t - 1, S_(0, LH))
+    def landing(t, h):
+        return ("mc", 12 * t - (9 if h == 0 else 1))
 
-    def leaving(what, t, h):
-        if opt["cmb"]:
-            part = S_(0, 16) if what == "S" else S_(16, 32)
-            return ("mc0", S_(7 * t + 3 - own, 7 * t + 7 - own), own, part) if h == 0 else ("mc1", 2 * t, S_(0, NB), part)
-        if h == 0:
-            return ("m%s0" % what, S_(7 * t + 3 - own, 7 * t + 7 - own), S_(16 * own, 16 * own + 16))
-        return ("m%s1" % what, 2 * t, S_(0, LH))
+    def leaving(t, h, a):
+        r = 12 * t + (7 if h else 3 - own)
+        return ("mc", S_(r, r + NB), own // 2, S_(a, a + 16))
 
-    def send(what, t, hs, pks):
-        trs = []
-        for h in hs:
-            for j in range(NB):
-                if (h or j != own) and what == "c":
-                    src = ("mc0", 7 * t + 3 - own + j, own, S_(0, 32)) if h == 0 else ("mc1", 2 * t, j, S_(0, 32))
-                    trs.append((NB * (half ^ h) + j, src, landing(what, t + 1, h)[:2] + (own, S_(0, 32))))
-                elif h or j != own:
-                    b = NB * (half ^ h) + j
-                    src = ("m%s0" % what, 7 * t + 3 - own + j, S_(16 * own, 16 * own + 16)) if h == 0 else \
-                        ("m%s1" % what, 2 * t, S_(16 * j, 16 * j + 16))
-                    trs.append((b, src, landing(what, t + 1, h)[:2] + (S_(16 * own, 16 * own + 16),)))
-        per = 4 if len(trs) <= 4 else 2
-        a = (calls[0], trs, per)
-        calls[0] += 1
-        me = add("G", "send", a, [], [], len(trs), "snd", pks)
-        ops[me]["key"] += what
-        me = add("R", "arr", a, [], [], 128 // per, "xch", [me])
-        for h in hs:
-            arrive[what, t + 1, h] = me
+    def send(t, h, pks):
+        mine = (own // 2, S_(32 * (own % 2), 32 * (own % 2) + 32))
+        trs = [(NB * (half ^ h) + j, ("mc", leaving(t, h, 0)[1].start + j) + mine, landing(t + 1, h) + mine)
+               for j in range(NB) if h or j != own]
+        a = (NS * t + h, trs)
+        arrive[t + 1, h] = add("R", "arr", a, [], [], 128 // NB, "xch", [add("G", "send", a, [], [], len(trs), "snd", pks)])
 
     for t in range(RO):
         last = t == RO - 1
         par = t & 1
         tag[1] = t
-        pks = {"S": [], "z": []}
+        pl = "p6" if last else "p7"
+        cols = []
+        tag[2] = "sums"
         if last:
             for m in range(32):
                 mm([(("p7", S_(0, 256)), ("Dg", m, full), ("X", S_(256 * m, 256 * m + 256)), m == 0, m == 31)])
@@ -370,9 +339,8 @@ def build(opt, rank):
                 mm([(("p7", S_(0, 256)), ("Dg", m, full), ("C16", S_(256 * m, 256 * m + 256)), m == 0, m == 7)
                     for m in (2 * j, 2 * j + 1)])
             lin("yb", ("yc0", S_(0, 256)), ("p7", S_(0, 256)))
-        zz = []
         for h in range(NS):
-            tag[0] = h
+            tag[0], tag[2] = h, "members%d" % h
             w = S_(LH * h, LH * h + LH)
             real = S_(LH * (h ^ half), LH * (h ^ half) + LH)
             o = 16 * LH * h
@@ -380,74 +348,86 @@ def build(opt, rank):
             a0, a1 = S_(0, LH), S_(128, 128 + LH)
             chunks = [(LH * h + 32 * j, o + 512 * j) for j in range(LH // 32)]
             if t == 0:
-                lin("Sl", ("Sl", w), ("s0b", real))
-                lin("z16", ("zf", w), ("z0b", real), 1.0, R0)
-                zz.append(("zf", w))
+                copy("Sl", ("Sl", w), ("s0b", real))
+                zz = ("z0b", real)
                 seats = [("Sl", S_(l0, l0 + 32)) for (l0, c0) in chunks]
-            elif opt["cmb"]:
-                row = landing("c", t, h)[:2]
-                after(lin("z16", ("zf", w), row + (S_(0, NB), S_(16, 32))), arrive["c", t, h])
-                zz.append(("zf", w))
-                seats = [row + (j, S_(0, 16)) for j in range(NB)]
-                arrive["S", t, h] = arrive["c", t, h]
             else:
-                zz.append(landing("z", t, h))
-                seats = [landing("S", t, h)[:2] + (S_(l0 - LH * h, l0 - LH * h + 32),) for (l0, c0) in chunks]
+                for j in range(2):
+                    after(copy("z16", ("zf", S_(NB * h + j, NB * h + NB, 2), S_(0, 16)),
+                               landing(t, h) + (S_(0, 2), S_(48 * j, 48 * j + 16))), arrive[t, h])
+                zz = ("zf", S_(NB * h, NB * h + NB), S_(0, 16))
+                seats = [landing(t, h) + (j, S_(16, 48)) for j in range(2)]
             n = 1024 // len(seats)
             for j, s in enumerate(seats):
-                after(gather("gC", ("G", S_(o + n * j, o + n * j + n)), Cw, s), arrive.get(("S", t, h)))
-            after(mm(grp((pc, a0), [(k_(B32), zz[h])])), arrive.get(("z", t, h)))
-            lin("fl", ("fl", par, w), (pc, a0), 2.0, 1536.0 - 0.0625 - 0.46875)
+                after(gather("gC", ("G", S_(o + n * j, o + n * j + n)), Cw, s), arrive.get((t, h)))
+            mm(grp((pc, a0), [(k_(B512), ("one", a0)), (k_(B32), zz)]))
+            lin("fl", ("fl", par, w), (pc, a0), -2.0, 0.0625 + 0.46875 - 1536.0)
+            cols.append(grp((pl, w), [(k_(B32), ("St", S_(256 + LH * h, 256 + LH * h + LH))), (k_(BM), zz),
+                                      (("Dg", 15, full), ("fl", par, w))]))
 
             def fold(src, lhs):
                 mm(grp((pa, a1), [(lhs(k), (src, S_(o + k, o + 16 * LH, 16))) for k in range(16)]))
             fold("G", lambda k: ("Z", S_(128 * ((k + t) & 15) + 16 - k, 128 * ((k + t) & 15) + 144 - k)))
             lin("E16", ("E16", w), (pa, a1))
-            pre = opt["pre"][t] >> h & 1
-            if pre:
-                lin("eu", ("eu", w), ("E16", w), 1.0, 8.0)
-                for l0 in range(w.start, w.stop, opt["gp"]):
-                    gather("gM", ("mg", S_(16 * l0, 16 * (l0 + opt["gp"]))), Mw, ("eu", S_(l0, l0 + opt["gp"])))
-            mm([((pb, S_(LH * d, LH * d + LH)), ("Dm", d, full), ("E16", w), True, True) for d in range(8)])
-            tt(("Pp", w), ("E16", w), (pc, a0), AL.mult)
+            tag[2] = "samplers%d" % h
+            copy("eu", ("eu", w), ("E16", w))
+            for l0 in range(w.start, w.stop, opt["gp"]):
+                gather("gM", ("mg", S_(16 * l0, 16 * (l0 + opt["gp"]))), Mw, ("eu", S_(l0, l0 + opt["gp"])))
+            tag[2] = "coins%d" % h
             e0 = 8 * LH * h
-            ts(("eq", S_(e0, e0 + 8 * LH)), (pb, S_(0, 8 * LH)), 0.0, AL.is_equal)
-            ts(("Qm", w), ("Pp", w), -0.484375, AL.add, 12582912.0, AL.add)
-            oa = grp((pa, a0), [(("I32", full), ("Qm", w)), (k_(CN), ("c16", a0)), (k_(ID), ("E16", w))] +
-                     ([(k_(ID), ("Ab", a0))] if t else []) +
+            cut = opt["cut"]
+            po = pc if cut < 8 else pa
+            for pk, d0, d1 in ((pb, 0, cut), (pa, cut, 8))[:1 + (cut < 8)]:
+                mm([((pk, S_(LH * d, LH * d + LH)), ("Dm", d, full), ("E16", w), True, True) for d in range(d0, d1)])
+            tt(("Pp", w), ("E16", w), (pc, a0), AL.mult)
+            for pk, d0, d1 in ((pb, 0, cut), (pa, cut, 8))[:1 + (cut < 8)]:
+                ts(("eq", S_(e0 + LH * d0, e0 + LH * d1)), (pk, S_(LH * d0, LH * d1)), 0.0, AL.is_equal)
+            ts(("Qm", w), ("Pp", w), c_(AC), AL.add, 12582911.0, AL.add)
+            oa = grp((po, a0), [(("I32", full), ("Qm", w)), (("CN", full), ("one", a0)), (ID, ("E16", w))] +
                      [(("Om", d, full), ("eq", S_(e0 + LH * d, e0 + LH * d + LH))) for d in range(8)])
-            mm(oa[:-8])
-            mm(oa[-8:])
-            lin("hr", ("hr", w), (pa, a0), 1.0, -4095.5)
-            tt(("hu", w), (pa, a0), ("hr", w), AL.subtract)
+            mm(oa[:3])
+            mm(oa[3:3 + cut])
+            if cut < 8:
+                mm(oa[3 + cut:])
+            lin("hr", ("hr", w), (po, a0), 1.0, -4095.5)
+            tt(("hu", w), (po, a0), ("hr", w), AL.subtract)
             for (l0, c0) in chunks:
                 gather("gX", ("xg", S_(c0, c0 + 512)), Xw, ("hu", S_(l0, l0 + 32)))
-            lin("hh", ("kh", S_(128 + LH * h, 128 + LH * h + LH)), ("hu", w), 0.0078125, 1536.0 - 0.49609375)
+            if h:
+                lin("hh", ("kh", S_(128, 256)), ("hu", full), 0.0078125, 1536.0 - 0.49609375)
+            tag[2] = "bins%d" % h
             fold("xg", lambda k: ("Wz", S_(15 - k, 143 - k)))
             for j in range(4):
-                lin("gq", ("gq", j, w), (pa, a1), 0.25, 1536.0 - 0.375 + 0.25 * j)
+                sign = -1.0 if j else 1.0
+                lin("gq", ("gq", j, w), (pa, a1), 0.25 * sign, (1536.0 - 0.375 + 0.25 * j) * sign)
             tests = grp((pc, a0), [(("Fl", j, full), ("gq", j, w)) for j in range(4)])
             mm(tests[:3])
             mm(tests[3:])
-            dl = grp((pb, a0), [(k_(I3K), ("gq", 0, w))] + [(k_(IN4K), ("gq", j, w)) for j in (1, 2, 3)] +
-                     [(k_(ID), ("E16", w)), (k_(BE), ("wn", w))])
-            mm(dl[:5])
-            ts(("fg", w), (pc, a0), c_(THR), AL.is_gt)
+            dl = grp((pb, a0), [(("Dg", 2, full), ("gq", 0, w))] + [(ID, ("gq", j, w)) for j in (1, 2, 3)] +
+                     [(k_(BE), ("wn", w))])
+            mm(dl[:4])
+            sign = opt["sign"] >> h & 1
+            if sign:
+                vec("sgn", ("fg", w), [(pc, a0), c_(NTH)], (("fg", w), (pc, a0), c_(NTH)), "S")
+            else:
+                ts(("fg", w), (pc, a0), c_(THR), AL.is_gt)
             mm(grp((pa, a0), [(k_(LO), ("fg", w))]))
-            far = grp((pc, a0), [(k_(S3K), ("gq", 0, w))] + [(k_(SN4K), ("gq", j, w)) for j in (1, 2, 3)] +
+            far = grp((pc, a0), [(k_(S3K), ("gq", 0, w))] + [(k_(SH8), ("gq", j, w)) for j in (1, 2, 3)] +
                       [(k_(BE), ("wn", w))]) * (opt["far"][t] >> h & 1)
             if far:
                 mm(far[:4])
-            lin("wn", ("wn", w), (pa, a0), 1.0, 1.0, True)
-            mm(dl[5:] + far[4:])
-            if not pre:
-                ts(("eu", w), (pb, a0), 8.0, AL.add, 2056.0, AL.min)
-            tt(("sv", w, 0), ("E16", w), (pb, a0), AL.is_equal)
-            if opt["far"][t] >> h & 1:
-                ts(("sv", w, 1), (pc, a0), c_(NR8), AL.is_equal, c_(R82), AL.add)
+            if sign:
+                vec("lin", ("wn", w), [(pa, a0)], (("wn", w), (pa, a0), 0.5, -2.5, True), "S")
+            else:
+                lin("wn", ("wn", w), (pa, a0), 1.0, 1.0, True)
+            mm(dl[4:] + far[4:])
+            ts(("sv", w, 0), (pb, a0), 0.0, AL.is_equal)
+            if far:
+                ts(("sv", w, 1), (pc, a0), c_(R8H), AL.is_equal, c_(R82), AL.add)
             else:
                 mm(grp((pc, a0), [(k_(SH8), ("sv", w, 0))]))
                 lin("sx", ("sv", w, 1), (pc, a0), 1.0, c_(R82))
+            tag[2] = "maxima%d" % h
             ends = S_(o + 15, o + 16 * LH, 16)
             steps = []
             for j, (l0, c0) in enumerate(chunks):
@@ -458,147 +438,91 @@ def build(opt, rank):
                 if opt["ccp"][t] >> (2 * h + j) & 1:
                     vec("lin", ("cs", cw), [steps[j]], (("cs", cw), steps[j], 1.0, 0.0, False), "S")
                     steps[j] = ("cs", cw)
-                if pre:
-                    scan(("ms", cw), ("mg", cw), steps[j], -4 * STEP, AL.max, AL.add)
-                else:
-                    gather("gM", ("mg", cw), Mw, ("eu", S_(l0, l0 + 32)))
-                    scan(("ms", cw), ("rst", S_(0, 512)), ("mg", cw), 0.0, AL.mult, AL.max)
+                scan(("ms", cw), ("mg", cw), steps[j], -4 * STEP, AL.max, AL.add)
+                scan(("xs", cw), ("xg", cw), steps[j], -4 * STEP, AL.max, AL.add)
             if last:
-                lin("pk", ("ysb", real), ("ms", ends), 1.0, STEP * pre)
-            else:
-                pks["S"].append(lin("pk", leaving("S", t, h), ("ms", ends), 1.0, STEP * pre))
-                if (opt["sc"] == 2 or h) and not opt["cmb"]:
-                    send("S", t, [h] if opt["sc"] == 2 else [0, 1], pks["S"][-3 + opt["sc"]:])
-            for j, (l0, c0) in enumerate(chunks):
-                scan(("xs", S_(c0, c0 + 512)), ("xg", S_(c0, c0 + 512)), steps[j], -4 * STEP, AL.max, AL.add)
-            if last:
+                lin("pk", ("ysb", real), ("ms", ends), 1.0, STEP)
                 lin("pk", ("yzb", real), ("xs", ends), 1.0, STEP)
             else:
-                pks["z"].append(lin("pk", leaving("z", t, h), ("xs", ends), 1.0, c_(SC)))
-                if opt["cmb"]:
-                    send("c", t, [h], [pks["S"][-1], pks["z"][-1]])
-                elif opt["zc"] == 2 or h:
-                    send("z", t, [h] if opt["zc"] == 2 else [0, 1], pks["z"][-3 + opt["zc"]:])
-        tag[0] = -1
-        mm([x for h in range(NS) for x in grp(("p6", S_(LH * h, LH * h + LH)), [
-            (k_(BM), ("St", S_(256 + LH * h, 256 + LH * h + LH))), (k_(BM), zz[h]),
-            (k_(IN16), ("fl", par, S_(LH * h, LH * h + LH)))])])
-        scan(("ls", S_(256, 384)), ("p6", full), ("cd", full), -65536.0, AL.max, AL.add)
-        lin("lu", ("lu", S_(16, 24)), ("ls", S_(256 + 15, 384, 16)), 1.0, 16384.0)
+                send(t, h, [lin("pk", leaving(t, h, 16 + 16 * (own % 2)), ("ms", ends), 1.0, STEP),
+                            lin("pk", leaving(t, h, 48 * (own % 2)), ("xs", ends), 1.0, STEP)])
+        tag[0], tag[2] = -1, "columns"
+        up = S_(128, 256)
+        sva = ("sv", full, 0)
+        mm(cols[0] + cols[1])
+        scan(("ls", S_(256, 384)), (pl, full), ("cd", full), -65536.0, AL.max, AL.add)
+        lin("lu", ("lu", S_(16, 24)), ("ls", S_(256 + 15, 384, 16)), 1.0, 16384.0 + 24576.0)
         if last:
-            gather("o16", ("o16", full), Cw, ("lu", S_(16, 24)))
-            lin("cv", ("Ft", full), ("p6", full))
-            mm(grp(("p6", S_(128, 136)), [(("Ft", full), ("K", ID, S_(0, 128, 16)))]))
+            vec("ts", ("o16", full), [("ind", Cw, ("lu", S_(16, 24)))],
+                (("o16", full), ("ind", Cw, ("lu", S_(16, 24))), -1.0, None, AL.mult, None))
+            lin("cv", ("Ft", full), ("p6", full), 1.0, 24576.0)
+            mm(grp(("p6", S_(128, 136)), [(("Ft", full), ("Dg", 0, S_(0, 128, 16)))]))
             lin("cv", ("cT", S_(0, 8)), ("p6", S_(128, 136)), 1.0, c_(MB))
             for q in range(8):
                 ts(("OH", q, S_(0, 256)), ("J", S_(0, 256)), ("cT", S_(q, q + 1)), AL.is_equal, c_(M1), AL.mult)
-        fs = 1 if last else opt["fs"][t]
-        W = 128 // fs
-        for r in range(fs):
-            tag[0] = r if fs > 1 else -1
-            w = S_(W * r, W * r + W)
-            pf, pv = ("p%d" % (3 * r + 1),) * 2 if fs > 1 else ("p4", "p1")
-
-            def seg(j, base=0):
-                return S_(base + W * j, base + W * j + W)
-            svw = ("sv", w, 0)
-            v0 = 2 * W * r
-            vw = S_(v0, v0 + 2 * W)
-            mm(grp((pf, seg(0)), [(k_(SG), svw)]))
-            lin("Rl", ("Rl", w), (pf, seg(0)), 1.0, c_(LC), True)
-            ft = fs == 1
-            if opt["f32"]:
-                pl = grp((pv, seg(0)), [(k_(ID), ("E16", w)), (k_(T128), svw), (k_(I128), ("Rl", w))])
-                mm(pl[:2])
-                mm(pl[2:])
-                lin("V16", ("R32", 0, w), (pv, seg(0)))
-                if ft:
-                    mm([(("p7", full), ("o129", full), ("FC", full), True, False)] +
-                       [(("p7", full), ("o16", full), k_(IN1), False, False)] * last)
-                    fm = [(("p7", S_(0, 8), S_(max(p - 1, 0), p + 1)), ("R32", p, w),
-                           ("Sel32", S_(0, 8), S_(0 if p else 1, 2)), False, p == 15) for p in range(16)]
-                else:
-                    fm = grp((pf, seg(0)), [(("Fw32", S_(16 - p, 144 - p) if p else S_(144, 272)), ("R32", p, w))
-                                            for p in range(16)])
-                for p in range(16):
-                    if p:
-                        lin("Rr", ("R32", p, w), ("R32", 0, w), 1.0, -2048.0 * p, True)
-                    mm(fm[p:p + 1])
-            else:
-                lin("eh", ("eh", w), ("E16", w), 0.0078125, 1536.0 - 0.49609375)
-                pl = [(k_(T128), svw), (k_(I128), ("Rl", w))]
-                mm(grp((pv, seg(0)), [(k_(ID), ("E16", w)), (k_(IN128), ("eh", w))] + pl) +
-                   grp((pv, seg(1)), [(k_(ID), ("eh", w))] + pl))
-                lin("V16", ("V16", seg(0, v0)), (pv, seg(0)), 1.0, 196608.0)
-                lin("V16", ("V16", seg(1, v0)), (pv, seg(1)), 1.0, -1536.0)
-                if ft:
-                    mm([(("p7", full), ("o129", full), ("FC", full), True, False)] +
-                       [(("p7", full), ("o16", full), k_(IN1), False, False)] * last)
-                    fm = [(("p7", S_(0, 8), S_(max(p - 1, 0), p + 1)), ("Rr", p - 1, seg(v)) if p else ("V16", seg(v)),
-                           ("Sel", v, S_(0, 8), S_(0 if p else 1, 2)), False, p == 15 and v == 1)
-                          for p in range(16) for v in range(2)]
-                else:
-                    fm = grp((pf, seg(0)), [(("Fw", v, S_(16 - p, 144 - p) if p else S_(144, 272)),
-                                             ("Rr", p - 1, seg(v, v0)) if p else ("V16", seg(v, v0)))
-                                            for p in range(16) for v in range(2)])
-                for p in range(16):
-                    if p:
-                        lin("Rr", ("Rr", p - 1, vw), ("V16", vw), 1.0, -128.0 * p, True)
-                    if p % 2:
-                        mm(fm[2 * p - 2:2 * p + 2])
-            if last:
-                break
-            if ft:
-                lin("Ft", ("Ft", full), ("p7", full))
-                mm(grp(("p7", S_(128, 256)), [(("Ft", full), k_(ID))]))
-                lin("Ff", ("Ff", w), ("p7", S_(128, 256)))
-            else:
-                lin("Ff", ("Ff", w), (pf, seg(0)), 1.0, c_(FB))
-            cp(("ind", Cw, ("lu", S_(16 + W * r // 16, 16 + W * (r + 1) // 16))), ("Ff", w))
-        tag[0] = -1
-        up = S_(128, 256)
-        mm(grp(("p6", full), [(k_(ID), ("kh", full)), (k_(ZF), ("sv", full, 0))]) +
-           grp(("p6", up), [(k_(ID), ("kh", up)), (k_(ZF), ("sv", full, 0))]))
+        tag[2] = "F"
+        mm(grp(("p1", full), [(k_(SG), sva)]) + grp(("p1", up), [(ID, ("E16", full)), (k_(T2K), sva)]))
+        lin("Rl", ("R32", 1, full), ("p1", full), 1.0, c_(L2K), True)
+        tt(("R32", 0, full), ("R32", 1, full), ("p1", up), AL.add)
+        mm([(("p4", full), ("one", full), ("FC", full), True, False)] + [(("p4", full), ("o16", full), ID, False, False)] * last)
+        for p in range(16):
+            if p:
+                lin("Rr", ("R32", p, full), ("R32", 0, full), 1.0, -2048.0 * p, True)
+            mm([(("p4", S_(0, 8), S_(max(p - 1, 0), p + 1)), ("R32", p, full), ("Sel", S_(0, 8), S_(0 if p else 1, 2)),
+                 False, p == 15)])
+        if not last:
+            lin("Ft", ("Ft", full), ("p4", full))
+            mm(grp(("p1", full), [(("Ft", full), ID)]))
+            lin("Ff", ("Ff", full), ("p1", full))
+            cp(("ind", Cw, ("lu", S_(16, 24))), ("Ff", full))
+        tag[2] = "first"
+        mm(grp(("p6", full), [(ID, ("kh", full)), (k_(ZF), sva)]) + grp(("p6", up), [(ID, ("kh", up)), (k_(ZF), sva)]))
         lin("sel", ("sel", S_(0, 256)), ("p6", S_(0, 256)), 1.0, -1600.0, True)
-        mm(grp(("p6", full), [(k_(BM), ("St", full)), (k_(BM), ("sel", full))]) +
-           grp(("p6", up), [(k_(BM), ("St", up)), (k_(BM128), ("sel", up))]))
+        mm(grp(("p6", full), [(k_(B32), ("St", full)), (k_(BM), ("sel", full))]) +
+           grp(("p6", up), [(k_(B32), ("St", up)), (k_(BM128), ("sel", up))]))
         scan(("ls", S_(0, 256)), ("p6", S_(0, 256)), ("cd", S_(0, 256)), -65536.0, AL.max, AL.add)
         if last:
             lin("mi", ("mi", full), ("p6", up), 1.0 / 256, 1.0 - 127.5 / 256)
         lin("lu", ("lu", S_(0, 16)), ("ls", S_(15, 256, 16)), 1.0, 16384.0)
-        tt(("xa", full), ("ind", ("xg", S_(0, 2048)), ("lu", S_(0, 8))), ("xs", S_(15, 2048, 16)), AL.add)
-        lin("xh", ("xh", full), ("xa", full), 0.5, STEP / 2 - 0.25)
+        if opt["xa"][t]:
+            gather("xf", ("xf", full), ("xg", S_(0, 2048)), ("lu", S_(0, 8)))
+            mm(grp(("p6", full), [(ID, ("xf", full)), (ID, ("xs", S_(15, 2048, 16)))]))
+            lin("xh", ("xh", full), ("p6", full), 0.5, STEP / 2 - 0.25)
+        else:
+            tt(("xa", full), ("ind", ("xg", S_(0, 2048)), ("lu", S_(0, 8))), ("xs", S_(15, 2048, 16)), AL.add)
+            lin("xh", ("xh", full), ("xa", full), 0.5, STEP / 2 - 0.25)
         if not last:
             cp(("ind", Xw, ("lu", S_(8, 16))), ("xh", full))
         else:
             lc = ("lc", S_(0, 8))
             yw = ("yxb", S_(0, 256))
-            lin("mi", ("mp", full), ("mi", full))
+            copy("mp", ("mp", full), ("mi", full))
             lin("mi", ("li", S_(0, 8)), ("ls", S_(128 + 15, 256, 16)), 1.0, 16384.0)
             ts(("li", S_(8, 16)), ("li", S_(0, 8)), 255, AL.bitwise_and)
-            lin("mi", lc, ("li", S_(8, 16)))
+            copy("lc", lc, ("li", S_(8, 16)))
             tt(("old", full), ("ind", Xw, ("lu", S_(8, 16))), ("mp", full), AL.mult)
             tt(("adj", full), ("ind", yw, lc), ("old", full), AL.subtract)
             tt(("vv", full), ("xh", full), ("mp", full), AL.mult)
             tt(("ind", yw, lc), ("vv", full), ("adj", full), AL.add)
         if not last:
-            mm(grp(("p6", full), [(k_(BM), ("sv", full, 0))]))
-            vec("acc", ("junk", full), [("p6", full)], (("junk", full), ("p6", full), c_(AC)), "S", [c_(AC)])
-            lin("A", ("Ab", S_(0, LH)), ("one", S_(0, LH)), c_(AC))
+            more = S_(0, 129)
+            mm(grp(("p6", more), [(k_(BM), ("sv", more, 0))]))
+            vec("acc", ("junk", more), [("p6", more)], (("junk", more), ("p6", more), c_(AC)), "S", [c_(AC)])
         else:
-            lin("Fz", ("Fz", S_(0, 72, 9), S_(0, 16)), ("p7", full))
-            fin = grp(("p4", S_(0, 256)), [(("Fz", S_(8 * q, 8 * q + 8), S_(0, 16)), ("OH", q, S_(0, 256))) for q in range(8)])
+            tag[2] = "F"
+            lin("Fz", ("Fz", S_(0, 72, 9), S_(0, 16)), ("p4", full))
+            fin = grp(("p1", S_(0, 256)), [(("Fz", S_(8 * q, 8 * q + 8), S_(0, 16)), ("OH", q, S_(0, 256))) for q in range(8)])
             mm(fin)
-            tt(("ycb", S_(0, 256)), ("yc0", S_(0, 256)), ("p4", S_(0, 256)), AL.add)
+            tt(("ycb", S_(0, 256)), ("yc0", S_(0, 256)), ("p1", S_(0, 256)), AL.add)
     for (y, src) in (("ys", ("ysb", full)), ("yz", ("yzb", full)), ("yx", ("yxb", S_(0, 256))), ("yc", ("ycb", S_(0, 256)))):
-        add("Y", "st", (y, src), [src], [], 131072, "dma")
+        add("S" if y == "yc" else "Y", "st", (y, src), [src], [], 131072, "dma")
     return ops
 
 
 def cost(op, eng, pr):
     r, n = op["rate"], op["n"]
     if r == "dma":
-        return n / pr["bw"], pr["dma"]
+        return (n / pr["bw"], pr["dma"]) if eng == "Y" else (100.0, n / pr["bw"] + pr["dma"])
     if r == "snd":
         return pr["snd"] + n * pr["trf"], 0.0
     if r == "xch":
@@ -614,7 +538,7 @@ def cost(op, eng, pr):
     return pr["fix"] + max(64.0, n * r) * pr["cyc"], 0.0
 
 
-def schedule(ops, opt, pr):
+def schedule(ops, opt, pr, start=None):
     n = len(ops)
     lat = pr["lat"]
     pred = [[(d, d in o["deps"]) for d in sorted(o["deps"] | o["bank"])] for o in ops]
@@ -676,18 +600,26 @@ def schedule(ops, opt, pr):
     key = [0.0] * n
     for i in range(n - 1, -1, -1):
         key[i] = min([key[j] for j, _ in succ[i]] + [0.0]) - sum(tab[i][ops[i]["eng"][0]]) - lat
-    kinds = {}
+    kinds, parts = {}, {}
     for i, o in enumerate(ops):
         kinds.setdefault(o["key"], []).append(i)
-    kinds = list(kinds.values())
+        parts.setdefault(o["part"], []).append(i)
+        parts.setdefault((o["part"], o["level"]), []).append(i)
+    kinds, parts = list(kinds.values()), list(parts.values())
     rng = np.random.RandomState(opt["seed"])
     bias = [1.4] * n
+    if start:
+        key, bias = start[2], [0.05 if e == "V" else 20.0 for e in start[1]]
     best = cur = passes(key, bias, 2)
     for it in range(opt["it"]):
         key = [cur[3][i] - tab[i][cur[2][i]][0] for i in range(n)]
         b2 = list(bias)
         u = rng.rand()
-        if u < 0.4:
+        if u < opt["parts"]:
+            d = float(rng.randn()) * 600.0
+            for i in parts[rng.randint(len(parts))]:
+                key[i] += d
+        elif u < 0.4:
             for _ in range(rng.randint(1, 4)):
                 d = float(rng.randn()) * 1200.0
                 for i in kinds[rng.randint(len(kinds))]:
@@ -735,16 +667,13 @@ def polish(ops, order, where, opt, prs):
             a, b = tab[i][e]
             free[e] = end[i] = st + a
             fin[i] = st + a + b + lat
-        return max(fin) - lat
+        return max(fin) - lat + opt["marks"] * sum(fin[i] for i in marks)
 
-    def held(seq, where, s, end, fin):
-        last, before = {}, [None] * n
-        for i in seq:
-            before[i] = last.get(where[i])
-            last[where[i]] = i
-        i = fin.index(max(fin))
+    marks = [i for i, o in enumerate(ops) if o["kind"] in ("arr", "st") or o["rate"] == "sc"]
+
+    def held(before, where, s, end, fin, i):
         pairs = []
-        while i is not None:
+        while i is not None and len(pairs) < opt["reach"]:
             e, nxt = where[i], None
             for d, hard in pred[i]:
                 if (end[d] if where[d] == e and (e == "P" or not hard) else fin[d]) > end[i] - tabs[s][i][e][0] - 1e-6:
@@ -764,28 +693,41 @@ def polish(ops, order, where, opt, prs):
                 pos[e] += 1
     ends, fins = [[0.0] * n for _ in prs], [[0.0] * n for _ in prs]
     base = [run(seq, where, s, 0, ends[s], fins[s]) for s in range(ns)]
-    weight = [base[0] / b / ns for b in base]
-    cur, fresh = base[0], True
-    best = (cur, seq, where)
+    fresh = True
+    weight = [1.0 / ns, prs[0]["cyc"] / prs[-1]["cyc"] / ns][:ns]
+    cur = sum(w * b for w, b in zip(weight, base))
+    best = (cur, seq, where, ends[0])
     rng = np.random.RandomState(opt["seed"])
     at = [0] * n
     for it in range(opt["moves"]):
         if fresh:
             seq = sorted(seq, key=lambda i: ends[0][i] - tabs[0][i][where[i]][0])
+            last, before, pairs = {}, [None] * n, {}
             for p, i in enumerate(seq):
                 at[i] = p
-            pairs = [held(seq, where, s, ends[s], fins[s]) for s in range(ns)]
+                before[i] = last.get(where[i])
+                last[where[i]] = i
             fresh = False
-        some = pairs[rng.randint(ns)]
-        u, v = some[rng.randint(len(some))]
+        x = (rng.randint(ns), marks[rng.randint(len(marks))])
+        if x not in pairs:
+            pairs[x] = held(before, where, x[0], ends[x[0]], fins[x[0]], x[1])
+        if not pairs[x]:
+            continue
+        u, v = pairs[x][rng.randint(len(pairs[x]))]
         r = rng.rand()
         s2, w2 = list(seq), where
-        if r < 0.4:
+        if r < 0.3:
             p0 = max([at[u] - (rng.randint(12) if rng.rand() < 0.3 else 0)] + [at[d] + 1 for d, _ in pred[v]])
             if p0 > at[u]:
                 continue
             s2.insert(p0, s2.pop(at[v]))
-        elif r < 0.75:
+        elif r < 0.55:
+            lo = max([at[u] - 80, 0] + [at[d] + 1 for d, _ in pred[u]])
+            if lo >= at[u]:
+                continue
+            p0 = rng.randint(lo, at[u])
+            s2.insert(p0, s2.pop(at[u]))
+        elif r < 0.8:
             p = min([at[v] + 1 + (rng.randint(25) if rng.rand() < 0.5 else 0), n] + [at[d] for d in succ[u]])
             if p <= at[v]:
                 continue
@@ -802,8 +744,18 @@ def polish(ops, order, where, opt, prs):
         c = sum(weight[s] * run(s2, w2, s, p0, e2[s], f2[s]) for s in range(ns))
         if c <= cur - 50.0 * 0.16 ** (it / opt["moves"]) * math.log(1.0 - rng.rand()):
             cur, seq, where, ends, fins, fresh = c, s2, w2, e2, f2, True
-            best = (c, seq, where) if c < best[0] else best
-    return {e: [i for i in best[1] if best[2][i] == e] for e in order}, best[2]
+            best = (c, seq, where, ends[0]) if c < best[0] else best
+    return ({e: [i for i in best[1] if best[2][i] == e] for e in order}, best[2],
+            [best[3][i] - tabs[0][i][best[2][i]][0] for i in range(n)], best[0])
+
+
+def plan(ops, opt, prs):
+    best = cur = None
+    for r in range(opt["rounds"]):
+        o = dict(opt, seed=opt["seed"] + 1000 * r)
+        cur = polish(ops, *schedule(ops, o, prs[0], cur), o, prs)
+        best = cur if best is None or cur[3] < best[3] else best
+    return best[:2]
 
 
 PLAN = []
@@ -815,7 +767,7 @@ def rank_program(g, core, T, topo):
         return
     ops = build(OPT, rank)
     if not PLAN:
-        PLAN.extend(polish(ops, *schedule(ops, OPT, PAR0), OPT, [PAR0, PAR1]))
+        PLAN.extend(plan(ops, OPT, [PAR0, PAR1]))
     order, where = PLAN
     queue = {"V": g.vector, "S": g.scalar, "P": g.tensor, "G": g, "Y": g.sync}
 
@@ -824,7 +776,7 @@ def rank_program(g, core, T, topo):
             return x
         if x[0] == "ind":
             return ap(x[1]).indirect(ap(x[2]))
-        if len(x) == 2 and x[0] == "p7":
+        if len(x) == 2 and x[0] == "p4":
             return T[x[0]][:, x[1].start // 16:x[1].stop // 16, :]
         return T[x[0]][(slice(None),) + x[1:]]
 
@@ -836,16 +788,17 @@ def rank_program(g, core, T, topo):
     for e in "VSPG":
         n = 0
         for i in order[e]:
-            if i in needed:
+            if i in needed and ops[i]["rate"] != "dma":
                 n += 1
                 signal[i] = ("q" + e, n)
         total["q" + e] = n
-    for i in order["Y"]:
+    for i in order["Y"] + order["S"]:
         if ops[i]["kind"] == "ld":
             signal[i] = ("ld%d" % ops[i]["args"][2], 16)
+    per = min(len(topo.engines(core, c)) for c in T.cores if c != core) // NB
     for i in order["R"]:
         a = ops[i]["args"]
-        signal[i] = ("arr%d" % a[0], a[2] * len(a[1]))
+        signal[i] = ("arr%d" % a[0], per * len(a[1]))
     left = 0
     for e in "YGPSV":
         q = queue[e]
@@ -879,6 +832,8 @@ def rank_program(g, core, T, topo):
                 ins = q.tensor_scalar(ap(a[0]), ap(a[1]), ap(a[2]), ap(a[3]), a[4], a[5])
             elif k == "scan":
                 ins = q.tensor_tensor_scan(ap(a[0]), ap(a[1]), ap(a[2]), a[3], a[4], a[5])
+            elif k == "sgn":
+                ins = q.activation(ap(a[0]), ap(a[1]), AF.Sign, ap(a[2]))
             elif k == "ms":
                 ins = q.memset(ap(a[0]), a[1])
             elif k == "acc":
@@ -900,12 +855,12 @@ def rank_program(g, core, T, topo):
                 tr = []
                 for j, (b, src, dst) in enumerate(a[1]):
                     rid, pid, _ = topo.addr(T.cores[b])
-                    mask = sum(1 << x for x in topo.engines(core, T.cores[b])[a[2] * j:a[2] * (j + 1)])
+                    mask = sum(1 << x for x in topo.engines(core, T.cores[b])[per * j:per * (j + 1)])
                     tr.append(RemoteDMATransfer(dst_ids=[DstId(rid=rid, pnc=pid)], dma_engine_mask=mask,
                                                 remote_sem=T.sem["arr%d" % a[0]], src=ap(src), dst=ap(dst)))
                 q.remote_dma_fused(tr, local_sem=T.sem.left)
-                left += a[2] * len(tr)
-            if i in signal and e != "Y":
+                left += per * len(tr)
+            if i in signal and k != "ld":
                 ins.then_inc(T.sem[signal[i][0]], 1)
         if e == "Y":
             q.wait_ge(T.sem.stored, 64)

import math
import numpy as np
from concourse.bass import DstId, RemoteDMATransfer
from concourse.mybir import AluOpType, ActivationFunctionType

AL = AluOpType
AF = ActivationFunctionType
RO, NS = 4, 2
LH = 128 // NS
NB = 8 // NS
STEP = 2048.0
F16, BF, F32, I32, U16 = "float16", "bfloat16", "float32", "int32", "uint16"


def sb(n, d):
    return ("sbuf", [128] + (n if isinstance(n, list) else [n]), d)


SCRATCH = {
    "s0b": sb(128, I32), "z0b": sb(128, BF), "cmb": sb(2048, I32), "X": sb(8192, BF),
    "C": sb(2048, I32), "M": sb(2048, I32),
    "DJ": sb(160, BF), "BI": sb(128, BF), "CcM": sb(128, BF), "ki": sb(8, I32), "ia": sb(17, F32), "t5": sb(5, F32),
    "St": sb(384, BF), "cd": sb(256, BF), "col": sb(32, F32), "R": sb(17, F32), "Rd": sb(16, F32),
    "tny": sb(64, F32), "Z": sb(2064, BF), "Wz": sb(144, BF), "Sel": sb([8, 2], F32), "FC": sb(128, BF),
    "K": sb([18, 128], F16), "CN": sb(128, BF), "I32": sb(128, F32), "Cy": sb([8, 32], F16), "Dm": sb([8, 128], F16),
    "Om": sb([8, 128], F16), "Cm": sb([8, 128], BF), "Fl": sb([4, 128], F16), "Bj": sb([4, 128], F16),
    "Dg": sb([32, 128], BF), "one": sb(128, BF), "J": sb(256, BF),
    "mc": sb([36, 2, 64], U16), "Sl": sb(128, U16), "zf": sb([8, 16], F16), "xf": sb(128, BF),
    "fl": sb([2, 128], F16), "G": sb(2048, F16), "E16": sb(128, F16),
    "Pp": sb(128, F32), "eq": sb(1024, F16), "Qm": sb(128, F32), "hr": sb(128, BF),
    "OH": sb([8, 256], F16), "cT": sb(8, F32), "o16": sb(128, F16), "Ft": sb(128, F16),
    "R32": sb([16, 128], F32), "Fz": sb([72, 16], F16), "yc0": sb(256, F32),
    "hu": sb(128, U16), "kh": sb(256, F16), "xg": sb(2048, BF), "gq": sb([4, 128], F16), "fg": sb(128, F16),
    "wn": sb(128, F16), "sv": sb([129, 2], F16), "eu": sb(128, U16), "mg": sb(2048, F16), "ms": sb(2048, F16),
    "xs": sb(2048, F16),
    "Ff": sb(128, F32), "sel": sb(256, F16), "ls": sb(384, F32), "lu": sb(24, U16), "junk": sb(129, F32),
    "xa": sb(128, F32), "xh": sb(128, I32), "cs": sb(2048, BF),
    "yxb": sb(256, F32), "ycb": sb(256, F32), "ysb": sb(128, F32), "yzb": sb(128, BF), "C16": sb(2048, F16),
    "mi": sb(128, I32), "mp": sb(128, F32), "li": sb(16, I32), "lc": sb(8, U16), "old": sb(128, F32),
    "adj": sb(128, F32), "vv": sb(128, F32),
}
for _b in range(8):
    SCRATCH["p%d" % _b] = ("psum", [128, 512] if _b != 4 else [128, 32, 16], F32)
SEMAPHORES = ["qV", "qS", "qP", "qG", "left", "stored"] + ["ld%d" % s for s in range(8)] + \
    ["arr%d" % s for s in range(NS * (RO - 1))]

LC, CC, CP, PAR, WW, DG, NDG, THR, CQ, W8, AC, L15B, M1, MB, L2K, R82, R8H, NTH = range(18)
BM, DMB, DMN, B2K, T2K, SG, ZF, BM128, LO, BE, TMP, TM2, TM3, B32, B512, S3K, SH8 = range(17)

PAR0 = {"cyc": 0.87, "fix": 40.0, "g": 1.56, "sc": 3.8, "pe": 0.5, "lat": 170.0, "xch": 100.0, "row": 40.0,
        "snd": 600.0, "trf": 45.0, "bw": 400.0, "dma": 1000.0, "sfix": 30.0}
PAR1 = dict(PAR0, cyc=1.1, g=1.9, pe=0.58, sc=4.5, snd=1200.0, trf=80.0, xch=800.0, lat=220.0, dma=1800.0)
OPT = {"seed": 0, "it": 600, "moves": 4000, "slack": 60.0, "ccp": [1, 1, 1, 5], "far": [3, 3, 3, 3],
       "marks": 0.03, "reach": 60, "sign": 0, "xa": [0, 0, 0, 0], "rounds": 9, "parts": 0.1,
       "pieces": [0, 576, 1152, 1728, 2048],
       "gp": 32, "cut": 4, "gp_copies": ("eu", "z16", "mp", "lc", "cd"), "eng": {"gM": "S"}}


def S_(a, b, c=None):
    return slice(a, b, c)


def build(opt, rank):
    ops = []
    acc = {}
    tag = [-1, -1, "constants"]
    half, own = rank // NB, rank % NB

    def span(a):
        if len(a) == 2 and a[0] == "p4":
            return 0, a[1].start, a[1].stop - a[1].start
        shp = SCRATCH[a[0]][1][1:]
        ix = np.arange(int(np.prod(shp))).reshape(shp)[a[1:]].ravel().tolist()
        if ix[-1] - ix[0] + 1 == len(ix):
            return ((1 << len(ix)) - 1) << ix[0], ix[0], len(ix)
        return sum(1 << j for j in ix), ix[0], len(ix)

    def two(a):
        return SCRATCH[a[0]][2] in (F16, BF, U16)

    def add(eng, kind, args, rd, wr, n, rate, extra=()):
        me = len(ops)
        deps = set(extra)
        bank = set()
        for lst, w in ((rd, False), (wr, True)):
            for a in lst:
                if SCRATCH[a[0]][0] == "psum":
                    last = acc.setdefault(a[0], {})
                    for e in list(last):
                        if (e == "P") != (eng == "P"):
                            deps.add(last[e])
                        else:
                            bank.add(last[e])
                    if eng == "P":
                        last.clear()
                    last[eng if eng in ("P", "V", "S") else me] = me
                    continue
                mine = span(a)[0]
                rec = acc.setdefault(a[0], [])
                for (o, its, w2) in rec:
                    if (w or w2) and its & mine:
                        deps.add(o)
                if w:
                    rec[:] = [r for r in rec if r[1] & ~mine]
                rec.append((me, mine, w))
        deps.discard(me)
        bank.discard(me)
        ops.append({"eng": eng, "kind": kind, "args": args, "deps": deps, "bank": bank - deps, "n": n, "rate": rate,
                    "level": tag[1], "part": tag[2], "key": kind + (wr[0][0] if wr else "") + str(tag[0])})
        return me

    def vec(kind, out, ins, args, eng="V", more=()):
        full = [x for x in ins if isinstance(x, tuple)]
        rd = [p for x in full for p in ([x[1], x[2]] if x[0] == "ind" else [x])]
        if out[0] == "ind":
            return add(eng, kind, args, rd + [out[2]], [out[1]], 16 * span(out[2])[2], "sc")
        if ins[0][0] == "ind":
            rate = "g"
        elif kind == "tt":
            rate = 2.0 if all(SCRATCH[x[0]][0] == "sbuf" for x in full) else 1.0
        else:
            rate = 0.5 if all(two(x) for x in [out] + [x for x in full if span(x)[2] > 1]) else 1.0
        return add(eng, kind, args, rd, [out] + list(more), span(out)[2], rate)

    def cp(out, i):
        return vec("cp", out, [i], (out, i))

    def tt(out, a, b, op):
        return vec("tt", out, [a, b], (out, a, b, op))

    def ts(out, a, s1, op0, s2=None, op1=None):
        return vec("ts", out, [a, s1, s2], (out, a, s1, s2, op0, op1))

    def scan(out, a, b, init, op0, op1):
        return vec("scan", out, [a, b], (out, a, b, init, op0, op1))

    def ms(out, v):
        return add("V", "ms", (out, v), [], [out], span(out)[2], 0.5 if two(out) else 1.0)

    def lin(name, out, a, mul=1.0, addc=0.0, relu=False):
        return vec("lin", out, [a, mul, addc], (out, a, mul, addc, relu), opt["eng"].get(name, "VS"))

    def gather(name, out, win, off):
        return add(opt["eng"].get(name, "VS"), "gat", (out, ("ind", win, off)), [win, off], [out], span(out)[2], "g")

    def mm(lst):
        n = sum(max(64, span(m[2])[2]) * (1 if two(m[2]) else 4) for m in lst)
        return add("P", "mm", lst, [x for m in lst for x in (m[1], m[2])], [m[0] for m in lst], n, "pe")

    def grp(out, pairs):
        return [(out, l, r, j == 0, j == len(pairs) - 1) for j, (l, r) in enumerate(pairs)]

    def iota(out, pat, base, cm):
        return add("G", "iota", (out, pat, base, cm), [], [out], span(out)[2], "gp")

    def put(out, src, pat, base, fill):
        return add("G", "sel", (out, src, pat, AL.not_equal, fill, base, 1), [src], [out], span(out)[2], "gp")

    def copy(name, out, src):
        if name in opt["gp_copies"]:
            return put(out, src, [[0, span(out)[2]]], 1, 0.0)
        return lin(name, out, src)

    def after(op, *deps):
        ops[op]["deps"].update(d for d in deps if d is not None)
        return op

    def c_(j):
        return ("col", S_(j, j + 1))

    def k_(j):
        return ("K", j, S_(0, 128))

    def y_(a, b):
        return ("tny", S_(a, b))

    def load(q, j, dst, src, nbytes):
        me = add(q, "ld", (dst, src, j), [], [dst], nbytes, "dma")
        if j and q == "Y":
            ops[me]["bank"].add(me - 1)

    full = S_(0, 128)
    quarters = [S_(512 * j, 512 * j + 512) for j in range(4)]
    pieces = [S_(a, b) for a, b in zip(opt["pieces"], opt["pieces"][1:])]
    for j, w in enumerate(pieces):
        load("Y", j, ("cmb", w), ("cm", w), 512 * (w.stop - w.start))
    load("Y", 4, ("X", S_(0, 8192)), ("x0", S_(0, 8192)), 2097152)
    load("S", 5, ("s0b", full), ("s0", full), 65536)
    load("S", 6, ("z0b", full), ("z0", full), 32768)

    DJ = ("DJ", S_(0, 160)); D0 = ("DJ", full)
    R0 = ("R", S_(0, 1))
    iota(("ki", S_(0, 1)), [[0, 1]], 0, 1)
    iota(("ia", S_(0, 17)), [[1, 17]], 0, 0)
    iota(DJ, [[1, 160]], 0, -1)
    iota(("BI", full), [[-16, 8], [0, 16]], 0, 1)
    iota(("t5", S_(0, 5)), [[-1, 5]], 4, 0)
    iota(("CcM", full), [[0, 8], [1, 4], [0, 4]], 0, 0)
    turn = LH * (1 - 2 * half)
    iota(("St", full), [[32, 128]], 0, 0)
    iota(("St", S_(128, 256)), [[2 * turn, NS], [2, LH]], 2 * LH * half, 0)
    iota(("St", S_(256, 384)), [[32 * turn, NS], [32, LH]], 32 * LH * half, 0)
    ms(("Z", S_(0, 1040)), 0.0)
    lin("k", ("Z", S_(1040, 2064)), ("Z", S_(0, 1024)))
    for k in (0, 4):
        a = ("Cm", S_(k, k + 4), full)
        put(a, ("Z", S_(0, 512)), [[-1, 4], [-16, 8], [0, 16]], -k, STEP)
        put(a, a, [[-1, 4], [-16, 8], [0, 16]], -k - 1, -STEP)
    put(("Z", S_(16, 2064, 16)), ("Z", S_(16, 2064, 16)), [[-1, 16], [-16, 8]], 0, 1.0)

    def diag(out, v):
        add("G", "sel", (out, ("DJ", S_(v, v + 128)), [[-1, 128]], AL.is_equal, 0.0, 0, 1), [DJ], [out], 128, "gp")
    for m in range(32):
        diag(("Dg", m, full), m + 1)
    diag(("I32", full), 1)
    ID = ("Dg", 0, full)
    ki = ("ki", S_(0, 1))
    ts(("ki", S_(4, 5)), ki, 15, AL.bitwise_and)
    ts(("ki", S_(5, 6)), ki, 2, AL.logical_shift_right, 3, AL.bitwise_and)
    ts(("ki", S_(6, 7)), ki, 3, AL.bitwise_and)
    ts(("ki", S_(7, 8)), ki, 1, AL.bitwise_and)
    cp(("col", S_(0, 4)), ("ki", S_(4, 8)))
    ts(("R", S_(0, 17)), ("ia", S_(0, 17)), c_(LC), AL.is_equal)
    for j, src, mul, addc in ((L15B, LC, -1.0, 15.0), (WW, PAR, -2.0, 1.0), (CQ, CC, 0.25, 0.0), (L2K, LC, 2048.0, 0.0)):
        lin("k", c_(j), c_(src), mul, addc)
    ts(k_(BM), ("BI", full), c_(LC), AL.is_equal)
    lin("k", k_(TMP), k_(BM), -1024.0, 1024.0)
    tt(k_(DMB), D0, k_(TMP), AL.add)
    for j, v in ((S3K, 3.0),) * (max(opt["far"]) > 0) + ((SH8, 1.0),):
        ts(k_(j), k_(DMB), -8.0, AL.is_equal, v, AL.mult)
    lin("k", c_(R82), ("R", S_(8, 9)), 2.0)
    lin("k", c_(R8H), ("R", S_(8, 9)), 0.5)
    for rep in range(2):
        lin("k", ("Cy", S_(0, 8), S_(16 * rep, 16 * rep + 16)), ID, -1.0)
    for j in range(2):
        pk = "p%d" % (6 + j)
        mm([x for d in range(4) for x in grp((pk, S_(128 * d, 128 * d + 128)), [
            (ID, ID), (ID, ("Cy", S_(0, 8), S_(4 * j + d + 1, 4 * j + d + 17)))])])
        lin("k", ("Dm", S_(4 * j, 4 * j + 4), full), (pk, S_(0, 512)))
    ts(y_(0, 8), ("ia", S_(1, 9)), c_(LC), AL.add, 16.0, AL.is_lt)
    tt(y_(8, 16), y_(0, 8), ("ia", S_(1, 9)), AL.mult)
    lin("k", c_(W8), y_(7, 8), 613.0)
    for d in range(1, 9):
        ts(("Om", d - 1, full), k_(DMB), y_(7 + d, 8 + d), AL.is_equal, 613.0 if d < 8 else c_(W8), AL.mult)
    ts(("Wz", S_(0, 144)), ("DJ", S_(0, 144)), c_(L15B), AL.is_equal, c_(WW), AL.mult)
    lin("k", k_(BM128), k_(BM), 128.0)
    lin("k", k_(BE), k_(BM), c_(CQ))
    ms(("t5", S_(0, 1)), 0.0)
    ts(y_(16, 21), ("t5", S_(0, 5)), c_(CC), AL.is_equal)
    ts(y_(21, 26), ("t5", S_(0, 5)), c_(CP), AL.is_equal)
    tt(c_(DG), c_(CC), c_(CP), AL.is_equal)
    lin("k", c_(NDG), c_(DG), -7.0, -1.0)
    tt(y_(26, 30), y_(16, 20), y_(17, 21), AL.subtract)
    tt(y_(30, 34), y_(21, 25), y_(22, 26), AL.subtract)
    tt(y_(34, 38), y_(26, 30), y_(30, 34), AL.subtract)
    ts(y_(38, 42), y_(26, 30), c_(DG), AL.mult, -0.25, AL.mult)
    tt(y_(42, 46), y_(34, 38), y_(38, 42), AL.add)
    for j in range(4):
        ts(("Bj", j, full), ID, y_(42 + j, 43 + j), AL.mult, -4.0 if j else 4.0, AL.mult)
    mm([(("p6", S_(128 * j, 128 * j + 128)), k_(BM), ("Bj", j, full), True, True) for j in range(4)])
    lin("k", ("Fl", S_(0, 4), full), ("p6", S_(0, 512)))
    tt(y_(46, 47), y_(21, 22), y_(16, 17), AL.subtract)
    ts(y_(47, 48), y_(46, 47), 64.0, AL.mult, c_(CP), AL.add)
    lin("k", y_(48, 49), y_(16, 17), 16.0, -0.5)
    ts(y_(49, 50), y_(48, 49), c_(DG), AL.mult, c_(CC), AL.subtract)
    lin("k", c_(THR), y_(47, 48), 1.0, y_(49, 50))
    if opt["sign"]:
        lin("k", c_(NTH), c_(THR), -1.0)
    ts(k_(TM2), ("CcM", full), c_(CC), AL.is_equal, c_(NDG), AL.mult)
    lin("k", k_(TM3), k_(TM2), 1.0, c_(DG))
    tt(k_(LO), k_(TM3), k_(BM), AL.mult)
    tt(("Rd", S_(0, 16)), ("R", S_(0, 16)), ("R", S_(1, 17)), AL.subtract)
    iota(("one", full), [[0, 128]], 1, 0)
    lin("k", ("cd", S_(0, 16)), ("Rd", S_(0, 16)), 16384.0)
    lin("k", ("cd", S_(15, 16)), ("Rd", S_(15, 16)), 16384.0, -32768.0)
    for a in (16, 32, 64, 128):
        copy("cd", ("cd", S_(a, 2 * a)), ("cd", S_(0, a)))

    def beside(out, src, sign):
        return add("G", "sel", (out, src, [[-sign, 128]], AL.is_gt, 0.0, 0, sign), [src], [out], 128, "gp")
    lin("k", k_(B2K), k_(BM), 2048.0)
    beside(k_(DMN), k_(B2K), 1)
    put(k_(DMN), k_(DMN), [[-1, 128]], 0, -31.0 * 2048)
    beside(k_(T2K), k_(B2K), -1)
    tt(k_(SG), k_(DMN), k_(T2K), AL.subtract)
    lin("k", k_(ZF), k_(T2K), -1.0 / 32)
    put(k_(ZF), k_(ZF), [[-1, 128]], 0, 64.0)
    iota(("FC", full), [[0, 8], [16, 16]], -240, 0)
    for j in range(2):
        lin("k", ("Sel", S_(0, 8), j), ("K", BM, S_(0, 128, 16)), 2.0 * j - 1.0)
    iota(("J", S_(0, 256)), [[1, 256]], 0, 0)
    iota(("ki", S_(1, 2)), [[0, 1]], LH * half, 1)
    ts(("ki", S_(2, 3)), ("ki", S_(1, 2)), 4, AL.logical_shift_right, 7, AL.bitwise_and)
    lin("k", c_(M1), ("ki", S_(2, 3)), 1.0, 1.0)
    lin("k", c_(MB), ("ki", S_(2, 3)), -256.0)
    add("G", "sel", (("Fz", S_(0, 72), S_(0, 16)), ("Z", S_(0, 1152)), [[0, 1152]], AL.is_equal, 0.0, 1, 1),
        [("Z", S_(0, 1152))], [("Fz", S_(0, 72), S_(0, 16))], 1152, "gp")
    ts(("kh", full), ("one", full), c_(LC), AL.mult, 1536.0, AL.add)
    lin("k", k_(B32), k_(BM), 1.0 / 32)
    lin("k", k_(B512), k_(BM), 1.0 / 512)
    lin("k", ("CN", full), k_(BM), -688128.0)
    ms(c_(AC), 33.0 / 64)
    ms(("sv", S_(128, 129), 0), 95.0 / 1024)
    for w in pieces:
        ts(("C", w), ("cmb", w), 2047, AL.bitwise_and)
    for w in quarters:
        lin("M", ("M", w), ("cmb", w), 1.0 / 2048, -1023.5 / 2048)

    Cw = ("C", S_(0, 2048)); Xw = ("X", S_(0, 8192)); Mw = ("M", S_(0, 2048))
    arrive = {}

    def landing(t, h):
        return ("mc", 12 * t - (9 if h == 0 else 1))

    def leaving(t, h, a):
        r = 12 * t + (7 if h else 3 - own)
        return ("mc", S_(r, r + NB), own // 2, S_(a, a + 16))

    def send(t, h, pks):
        mine = (own // 2, S_(32 * (own % 2), 32 * (own % 2) + 32))
        trs = [(NB * (half ^ h) + j, ("mc", leaving(t, h, 0)[1].start + j) + mine, landing(t + 1, h) + mine)
               for j in range(NB) if h or j != own]
        a = (NS * t + h, trs)
        arrive[t + 1, h] = add("R", "arr", a, [], [], 128 // NB, "xch", [add("G", "send", a, [], [], len(trs), "snd", pks)])

    for t in range(RO):
        last = t == RO - 1
        par = t & 1
        tag[1] = t
        pl = "p6" if last else "p7"
        cols = []
        tag[2] = "sums"
        if last:
            for m in range(32):
                mm([(("p7", S_(0, 256)), ("Dg", m, full), ("X", S_(256 * m, 256 * m + 256)), m == 0, m == 31)])
            lin("yb", ("yxb", S_(0, 256)), ("p7", S_(0, 256)))
            for j, w in enumerate(quarters):
                put(("C16", w), ("C", w), [[0, 512]], 1, 0.0)
                mm([(("p7", S_(0, 256)), ("Dg", m, full), ("C16", S_(256 * m, 256 * m + 256)), m == 0, m == 7)
                    for m in (2 * j, 2 * j + 1)])
            lin("yb", ("yc0", S_(0, 256)), ("p7", S_(0, 256)))
        for h in range(NS):
            tag[0], tag[2] = h, "members%d" % h
            w = S_(LH * h, LH * h + LH)
            real = S_(LH * (h ^ half), LH * (h ^ half) + LH)
            o = 16 * LH * h
            pa, pb, pc = "p%d" % (3 * h), "p%d" % (3 * h + 1), "p%d" % (3 * h + 2)
            a0, a1 = S_(0, LH), S_(128, 128 + LH)
            chunks = [(LH * h + 32 * j, o + 512 * j) for j in range(LH // 32)]
            if t == 0:
                copy("Sl", ("Sl", w), ("s0b", real))
                zz = ("z0b", real)
                seats = [("Sl", S_(l0, l0 + 32)) for (l0, c0) in chunks]
            else:
                for j in range(2):
                    after(copy("z16", ("zf", S_(NB * h + j, NB * h + NB, 2), S_(0, 16)),
                               landing(t, h) + (S_(0, 2), S_(48 * j, 48 * j + 16))), arrive[t, h])
                zz = ("zf", S_(NB * h, NB * h + NB), S_(0, 16))
                seats = [landing(t, h) + (j, S_(16, 48)) for j in range(2)]
            n = 1024 // len(seats)
            for j, s in enumerate(seats):
                after(gather("gC", ("G", S_(o + n * j, o + n * j + n)), Cw, s), arrive.get((t, h)))
            mm(grp((pc, a0), [(k_(B512), ("one", a0)), (k_(B32), zz)]))
            lin("fl", ("fl", par, w), (pc, a0), -2.0, 0.0625 + 0.46875 - 1536.0)
            cols.append(grp((pl, w), [(k_(B32), ("St", S_(256 + LH * h, 256 + LH * h + LH))), (k_(BM), zz),
                                      (("Dg", 15, full), ("fl", par, w))]))

            def fold(src, lhs):
                mm(grp((pa, a1), [(lhs(k), (src, S_(o + k, o + 16 * LH, 16))) for k in range(16)]))
            fold("G", lambda k: ("Z", S_(128 * ((k + t) & 15) + 16 - k, 128 * ((k + t) & 15) + 144 - k)))
            lin("E16", ("E16", w), (pa, a1))
            tag[2] = "samplers%d" % h
            copy("eu", ("eu", w), ("E16", w))
            for l0 in range(w.start, w.stop, opt["gp"]):
                gather("gM", ("mg", S_(16 * l0, 16 * (l0 + opt["gp"]))), Mw, ("eu", S_(l0, l0 + opt["gp"])))
            tag[2] = "coins%d" % h
            e0 = 8 * LH * h
            cut = opt["cut"]
            po = pc if cut < 8 else pa
            for pk, d0, d1 in ((pb, 0, cut), (pa, cut, 8))[:1 + (cut < 8)]:
                mm([((pk, S_(LH * d, LH * d + LH)), ("Dm", d, full), ("E16", w), True, True) for d in range(d0, d1)])
            tt(("Pp", w), ("E16", w), (pc, a0), AL.mult)
            for pk, d0, d1 in ((pb, 0, cut), (pa, cut, 8))[:1 + (cut < 8)]:
                ts(("eq", S_(e0 + LH * d0, e0 + LH * d1)), (pk, S_(LH * d0, LH * d1)), 0.0, AL.is_equal)
            ts(("Qm", w), ("Pp", w), c_(AC), AL.add, 12582911.0, AL.add)
            oa = grp((po, a0), [(("I32", full), ("Qm", w)), (("CN", full), ("one", a0)), (ID, ("E16", w))] +
                     [(("Om", d, full), ("eq", S_(e0 + LH * d, e0 + LH * d + LH))) for d in range(8)])
            mm(oa[:3])
            mm(oa[3:3 + cut])
            if cut < 8:
                mm(oa[3 + cut:])
            lin("hr", ("hr", w), (po, a0), 1.0, -4095.5)
            tt(("hu", w), (po, a0), ("hr", w), AL.subtract)
            for (l0, c0) in chunks:
                gather("gX", ("xg", S_(c0, c0 + 512)), Xw, ("hu", S_(l0, l0 + 32)))
            if h:
                lin("hh", ("kh", S_(128, 256)), ("hu", full), 0.0078125, 1536.0 - 0.49609375)
            tag[2] = "bins%d" % h
            fold("xg", lambda k: ("Wz", S_(15 - k, 143 - k)))
            for j in range(4):
                sign = -1.0 if j else 1.0
                lin("gq", ("gq", j, w), (pa, a1), 0.25 * sign, (1536.0 - 0.375 + 0.25 * j) * sign)
            tests = grp((pc, a0), [(("Fl", j, full), ("gq", j, w)) for j in range(4)])
            mm(tests[:3])
            mm(tests[3:])
            dl = grp((pb, a0), [(("Dg", 2, full), ("gq", 0, w))] + [(ID, ("gq", j, w)) for j in (1, 2, 3)] +
                     [(k_(BE), ("wn", w))])
            mm(dl[:4])
            sign = opt["sign"] >> h & 1
            if sign:
                vec("sgn", ("fg", w), [(pc, a0), c_(NTH)], (("fg", w), (pc, a0), c_(NTH)), "S")
            else:
                ts(("fg", w), (pc, a0), c_(THR), AL.is_gt)
            mm(grp((pa, a0), [(k_(LO), ("fg", w))]))
            far = grp((pc, a0), [(k_(S3K), ("gq", 0, w))] + [(k_(SH8), ("gq", j, w)) for j in (1, 2, 3)] +
                      [(k_(BE), ("wn", w))]) * (opt["far"][t] >> h & 1)
            if far:
                mm(far[:4])
            if sign:
                vec("lin", ("wn", w), [(pa, a0)], (("wn", w), (pa, a0), 0.5, -2.5, True), "S")
            else:
                lin("wn", ("wn", w), (pa, a0), 1.0, 1.0, True)
            mm(dl[4:] + far[4:])
            ts(("sv", w, 0), (pb, a0), 0.0, AL.is_equal)
            if far:
                ts(("sv", w, 1), (pc, a0), c_(R8H), AL.is_equal, c_(R82), AL.add)
            else:
                mm(grp((pc, a0), [(k_(SH8), ("sv", w, 0))]))
                lin("sx", ("sv", w, 1), (pc, a0), 1.0, c_(R82))
            tag[2] = "maxima%d" % h
            ends = S_(o + 15, o + 16 * LH, 16)
            steps = []
            for j, (l0, c0) in enumerate(chunks):
                pk = (pa, pc)[j & 1]
                cw = S_(c0, c0 + 512)
                mm([((pk, S_(k, 512, 8)), ("Cm", k, full), ("sv", S_(l0, l0 + 32), S_(0, 2)), True, True) for k in range(8)])
                steps.append((pk, S_(0, 512)))
                if opt["ccp"][t] >> (2 * h + j) & 1:
                    vec("lin", ("cs", cw), [steps[j]], (("cs", cw), steps[j], 1.0, 0.0, False), "S")
                    steps[j] = ("cs", cw)
                scan(("ms", cw), ("mg", cw), steps[j], -4 * STEP, AL.max, AL.add)
                scan(("xs", cw), ("xg", cw), steps[j], -4 * STEP, AL.max, AL.add)
            if last:
                lin("pk", ("ysb", real), ("ms", ends), 1.0, STEP)
                lin("pk", ("yzb", real), ("xs", ends), 1.0, STEP)
            else:
                send(t, h, [lin("pk", leaving(t, h, 16 + 16 * (own % 2)), ("ms", ends), 1.0, STEP),
                            lin("pk", leaving(t, h, 48 * (own % 2)), ("xs", ends), 1.0, STEP)])
        tag[0], tag[2] = -1, "columns"
        up = S_(128, 256)
        sva = ("sv", full, 0)
        mm(cols[0] + cols[1])
        scan(("ls", S_(256, 384)), (pl, full), ("cd", full), -65536.0, AL.max, AL.add)
        lin("lu", ("lu", S_(16, 24)), ("ls", S_(256 + 15, 384, 16)), 1.0, 16384.0 + 24576.0)
        if last:
            vec("ts", ("o16", full), [("ind", Cw, ("lu", S_(16, 24)))],
                (("o16", full), ("ind", Cw, ("lu", S_(16, 24))), -1.0, None, AL.mult, None))
            lin("cv", ("Ft", full), ("p6", full), 1.0, 24576.0)
            mm(grp(("p6", S_(128, 136)), [(("Ft", full), ("Dg", 0, S_(0, 128, 16)))]))
            lin("cv", ("cT", S_(0, 8)), ("p6", S_(128, 136)), 1.0, c_(MB))
            for q in range(8):
                ts(("OH", q, S_(0, 256)), ("J", S_(0, 256)), ("cT", S_(q, q + 1)), AL.is_equal, c_(M1), AL.mult)
        tag[2] = "F"
        mm(grp(("p1", full), [(k_(SG), sva)]) + grp(("p1", up), [(ID, ("E16", full)), (k_(T2K), sva)]))
        lin("Rl", ("R32", 1, full), ("p1", full), 1.0, c_(L2K), True)
        tt(("R32", 0, full), ("R32", 1, full), ("p1", up), AL.add)
        mm([(("p4", full), ("one", full), ("FC", full), True, False)] + [(("p4", full), ("o16", full), ID, False, False)] * last)
        for p in range(16):
            if p:
                lin("Rr", ("R32", p, full), ("R32", 0, full), 1.0, -2048.0 * p, True)
            mm([(("p4", S_(0, 8), S_(max(p - 1, 0), p + 1)), ("R32", p, full), ("Sel", S_(0, 8), S_(0 if p else 1, 2)),
                 False, p == 15)])
        if not last:
            lin("Ft", ("Ft", full), ("p4", full))
            mm(grp(("p1", full), [(("Ft", full), ID)]))
            lin("Ff", ("Ff", full), ("p1", full))
            cp(("ind", Cw, ("lu", S_(16, 24))), ("Ff", full))
        tag[2] = "first"
        mm(grp(("p6", full), [(ID, ("kh", full)), (k_(ZF), sva)]) + grp(("p6", up), [(ID, ("kh", up)), (k_(ZF), sva)]))
        lin("sel", ("sel", S_(0, 256)), ("p6", S_(0, 256)), 1.0, -1600.0, True)
        mm(grp(("p6", full), [(k_(B32), ("St", full)), (k_(BM), ("sel", full))]) +
           grp(("p6", up), [(k_(B32), ("St", up)), (k_(BM128), ("sel", up))]))
        scan(("ls", S_(0, 256)), ("p6", S_(0, 256)), ("cd", S_(0, 256)), -65536.0, AL.max, AL.add)
        if last:
            lin("mi", ("mi", full), ("p6", up), 1.0 / 256, 1.0 - 127.5 / 256)
        lin("lu", ("lu", S_(0, 16)), ("ls", S_(15, 256, 16)), 1.0, 16384.0)
        if opt["xa"][t]:
            gather("xf", ("xf", full), ("xg", S_(0, 2048)), ("lu", S_(0, 8)))
            mm(grp(("p6", full), [(ID, ("xf", full)), (ID, ("xs", S_(15, 2048, 16)))]))
            lin("xh", ("xh", full), ("p6", full), 0.5, STEP / 2 - 0.25)
        else:
            tt(("xa", full), ("ind", ("xg", S_(0, 2048)), ("lu", S_(0, 8))), ("xs", S_(15, 2048, 16)), AL.add)
            lin("xh", ("xh", full), ("xa", full), 0.5, STEP / 2 - 0.25)
        if not last:
            cp(("ind", Xw, ("lu", S_(8, 16))), ("xh", full))
        else:
            lc = ("lc", S_(0, 8))
            yw = ("yxb", S_(0, 256))
            copy("mp", ("mp", full), ("mi", full))
            lin("mi", ("li", S_(0, 8)), ("ls", S_(128 + 15, 256, 16)), 1.0, 16384.0)
            ts(("li", S_(8, 16)), ("li", S_(0, 8)), 255, AL.bitwise_and)
            copy("lc", lc, ("li", S_(8, 16)))
            tt(("old", full), ("ind", Xw, ("lu", S_(8, 16))), ("mp", full), AL.mult)
            tt(("adj", full), ("ind", yw, lc), ("old", full), AL.subtract)
            tt(("vv", full), ("xh", full), ("mp", full), AL.mult)
            tt(("ind", yw, lc), ("vv", full), ("adj", full), AL.add)
        if not last:
            more = S_(0, 129)
            mm(grp(("p6", more), [(k_(BM), ("sv", more, 0))]))
            vec("acc", ("junk", more), [("p6", more)], (("junk", more), ("p6", more), c_(AC)), "S", [c_(AC)])
        else:
            tag[2] = "F"
            lin("Fz", ("Fz", S_(0, 72, 9), S_(0, 16)), ("p4", full))
            fin = grp(("p1", S_(0, 256)), [(("Fz", S_(8 * q, 8 * q + 8), S_(0, 16)), ("OH", q, S_(0, 256))) for q in range(8)])
            mm(fin)
            tt(("ycb", S_(0, 256)), ("yc0", S_(0, 256)), ("p1", S_(0, 256)), AL.add)
    for (y, src) in (("ys", ("ysb", full)), ("yz", ("yzb", full)), ("yx", ("yxb", S_(0, 256))), ("yc", ("ycb", S_(0, 256)))):
        add("S" if y == "yc" else "Y", "st", (y, src), [src], [], 131072, "dma")
    return ops


def cost(op, eng, pr):
    r, n = op["rate"], op["n"]
    if r == "dma":
        return (n / pr["bw"], pr["dma"]) if eng == "Y" else (100.0, n / pr["bw"] + pr["dma"])
    if r == "snd":
        return pr["snd"] + n * pr["trf"], 0.0
    if r == "xch":
        return n * pr["row"], pr["xch"]
    if r == "pe":
        return n * pr["pe"], 60.0
    if r == "gp":
        return 170.0 + 2 * n * pr["cyc"], 0.0
    if r in ("g", "sc"):
        return (50.0 if eng == "V" else 65.0) + n * pr[r] * pr["cyc"], 0.0
    if eng == "S":
        return pr["sfix"] + max(64.0, n) * pr["cyc"], 0.0
    return pr["fix"] + max(64.0, n * r) * pr["cyc"], 0.0


def schedule(ops, opt, pr, start=None):
    n = len(ops)
    lat = pr["lat"]
    pred = [[(d, d in o["deps"]) for d in sorted(o["deps"] | o["bank"])] for o in ops]
    succ = [[] for _ in ops]
    for i in range(n):
        for d, hard in pred[i]:
            succ[d].append((i, hard))
    tab = [{e: cost(o, e, pr) for e in o["eng"]} for o in ops]

    def sweep(key, back, bias, fixed=None):
        before = succ if back else pred
        key = list(key)
        for i in (range(n - 1, -1, -1) if back else range(n)):
            for d, _ in before[i]:
                if key[d] >= key[i]:
                    key[i] = key[d] + 0.001
        start = {e: [] for e in "VSPGYR"}
        stop = {e: [] for e in "VSPGYR"}
        order = {e: [] for e in "VSPGYR"}
        end = [0.0] * n
        where = [None] * n
        for i in np.argsort(key, kind="stable").tolist():
            best = None
            for e in (fixed[i] if fixed else ops[i]["eng"]):
                a, b = tab[i][e]
                st = b if back else 0.0
                for d, hard in before[i]:
                    x = end[d]
                    if where[d] != e or (hard and e != "P"):
                        x += lat + (b if back else tab[d][where[d]][1])
                    if x > st:
                        st = x
                s0, s1 = start[e], stop[e]
                p = m = len(s0)
                while p and s1[p - 1] > st:
                    p -= 1
                while p < m and st + a > s0[p]:
                    st = s1[p]
                    p += 1
                k = st + a * (bias[i] if e == "V" else 1.0)
                if best is None or k < best[0]:
                    best = (k, e, st, a, p)
            _, e, st, a, p = best
            start[e].insert(p, st)
            stop[e].insert(p, st + a)
            order[e].insert(p, i)
            end[i] = st + a
            where[i] = e
        return max(end[i] + tab[i][where[i]][1] for i in range(n)), order, where, end

    def passes(key, bias, more):
        best = cur = sweep(key, False, bias)
        for _ in range(more):
            b = sweep([-(cur[3][i] + tab[i][cur[2][i]][1]) for i in range(n)], True, bias, cur[2])
            cur = sweep([-x for x in b[3]], False, bias, cur[2])
            best = cur if cur[0] < best[0] else best
        return best

    key = [0.0] * n
    for i in range(n - 1, -1, -1):
        key[i] = min([key[j] for j, _ in succ[i]] + [0.0]) - sum(tab[i][ops[i]["eng"][0]]) - lat
    kinds, parts = {}, {}
    for i, o in enumerate(ops):
        kinds.setdefault(o["key"], []).append(i)
        parts.setdefault(o["part"], []).append(i)
        parts.setdefault((o["part"], o["level"]), []).append(i)
    kinds, parts = list(kinds.values()), list(parts.values())
    rng = np.random.RandomState(opt["seed"])
    bias = [1.4] * n
    if start:
        key, bias = start[2], [0.05 if e == "V" else 20.0 for e in start[1]]
    best = cur = passes(key, bias, 2)
    for it in range(opt["it"]):
        key = [cur[3][i] - tab[i][cur[2][i]][0] for i in range(n)]
        b2 = list(bias)
        u = rng.rand()
        if u < opt["parts"]:
            d = float(rng.randn()) * 600.0
            for i in parts[rng.randint(len(parts))]:
                key[i] += d
        elif u < 0.4:
            for _ in range(rng.randint(1, 4)):
                d = float(rng.randn()) * 1200.0
                for i in kinds[rng.randint(len(kinds))]:
                    key[i] += d
        elif u < 0.7:
            c = rng.rand() * cur[0]
            d = (rng.randn(n) * 600.0).tolist()
            key = [x + y if abs(x - c) < 3000.0 else x for x, y in zip(key, d)]
        else:
            x = (0.3, 1.0, 1.4, 2.0, 4.0)[rng.randint(5)]
            for i in (kinds[rng.randint(len(kinds))] if u < 0.85 else rng.randint(0, n, 8).tolist()):
                b2[i] = x
        c = passes(key, b2, int(rng.rand() < 0.3))
        if c[0] <= cur[0] + opt["slack"] * (1.0 - it / opt["it"]):
            cur, bias = c, b2
            best = c if c[0] < best[0] else best
    return best[1], best[2]


def polish(ops, order, where, opt, prs):
    n, ns = len(ops), len(prs)
    pred = [[(d, d in o["deps"]) for d in sorted(o["deps"] | o["bank"])] for o in ops]
    succ = [[] for _ in ops]
    for i in range(n):
        for d, _ in pred[i]:
            succ[d].append(i)
    tabs = [[{e: cost(o, e, pr) for e in o["eng"]} for o in ops] for pr in prs]

    def run(seq, where, s, p0, end, fin):
        tab, lat = tabs[s], prs[s]["lat"]
        free = {e: None for e in order}
        p, left = p0 - 1, len(free)
        while p >= 0 and left:
            if free[where[seq[p]]] is None:
                free[where[seq[p]]] = end[seq[p]]
                left -= 1
            p -= 1
        for i in seq[p0:]:
            e = where[i]
            st = free[e] or 0.0
            for d, hard in pred[i]:
                x = end[d] if where[d] == e and (e == "P" or not hard) else fin[d]
                if x > st:
                    st = x
            a, b = tab[i][e]
            free[e] = end[i] = st + a
            fin[i] = st + a + b + lat
        return max(fin) - lat + opt["marks"] * sum(fin[i] for i in marks)

    marks = [i for i, o in enumerate(ops) if o["kind"] in ("arr", "st") or o["rate"] == "sc"]

    def held(before, where, s, end, fin, i):
        pairs = []
        while i is not None and len(pairs) < opt["reach"]:
            e, nxt = where[i], None
            for d, hard in pred[i]:
                if (end[d] if where[d] == e and (e == "P" or not hard) else fin[d]) > end[i] - tabs[s][i][e][0] - 1e-6:
                    nxt = d
            if nxt is None and before[i] is not None:
                nxt = before[i]
                pairs.append((nxt, i))
            i = nxt
        return pairs

    done, seq, pos = [False] * n, [], {e: 0 for e in order}
    while len(seq) < n:
        for e in order:
            while pos[e] < len(order[e]) and all(done[d] for d, _ in pred[order[e][pos[e]]]):
                done[order[e][pos[e]]] = True
                seq.append(order[e][pos[e]])
                pos[e] += 1
    ends, fins = [[0.0] * n for _ in prs], [[0.0] * n for _ in prs]
    base = [run(seq, where, s, 0, ends[s], fins[s]) for s in range(ns)]
    fresh = True
    weight = [1.0 / ns, prs[0]["cyc"] / prs[-1]["cyc"] / ns][:ns]
    cur = sum(w * b for w, b in zip(weight, base))
    best = (cur, seq, where, ends[0])
    rng = np.random.RandomState(opt["seed"])
    at = [0] * n
    for it in range(opt["moves"]):
        if fresh:
            seq = sorted(seq, key=lambda i: ends[0][i] - tabs[0][i][where[i]][0])
            last, before, pairs = {}, [None] * n, {}
            for p, i in enumerate(seq):
                at[i] = p
                before[i] = last.get(where[i])
                last[where[i]] = i
            fresh = False
        x = (rng.randint(ns), marks[rng.randint(len(marks))])
        if x not in pairs:
            pairs[x] = held(before, where, x[0], ends[x[0]], fins[x[0]], x[1])
        if not pairs[x]:
            continue
        u, v = pairs[x][rng.randint(len(pairs[x]))]
        r = rng.rand()
        s2, w2 = list(seq), where
        if r < 0.3:
            p0 = max([at[u] - (rng.randint(12) if rng.rand() < 0.3 else 0)] + [at[d] + 1 for d, _ in pred[v]])
            if p0 > at[u]:
                continue
            s2.insert(p0, s2.pop(at[v]))
        elif r < 0.55:
            lo = max([at[u] - 80, 0] + [at[d] + 1 for d, _ in pred[u]])
            if lo >= at[u]:
                continue
            p0 = rng.randint(lo, at[u])
            s2.insert(p0, s2.pop(at[u]))
        elif r < 0.8:
            p = min([at[v] + 1 + (rng.randint(25) if rng.rand() < 0.5 else 0), n] + [at[d] for d in succ[u]])
            if p <= at[v]:
                continue
            p0 = at[u]
            s2.insert(p - 1, s2.pop(p0))
        else:
            x = u if rng.rand() < 0.6 else v
            if len(ops[x]["eng"]) < 2:
                continue
            w2 = list(where)
            w2[x] = "S" if where[x] == "V" else "V"
            p0 = at[x]
        e2, f2 = [list(x) for x in ends], [list(x) for x in fins]
        c = sum(weight[s] * run(s2, w2, s, p0, e2[s], f2[s]) for s in range(ns))
        if c <= cur - 50.0 * 0.16 ** (it / opt["moves"]) * math.log(1.0 - rng.rand()):
            cur, seq, where, ends, fins, fresh = c, s2, w2, e2, f2, True
            best = (c, seq, where, ends[0]) if c < best[0] else best
    return ({e: [i for i in best[1] if best[2][i] == e] for e in order}, best[2],
            [best[3][i] - tabs[0][i][best[2][i]][0] for i in range(n)], best[0])


def plan(ops, opt, prs):
    best = cur = None
    for r in range(opt["rounds"]):
        o = dict(opt, seed=opt["seed"] + 1000 * r)
        cur = polish(ops, *schedule(ops, o, prs[0], cur), o, prs)
        best = cur if best is None or cur[3] < best[3] else best
    return best[:2]


PLAN = []


def rank_program(g, core, T, topo):
    rank = T.rank_of(core)
    if rank is None:
        return
    ops = build(OPT, rank)
    if not PLAN:
        PLAN.extend(plan(ops, OPT, [PAR0, PAR1]))
    order, where = PLAN
    queue = {"V": g.vector, "S": g.scalar, "P": g.tensor, "G": g, "Y": g.sync}

    def ap(x):
        if not isinstance(x, tuple):
            return x
        if x[0] == "ind":
            return ap(x[1]).indirect(ap(x[2]))
        if len(x) == 2 and x[0] == "p4":
            return T[x[0]][:, x[1].start // 16:x[1].stop // 16, :]
        return T[x[0]][(slice(None),) + x[1:]]

    deps = [[d for d in o["deps"] if where[d] != "P" or where[i] != "P"] + [d for d in o["bank"] if where[d] != where[i]]
            for i, o in enumerate(ops)]
    needed = set(d for i, o in enumerate(ops) for d in deps[i] if o["kind"] != "arr")
    signal = {}
    total = {}
    for e in "VSPG":
        n = 0
        for i in order[e]:
            if i in needed and ops[i]["rate"] != "dma":
                n += 1
                signal[i] = ("q" + e, n)
        total["q" + e] = n
    for i in order["Y"] + order["S"]:
        if ops[i]["kind"] == "ld":
            signal[i] = ("ld%d" % ops[i]["args"][2], 16)
    per = min(len(topo.engines(core, c)) for c in T.cores if c != core) // NB
    for i in order["R"]:
        a = ops[i]["args"]
        signal[i] = ("arr%d" % a[0], per * len(a[1]))
    left = 0
    for e in "YGPSV":
        q = queue[e]
        seen = {}
        for i in order[e]:
            want = {}
            for d in deps[i]:
                s, v = signal[d]
                want[s] = max(want.get(s, 0), v)
            for s in sorted(want):
                if seen.get(s, 0) < want[s]:
                    q.wait_ge(T.sem[s], want[s])
                    seen[s] = want[s]
            k, a = ops[i]["kind"], ops[i]["args"]
            if k == "cp" or (k == "gat" and e == "V"):
                ins = q.tensor_copy(ap(a[0]), ap(a[1]))
            elif k == "gat":
                ins = q.activation(ap(a[0]), ap(a[1]), AF.Copy)
            elif k == "lin" and e == "S":
                f = AF.Relu if a[4] else (AF.Identity if isinstance(a[3], tuple) else AF.Copy)
                ins = q.activation(ap(a[0]), ap(a[1]), f, ap(a[3]), ap(a[2]))
            elif k == "lin" and a[4]:
                ins = q.tensor_scalar(ap(a[0]), ap(a[1]), ap(a[3]), 0.0, AL.add, AL.max)
            elif k == "lin":
                ins = q.tensor_scalar(ap(a[0]), ap(a[1]), ap(a[2]), ap(a[3]), AL.mult, AL.add)
            elif k == "tt":
                ins = q.tensor_tensor(ap(a[0]), ap(a[1]), ap(a[2]), a[3])
            elif k == "ts" and a[5] is None:
                ins = q.tensor_scalar(ap(a[0]), ap(a[1]), ap(a[2]), None, a[4])
            elif k == "ts":
                ins = q.tensor_scalar(ap(a[0]), ap(a[1]), ap(a[2]), ap(a[3]), a[4], a[5])
            elif k == "scan":
                ins = q.tensor_tensor_scan(ap(a[0]), ap(a[1]), ap(a[2]), a[3], a[4], a[5])
            elif k == "sgn":
                ins = q.activation(ap(a[0]), ap(a[1]), AF.Sign, ap(a[2]))
            elif k == "ms":
                ins = q.memset(ap(a[0]), a[1])
            elif k == "acc":
                ins = q.activation(ap(a[0]), ap(a[1]), AF.Relu, 2.0, -1.0, accum_out=ap(a[2]))
            elif k == "mm":
                for m in a:
                    ins = q.matmul(ap(m[0]), ap(m[1]), ap(m[2]), m[3], m[4])
            elif k == "iota" and SCRATCH[a[0][0]][2] == I32:
                ins = q.iota(ap(a[0]), a[1], a[2], a[3])
            elif k == "iota":
                ins = q.iota(ap(a[0]), a[1], a[2], a[3], allow_small_or_imprecise_dtypes=True)
            elif k == "sel":
                ins = q.affine_select(ap(a[0]), ap(a[1]), a[2], a[3], a[4], a[5], a[6])
            elif k == "ld":
                q.dma_start(ap(a[0]), ap(a[1])).then_inc(T.sem["ld%d" % a[2]], 16)
            elif k == "st":
                q.dma_start(T[a[0]][:], ap(a[1])).then_inc(T.sem.stored, 16)
            elif k == "send":
                tr = []
                for j, (b, src, dst) in enumerate(a[1]):
                    rid, pid, _ = topo.addr(T.cores[b])
                    mask = sum(1 << x for x in topo.engines(core, T.cores[b])[per * j:per * (j + 1)])
                    tr.append(RemoteDMATransfer(dst_ids=[DstId(rid=rid, pnc=pid)], dma_engine_mask=mask,
                                                remote_sem=T.sem["arr%d" % a[0]], src=ap(src), dst=ap(dst)))
                q.remote_dma_fused(tr, local_sem=T.sem.left)
                left += per * len(tr)
            if i in signal and k != "ld":
                ins.then_inc(T.sem[signal[i][0]], 1)
        if e == "Y":
            q.wait_ge(T.sem.stored, 64)
            for s in sorted(total):
                q.wait_ge(T.sem[s], total[s])
        if e == "G":
            q.wait_ge(T.sem.left, left)
